import numpy as np
import ml_dtypes


def mxq(x, axis, fmt="e4m3"):
    dtype, down = {"e4m3": (ml_dtypes.float8_e4m3fn, 7), "e5m2": (ml_dtypes.float8_e5m2, 14)}[fmt]
    v = np.moveaxis(np.asarray(x, np.float32).astype(ml_dtypes.bfloat16).astype(np.float64), axis, -1)
    blocks = v.reshape(v.shape[:-1] + (-1, 32))
    amax = np.abs(blocks).max(-1, keepdims=True)
    byte = np.maximum(np.where(amax > 0, np.frexp(amax)[1] - 1 + 127, 0) - down, 1)
    scale = np.exp2(byte - 127.0)
    codes = (blocks / scale).astype(np.float32).astype(dtype).astype(np.float64)
    return np.moveaxis((codes * scale).reshape(v.shape), -1, axis)


WIDE = False


def mx_kscale(k):
    if not WIDE:
        return np.ones(k)
    levels = np.array([18, -18])
    if k % 512:
        return np.exp2(np.random.permutation(np.resize(levels, k // 32))).repeat(32)
    a = np.empty((k // 512, 16))
    for p in range(k // 512):
        a[p, :8] = np.random.permutation(np.resize(levels, 8))
        for g in range(8):
            far = levels[np.abs(levels - a[p, g]) >= 10]
            a[p, g + 8] = far[np.random.randint(len(far))]
    return np.exp2(a.ravel()).repeat(32)


def f64(x):
    return np.asarray(x).astype(np.float64)


def striped(idx):
    return np.tile(np.asarray(idx).reshape(-1, 16).T, (8, 1)).astype(np.uint16)


def unstriped(offs):
    return offs[:16].T.reshape(-1).astype(np.int64)


B, N, T, D, R = 1, 512, 2048, 512, 1024
PAGE = 64


def setup_inputs():
    n = np.random.standard_normal
    pages = np.random.permutation(T // PAGE)[:B * N // PAGE]
    idx = (pages[:, None] * PAGE + np.arange(PAGE)[None, :]).reshape(-1)
    s = mx_kscale(D)[:, None]
    z = mx_kscale(R)[:, None]
    q = n((B, D, R))
    do = n((B, D, R))
    return {
        "qT": (q * s).astype(np.float32),
        "cT": (n((D, T)) * (0.50 / np.sqrt(D)) / s).astype(np.float32),
        "doT": (do * s).astype(np.float32),
        "lse": (np.log(N) + 0.12 + 0.1 * n((B, R, 1))).astype(np.float32),
        "delta": (0.3 * n((B, R, 1))).astype(np.float32),
        "rw": (np.random.uniform(0.5, 1.5, (B, R, 1)) * N / np.sqrt(R) * z).astype(np.float32),
        "qm": (q.transpose(0, 2, 1) / z).astype(np.float32),
        "dom": (do.transpose(0, 2, 1) / z).astype(np.float32),
        "offs": striped(idx),
    }


def reference(qT, cT, doT, lse, delta, rw, qm, dom, offs):
    idx = unstriped(offs)
    pick = lambda x: x[:, idx].reshape(x.shape[0], B, N).transpose(1, 0, 2)
    cq = mxq(pick(f64(cT)), 1, "e4m3")
    a = mxq(f64(qT), 1, "e4m3").transpose(0, 2, 1) @ cq
    p = np.exp(a - f64(lse))
    dp = mxq(f64(doT), 1, "e5m2").transpose(0, 2, 1) @ cq
    ds = f64(rw) * p * (dp - f64(delta))
    dk = mxq(f64(qm), 1, "e4m3").transpose(0, 2, 1) @ mxq(ds, 1, "e5m2")
    dv = mxq(f64(dom), 1, "e5m2").transpose(0, 2, 1) @ mxq(f64(rw) * p, 1, "e4m3")
    gc = np.zeros((D, T))
    gc[:, idx] = (dk + dv).transpose(1, 0, 2).reshape(D, B * N)
    return gc

@@ -1,0 +1,236 @@
+from contextlib import ExitStack
+
+import concourse.mybir as mybir
+
+N, T, D, R = 512, 2048, 512, 1024
+FLOPS = 4 * 2 * R * N * D
+
+F32 = mybir.dt.float32
+BF16 = mybir.dt.bfloat16
+U32 = mybir.dt.uint32
+U16 = mybir.dt.uint16
+U8 = mybir.dt.uint8
+E4 = mybir.dt.float8_e4m3fn_x4
+E5 = mybir.dt.float8_e5m2_x4
+ACT = mybir.ActivationFunctionType
+ALU = mybir.AluOpType
+
+P = 128
+PACK = 4
+KP = P * PACK
+G = R // KP
+DT = D // P
+
+
+def tile_attend_gat_lse_c_kernel(tc, qT, cT, doT, lse, delta, rw, qm, dom, offs, out):
+    nc = tc.nc
+    with ExitStack() as ctx:
+        keep = ctx.enter_context(tc.tile_pool(name="keep", bufs=1))
+        ring = ctx.enter_context(tc.tile_pool(name="ring", bufs=1))
+        psum = ctx.enter_context(tc.psum_pool(name="psum", bufs=1))
+
+        def cast(engine, dst, src):
+            if engine == "S":
+                nc.scalar.copy(out=dst, in_=src)
+            else:
+                nc.vector.tensor_copy(out=dst, in_=src)
+
+        def mx_pair(name, width):
+            codes = keep.tile([P, width], U32, name=name + "_codes", align_bytes=64)
+            scales = keep.tile([P, width], U8, name=name + "_scales", align_bytes=64)
+            return codes, scales
+
+        def quantize(pair, fmt, words, src):
+            nc.vector.quantize_mx(out=pair[0][:, words].bitcast(fmt), scales=pair[1][:, words], in_=src)
+
+        offsets = keep.tile([P, N // 16], U16, name="offsets")
+        planes = [keep.tile([P, T], F32, name="plane%d" % j) for j in range(PACK)]
+        c_rows = cT.rearrange("(p j) w -> j p w", j=PACK)
+        nc.sync.dma_start(out=planes[0][:], in_=c_rows[0])
+        nc.sync.dma_start(offsets[:], offs)
+        for j in range(1, PACK):
+            nc.sync.dma_start(out=planes[j][:], in_=c_rows[j])
+
+        vecs = {}
+        for name, src in (("lse", lse), ("rw", rw), ("delta", delta)):
+            vecs[name] = keep.tile([P, G, PACK], F32, name=name + "_sb")
+            nc.scalar.dma_start(out=vecs[name][:], in_=src[0].rearrange("(g p t) o -> p g (t o)", g=G, t=PACK))
+
+        def load(src, rows, cols):
+            width = cols.stop - cols.start
+            raw = ring.tile([P, PACK, width], F32, name="raw", tag="raw%d" % width, bufs=8 if width == 256 else 2)
+            nc.sync.dma_start(out=raw[:], in_=src[0][rows, cols].rearrange("(p j) w -> p j w", j=PACK))
+            return raw
+
+        alld = slice(0, D)
+        H = KP // 2
+        raw = {}
+        for name, src in (("q", qT), ("do", doT)):
+            raw[name, 0] = [load(src, alld, slice(h * H, (h + 1) * H)) for h in range(2)]
+        for name, src in (("q", qT), ("do", doT)):
+            whole = load(src, alld, slice(KP, 2 * KP))
+            raw[name, 1] = [whole[:, :, h * H:(h + 1) * H] for h in range(2)]
+
+        windows = [keep.tile([P, T], F32, name="window%d" % k) for k in range(DT)]
+        for k in range(DT):
+            nc.vector.memset(windows[k][:], 0.0)
+        neg_lse = keep.tile([P, G * PACK], F32, name="neg_lse")
+        nc.scalar.activation(out=neg_lse[:], in_=vecs["lse"][:].rearrange("p g t -> p (g t)"), func=ACT.Identity, scale=-1.0)
+        rw_sb = vecs["rw"][:].rearrange("p g t -> p (g t)")
+        neg_rwd = keep.tile([P, G * PACK], F32, name="neg_rwd")
+        nc.vector.scalar_tensor_tensor(out=neg_rwd[:], in0=vecs["delta"][:].rearrange("p g t -> p (g t)"), scalar=-1.0, in1=rw_sb,
+                                       op0=ALU.mult, op1=ALU.mult)
+
+        c_bf = keep.tile([P, N, PACK], BF16, name="c_bf", align_bytes=64)
+        for j in range(PACK):
+            nc.vector.tensor_copy(out=c_bf[:, :, j], in_=planes[j][:].indirect(offsets[:]))
+        c_mx = mx_pair("c", N)
+        quantize(c_mx, E4, slice(0, N), c_bf[:].rearrange("p n j -> p (n j)"))
+
+        def group_tile(name):
+            return ring.tile([P, KP * PACK], BF16, name=name, tag="group", bufs=6, align_bytes=64)
+
+        fmt = {"q": E4, "do": E5, "qm": E4, "dom": E5, "pw": E4, "ds": E5}
+        mx = {}
+        grp = {}
+
+        def cast_first(name, g, quarter, engine):
+            if (name, g) not in grp:
+                grp[name, g] = group_tile(name + "_bf")
+            src = raw[name, g][quarter // 2][:].rearrange("p j (m t) -> p m t j", t=PACK)
+            dst = grp[name, g][:].rearrange("p (t m j) -> p m t j", t=PACK, j=PACK)
+            return src, dst
+
+        def cast_q(name, g, lo, hi, engine):
+            src, dst = cast_first(name, g, lo // 32, engine)
+            base = (lo // 64) * 64
+            cast(engine, dst[:, lo:hi], src[:, lo - base:hi - base])
+
+        def quant_group(name, g, h):
+            if (name, g) not in mx:
+                mx[name, g] = mx_pair("%s%d" % (name, g), KP)
+            quantize(mx[name, g], fmt[name], slice(h * H, (h + 1) * H), grp[name, g][:, h * H * PACK:(h + 1) * H * PACK])
+
+        e_sb = {}
+        g_sb = {}
+
+        def score(name, g, t):
+            bank = psum.tile([P, N], F32, name="score", tag="score", bufs=4)
+            codes, scales = mx[name, g]
+            cols = slice(t * P, (t + 1) * P)
+            nc.tensor.matmul_mx(out=bank[:], lhsT=codes[:, cols].bitcast(fmt[name]), lhsT_scale=scales[:, cols],
+                                rhs=c_mx[0][:].bitcast(E4), rhs_scale=c_mx[1][:], start=True, stop=True)
+            return bank
+
+        def probs(g):
+            e_sb[g] = keep.tile([P, PACK, N], F32, name="e%d" % g)
+            for t in range(PACK):
+                bank = score("q", g, t)
+                u = g * PACK + t
+                nc.scalar.activation(out=e_sb[g][:, t, :], in_=bank[:], func=ACT.Exp, bias=neg_lse[:, u:u + 1], scale=1.0)
+
+        def gates(g):
+            g_sb[g] = keep.tile([P, PACK, N], F32, name="g%d" % g)
+            for t in range(PACK):
+                bank = score("do", g, t)
+                u = g * PACK + t
+                nc.scalar.activation(out=g_sb[g][:, t, :], in_=bank[:], func=ACT.Identity, bias=neg_rwd[:, u:u + 1], scale=rw_sb[:, u:u + 1])
+
+        def product(name, g, h):
+            if (name, g) not in grp:
+                grp[name, g] = group_tile(name + "_bf")
+            cs = slice(h * 64, (h + 1) * 64)
+            dst = grp[name, g][:].rearrange("p (c i t) -> p c t i", i=4, t=PACK)[:, cs]
+            in0 = e_sb[g][:].rearrange("p t (c i) -> p c t i", i=4)[:, cs]
+            if name == "pw":
+                in1 = vecs["rw"][:, g, :].unsqueeze(1).unsqueeze(3).broadcast_to([P, 64, PACK, 4])
+            else:
+                in1 = g_sb[g][:].rearrange("p t (c i) -> p c t i", i=4)[:, cs]
+            nc.vector.tensor_tensor(out=dst, in0=in0, in1=in1, op=ALU.mult)
+
+        second = {}
+
+        def cast_second(name, g, k, engine):
+            tile = ring.tile([P, P * PACK], BF16, name="second_bf", tag="second", bufs=8, align_bytes=64)
+            second[name, g, k] = tile
+            src = raw[name, g, k // 2][:, :, (k % 2) * P:(k % 2 + 1) * P].rearrange("p j (c i) -> p c j i", i=4)
+            cast(engine, tile[:].rearrange("p (c i j) -> p c j i", i=4, j=PACK), src)
+
+        def quant_second(name, g, k):
+            if (name, g) not in mx:
+                mx[name, g] = mx_pair("%s%d" % (name, g), D)
+            quantize(mx[name, g], fmt[name], slice(k * P, (k + 1) * P), second[name, g, k][:])
+
+        acc = [psum.tile([P, N], F32, name="acc%d" % k) for k in range(DT)]
+        passes = [("dom", "pw", 0), ("qm", "ds", 0), ("dom", "pw", 1), ("qm", "ds", 1)]
+
+        def out_pass(k, i):
+            left, right, g = passes[i]
+            cols = slice(k * P, (k + 1) * P)
+            nc.tensor.matmul_mx(out=acc[k][:], lhsT=mx[left, g][0][:, cols].bitcast(fmt[left]), lhsT_scale=mx[left, g][1][:, cols],
+                                rhs=mx[right, g][0][:].bitcast(fmt[right]), rhs_scale=mx[right, g][1][:],
+                                start=(i == 0), stop=(i == len(passes) - 1))
+
+        def finish(k):
+            stage = ring.tile([P, N], F32, name="stage", tag="stage", bufs=2)
+            nc.scalar.copy(out=stage[:], in_=acc[k][:])
+            nc.vector.tensor_copy(out=windows[k][:].indirect(offsets[:]), in_=stage[:])
+            nc.sync.dma_start(out=out[k * P:(k + 1) * P, :], in_=windows[k][:])
+
+        cast_q("q", 0, 0, 64, "S")
+        cast_q("q", 0, 64, 96, "V")
+        cast_q("q", 0, 96, 128, "S")
+        quant_group("q", 0, 0)
+        quant_group("q", 0, 1)
+        probs(0)
+        cast_q("do", 0, 0, 64, "V")
+        cast_q("do", 0, 64, 128, "V")
+        quant_group("do", 0, 0)
+        quant_group("do", 0, 1)
+        gates(0)
+
+        for h in range(2):
+            for g in range(G):
+                for name, src in (("dom", dom), ("qm", qm)):
+                    raw[name, g, h] = load(src, slice(g * KP, (g + 1) * KP), slice(h * H, (h + 1) * H))
+
+        cast_q("q", 1, 0, 64, "V")
+        cast_q("q", 1, 64, 128, "V")
+        product("pw", 0, 0)
+        quant_group("q", 1, 0)
+        quant_group("q", 1, 1)
+        cast_q("do", 1, 0, 64, "S")
+        cast_q("do", 1, 64, 128, "S")
+        product("pw", 0, 1)
+        probs(1)
+        quant_group("do", 1, 0)
+        quant_group("do", 1, 1)
+        gates(1)
+        product("ds", 0, 0)
+        quant_group("pw", 0, 0)
+        product("ds", 0, 1)
+        quant_group("pw", 0, 1)
+        product("pw", 1, 0)
+        quant_group("ds", 0, 0)
+        product("pw", 1, 1)
+        quant_group("ds", 0, 1)
+        for left, right, g in passes:
+            cast_second(left, g, 0, "S")
+        product("ds", 1, 0)
+        quant_group("pw", 1, 0)
+        product("ds", 1, 1)
+        quant_group("pw", 1, 1)
+        quant_group("ds", 1, 0)
+        for left, right, g in passes:
+            quant_second(left, g, 0)
+        quant_group("ds", 1, 1)
+        for i in range(len(passes)):
+            out_pass(0, i)
+        finish(0)
+        for k in range(1, DT):
+            for i, (left, right, g) in enumerate(passes):
+                cast_second(left, g, k, "V" if (k > 1 and i >= 2) else "S")
+            for i, (left, right, g) in enumerate(passes):
+                quant_second(left, g, k)
+                out_pass(k, i)
+            finish(k)

@@ -97,14 +97,15 @@ def tile_attend_gat_lse_c_kernel(tc, qT, cT, doT, lse, delta, rw, qm, dom, offs,
         def cast_first(name, g, quarter, engine):
             if (name, g) not in grp:
                 grp[name, g] = group_tile(name + "_bf")
-            src = raw[name, g][quarter // 2][:].rearrange("p j (m t) -> p m t j", t=PACK)
-            dst = grp[name, g][:].rearrange("p (t m j) -> p m t j", t=PACK, j=PACK)
+            src = raw[name, g][quarter // 2][:].rearrange("p j (m u t) -> p u m j t", u=2, t=2)
+            dst = grp[name, g][:].rearrange("p (u t m j) -> p u m j t", u=2, t=2, j=PACK)
             return src, dst
 
         def cast_q(name, g, lo, hi, engine):
             src, dst = cast_first(name, g, lo // 32, engine)
             base = (lo // 64) * 64
-            cast(engine, dst[:, lo:hi], src[:, lo - base:hi - base])
+            for u in range(2):
+                cast(engine, dst[:, u, lo:hi], src[:, u, lo - base:hi - base])
 
         def quant_group(name, g, h):
             if (name, g) not in mx:
@@ -139,13 +140,13 @@ def tile_attend_gat_lse_c_kernel(tc, qT, cT, doT, lse, delta, rw, qm, dom, offs,
         def product(name, g, h):
             if (name, g) not in grp:
                 grp[name, g] = group_tile(name + "_bf")
-            cs = slice(h * 64, (h + 1) * 64)
-            dst = grp[name, g][:].rearrange("p (c i t) -> p c t i", i=4, t=PACK)[:, cs]
-            in0 = e_sb[g][:].rearrange("p t (c i) -> p c t i", i=4)[:, cs]
+            cs = slice(h * 128, (h + 1) * 128)
+            dst = grp[name, g][:].rearrange("p (c i t) -> p c t i", i=2, t=PACK)[:, cs]
+            in0 = e_sb[g][:].rearrange("p t (c i) -> p c t i", i=2)[:, cs]
             if name == "pw":
-                in1 = vecs["rw"][:, g, :].unsqueeze(1).unsqueeze(3).broadcast_to([P, 64, PACK, 4])
+                in1 = vecs["rw"][:, g, :].unsqueeze(1).unsqueeze(3).broadcast_to([P, 128, PACK, 2])
             else:
-                in1 = g_sb[g][:].rearrange("p t (c i) -> p c t i", i=4)[:, cs]
+                in1 = g_sb[g][:].rearrange("p t (c i) -> p c t i", i=2)[:, cs]
             nc.vector.tensor_tensor(out=dst, in0=in0, in1=in1, op=ALU.mult)
 
         second = {}
@@ -153,8 +154,8 @@ def tile_attend_gat_lse_c_kernel(tc, qT, cT, doT, lse, delta, rw, qm, dom, offs,
         def cast_second(name, g, k, engine):
             tile = ring.tile([P, P * PACK], BF16, name="second_bf", tag="second", bufs=8, align_bytes=64)
             second[name, g, k] = tile
-            src = raw[name, g, k // 2][:, :, (k % 2) * P:(k % 2 + 1) * P].rearrange("p j (c i) -> p c j i", i=4)
-            cast(engine, tile[:].rearrange("p (c i j) -> p c j i", i=4, j=PACK), src)
+            src = raw[name, g, k // 2][:, :, (k % 2) * P:(k % 2 + 1) * P].rearrange("p j (c i) -> p c j i", i=2)
+            cast(engine, tile[:].rearrange("p (c i j) -> p c j i", i=2, j=PACK), src)
 
         def quant_second(name, g, k):
             if (name, g) not in mx:

@@ -48,7 +48,7 @@ def tile_attend_gat_lse_c_kernel(tc, qT, cT, doT, lse, delta, rw, qm, dom, offs,
         c_rows = cT.rearrange("(p j) w -> j p w", j=PACK)
         nc.sync.dma_start(out=planes[0][:], in_=c_rows[0])
         nc.sync.dma_start(offsets[:], offs)
-        for j in range(1, PACK):
+        for j in range(1, PACK - 1):
             nc.sync.dma_start(out=planes[j][:], in_=c_rows[j])
 
         vecs = {}
@@ -58,18 +58,24 @@ def tile_attend_gat_lse_c_kernel(tc, qT, cT, doT, lse, delta, rw, qm, dom, offs,
 
         def load(src, rows, cols):
             width = cols.stop - cols.start
-            raw = ring.tile([P, PACK, width], F32, name="raw", tag="raw%d" % width, bufs=8 if width == 256 else 2)
+            raw = ring.tile([P, PACK, width], F32, name="raw", tag="raw%d" % width, bufs=12 if width == 256 else 2)
             nc.sync.dma_start(out=raw[:], in_=src[0][rows, cols].rearrange("(p j) w -> p j w", j=PACK))
             return raw
 
         alld = slice(0, D)
         H = KP // 2
         raw = {}
-        for name, src in (("q", qT), ("do", doT)):
-            raw[name, 0] = [load(src, alld, slice(h * H, (h + 1) * H)) for h in range(2)]
+        first_half = load(qT, alld, slice(0, H))
+        nc.sync.dma_start(out=planes[PACK - 1][:], in_=c_rows[PACK - 1])
+        raw["q", 0] = [first_half, load(qT, alld, slice(H, KP))]
+        raw["do", 0] = [load(doT, alld, slice(h * H, (h + 1) * H)) for h in range(2)]
         for name, src in (("q", qT), ("do", doT)):
             whole = load(src, alld, slice(KP, 2 * KP))
-            raw[name, 1] = [whole[:, :, h * H:(h + 1) * H] for h in range(2)]
+            raw[name, 1] = [whole]
+        for h in range(2):
+            for name, src in (("dom", dom), ("qm", qm)):
+                for g in range(G):
+                    raw[name, g, h] = load(src, slice(g * KP, (g + 1) * KP), slice(h * H, (h + 1) * H))
 
         windows = [keep.tile([P, T], F32, name="window%d" % k) for k in range(DT)]
         for k in range(DT):
@@ -87,151 +93,148 @@ def tile_attend_gat_lse_c_kernel(tc, qT, cT, doT, lse, delta, rw, qm, dom, offs,
         c_mx = mx_pair("c", N)
         quantize(c_mx, E4, slice(0, N), c_bf[:].rearrange("p n j -> p (n j)"))
 
-        def group_tile(name):
-            return ring.tile([P, KP * PACK], BF16, name=name, tag="group", bufs=6, align_bytes=64)
+
+        def half_tile(name):
+            return ring.tile([P, H * PACK], BF16, name=name, tag="half", bufs=12, align_bytes=64)
 
         fmt = {"q": E4, "do": E5, "qm": E4, "dom": E5, "pw": E4, "ds": E5}
         mx = {}
         grp = {}
 
-        def cast_first(name, g, quarter, engine):
+        def halves(name, g):
             if (name, g) not in grp:
-                grp[name, g] = group_tile(name + "_bf")
-            src = raw[name, g][quarter // 2][:].rearrange("p j (m u t) -> p u m j t", u=2, t=2)
-            dst = grp[name, g][:].rearrange("p (u t m j) -> p u m j t", u=2, t=2, j=PACK)
-            return src, dst
+                grp[name, g] = [half_tile(name + "_bf") for u in range(2)]
+            return grp[name, g]
 
-        def cast_q(name, g, lo, hi, engine):
-            src, dst = cast_first(name, g, lo // 32, engine)
-            base = (lo // 64) * 64
-            for u in range(2):
-                cast(engine, dst[:, u, lo:hi], src[:, u, lo - base:hi - base])
+        def cast_q(name, g, part, u, engine):
+            src = raw[name, g][part][:].rearrange("p j (m u e) -> p u m j e", u=2, e=2)[:, u]
+            dst = halves(name, g)[u][:].rearrange("p (e m j) -> p m j e", e=2, j=PACK)
+            width = src.shape[1]
+            cast(engine, dst[:, part * width:(part + 1) * width], src)
 
-        def quant_group(name, g, h):
+        def quant_half(name, g, h):
             if (name, g) not in mx:
                 mx[name, g] = mx_pair("%s%d" % (name, g), KP)
-            quantize(mx[name, g], fmt[name], slice(h * H, (h + 1) * H), grp[name, g][:, h * H * PACK:(h + 1) * H * PACK])
+            quantize(mx[name, g], fmt[name], slice(h * H, (h + 1) * H), halves(name, g)[h][:])
 
         e_sb = {}
         g_sb = {}
 
         def score(name, g, t):
-            bank = psum.tile([P, N], F32, name="score", tag="score", bufs=4)
+            bank = psum.tile([P, N], F32, name="score", tag="bank", bufs=8)
             codes, scales = mx[name, g]
             cols = slice(t * P, (t + 1) * P)
             nc.tensor.matmul_mx(out=bank[:], lhsT=codes[:, cols].bitcast(fmt[name]), lhsT_scale=scales[:, cols],
                                 rhs=c_mx[0][:].bitcast(E4), rhs_scale=c_mx[1][:], start=True, stop=True)
             return bank
 
-        def probs(g):
-            e_sb[g] = keep.tile([P, PACK, N], F32, name="e%d" % g)
-            for t in range(PACK):
-                bank = score("q", g, t)
-                u = g * PACK + t
-                nc.scalar.activation(out=e_sb[g][:, t, :], in_=bank[:], func=ACT.Exp, bias=neg_lse[:, u:u + 1], scale=1.0)
-
-        def gates(g):
-            g_sb[g] = keep.tile([P, PACK, N], F32, name="g%d" % g)
-            for t in range(PACK):
-                bank = score("do", g, t)
-                u = g * PACK + t
-                nc.scalar.activation(out=g_sb[g][:, t, :], in_=bank[:], func=ACT.Identity, bias=neg_rwd[:, u:u + 1], scale=rw_sb[:, u:u + 1])
+        def read_banks(name, g, parts):
+            banks = [score(name, g, t) for t in range(PACK)]
+            width = N // parts
+            tiles = []
+            for part in range(parts):
+                tile = keep.tile([P, PACK, width], F32, name="%s_f32_%d_%d" % (name, g, part))
+                tiles.extend([tile[:, :, i * H:(i + 1) * H] for i in range(width // H)])
+                cols = slice(part * width, (part + 1) * width)
+                for t in range(PACK):
+                    u = g * PACK + t
+                    if name == "q":
+                        nc.scalar.activation(out=tile[:, t, :], in_=banks[t][:, cols], func=ACT.Exp, bias=neg_lse[:, u:u + 1], scale=1.0)
+                    else:
+                        nc.scalar.activation(out=tile[:, t, :], in_=banks[t][:, cols], func=ACT.Identity, bias=neg_rwd[:, u:u + 1],
+                                             scale=rw_sb[:, u:u + 1])
+            (e_sb if name == "q" else g_sb)[g] = tiles
 
         def product(name, g, h):
-            if (name, g) not in grp:
-                grp[name, g] = group_tile(name + "_bf")
-            cs = slice(h * 128, (h + 1) * 128)
-            dst = grp[name, g][:].rearrange("p (c i t) -> p c t i", i=2, t=PACK)[:, cs]
-            in0 = e_sb[g][:].rearrange("p t (c i) -> p c t i", i=2)[:, cs]
+            dst = halves(name, g)[h][:].rearrange("p (c i t) -> p c t i", i=4, t=PACK)
+            in0 = e_sb[g][h].rearrange("p t (c i) -> p c t i", i=4)
             if name == "pw":
-                in1 = vecs["rw"][:, g, :].unsqueeze(1).unsqueeze(3).broadcast_to([P, 128, PACK, 2])
+                in1 = vecs["rw"][:, g, :].unsqueeze(1).unsqueeze(3).broadcast_to([P, 64, PACK, 4])
             else:
-                in1 = g_sb[g][:].rearrange("p t (c i) -> p c t i", i=2)[:, cs]
+                in1 = g_sb[g][h].rearrange("p t (c i) -> p c t i", i=4)
             nc.vector.tensor_tensor(out=dst, in0=in0, in1=in1, op=ALU.mult)
 
         second = {}
 
         def cast_second(name, g, k, engine):
-            tile = ring.tile([P, P * PACK], BF16, name="second_bf", tag="second", bufs=8, align_bytes=64)
-            second[name, g, k] = tile
-            src = raw[name, g, k // 2][:, :, (k % 2) * P:(k % 2 + 1) * P].rearrange("p j (c i) -> p c j i", i=2)
-            cast(engine, tile[:].rearrange("p (c i j) -> p c j i", i=2, j=PACK), src)
+            if (name, k) not in second:
+                second[name, k] = ring.tile([P, G, P * PACK], BF16, name="second_bf", tag="second", bufs=4, align_bytes=64)
+            src = raw[name, g, k // 2][:, :, (k % 2) * P:(k % 2 + 1) * P].rearrange("p j (c i) -> p c j i", i=4)
+            cast(engine, second[name, k][:, g, :].rearrange("p (c i j) -> p c j i", i=4, j=PACK), src)
 
-        def quant_second(name, g, k):
-            if (name, g) not in mx:
-                mx[name, g] = mx_pair("%s%d" % (name, g), D)
-            quantize(mx[name, g], fmt[name], slice(k * P, (k + 1) * P), second[name, g, k][:])
+        def quant_second(name, k, lo, hi):
+            if (name, k) not in mx:
+                mx[name, k] = mx_pair("%s%d" % (name, k), G * P)
+            quantize(mx[name, k], fmt[name], slice(lo * P, hi * P), second[name, k][:, lo:hi, :].rearrange("p g w -> p (g w)"))
 
-        acc = [psum.tile([P, N], F32, name="acc%d" % k) for k in range(DT)]
-        passes = [("dom", "pw", 0), ("qm", "ds", 0), ("dom", "pw", 1), ("qm", "ds", 1)]
+        acc = {}
+        partner = {"dom": "pw", "qm": "ds"}
 
-        def out_pass(k, i):
-            left, right, g = passes[i]
-            cols = slice(k * P, (k + 1) * P)
-            nc.tensor.matmul_mx(out=acc[k][:], lhsT=mx[left, g][0][:, cols].bitcast(fmt[left]), lhsT_scale=mx[left, g][1][:, cols],
-                                rhs=mx[right, g][0][:].bitcast(fmt[right]), rhs_scale=mx[right, g][1][:],
-                                start=(i == 0), stop=(i == len(passes) - 1))
+        def out_passes(name, k, lo, hi):
+            if k not in acc:
+                acc[k] = psum.tile([P, N], F32, name="acc", tag="bank", bufs=8)
+            right = partner[name]
+            for g in range(lo, hi):
+                cols = slice(g * P, (g + 1) * P)
+                nc.tensor.matmul_mx(out=acc[k][:], lhsT=mx[name, k][0][:, cols].bitcast(fmt[name]), lhsT_scale=mx[name, k][1][:, cols],
+                                    rhs=mx[right, g][0][:].bitcast(fmt[right]), rhs_scale=mx[right, g][1][:],
+                                    start=(name == "dom" and g == 0), stop=(name == "qm" and g == G - 1))
 
         def finish(k):
             stage = ring.tile([P, N], F32, name="stage", tag="stage", bufs=2)
-            nc.scalar.copy(out=stage[:], in_=acc[k][:])
+            cast("V" if k == 0 else "S", stage[:], acc[k][:])
             nc.vector.tensor_copy(out=windows[k][:].indirect(offsets[:]), in_=stage[:])
             nc.sync.dma_start(out=out[k * P:(k + 1) * P, :], in_=windows[k][:])
 
-        cast_q("q", 0, 0, 64, "S")
-        cast_q("q", 0, 64, 96, "V")
-        cast_q("q", 0, 96, 128, "S")
-        quant_group("q", 0, 0)
-        quant_group("q", 0, 1)
-        probs(0)
-        cast_q("do", 0, 0, 64, "V")
-        cast_q("do", 0, 64, 128, "V")
-        quant_group("do", 0, 0)
-        quant_group("do", 0, 1)
-        gates(0)
+        def both(step, name, g):
+            for h in range(2):
+                step(name, g, h)
 
         for h in range(2):
-            for g in range(G):
-                for name, src in (("dom", dom), ("qm", qm)):
-                    raw[name, g, h] = load(src, slice(g * KP, (g + 1) * KP), slice(h * H, (h + 1) * H))
-
-        cast_q("q", 1, 0, 64, "V")
-        cast_q("q", 1, 64, 128, "V")
-        product("pw", 0, 0)
-        quant_group("q", 1, 0)
-        quant_group("q", 1, 1)
-        cast_q("do", 1, 0, 64, "S")
-        cast_q("do", 1, 64, 128, "S")
-        product("pw", 0, 1)
-        probs(1)
-        quant_group("do", 1, 0)
-        quant_group("do", 1, 1)
-        gates(1)
-        product("ds", 0, 0)
-        quant_group("pw", 0, 0)
-        product("ds", 0, 1)
-        quant_group("pw", 0, 1)
-        product("pw", 1, 0)
-        quant_group("ds", 0, 0)
-        product("pw", 1, 1)
-        quant_group("ds", 0, 1)
-        for left, right, g in passes:
-            cast_second(left, g, 0, "S")
+            for u in range(2):
+                cast_q("q", 0, h, u, "S")
+        both(quant_half, "q", 0)
+        for u in range(2):
+            cast_q("do", 0, 0, u, "S")
+        read_banks("q", 0, 1)
+        for u in range(2):
+            cast_q("do", 0, 1, u, "V")
+        both(quant_half, "do", 0)
+        read_banks("do", 0, 1)
+        for u in range(2):
+            cast_q("q", 1, 0, u, "V")
+        both(quant_half, "q", 1)
+        for u in range(2):
+            cast_q("do", 1, 0, u, "S")
+        read_banks("q", 1, 1)
+        for name in ("dom", "qm"):
+            cast_second(name, 0, 0, "S")
+        both(product, "pw", 0)
+        both(product, "ds", 0)
+        both(quant_half, "do", 1)
+        both(quant_half, "pw", 0)
+        both(quant_half, "ds", 0)
+        read_banks("do", 1, 2)
+        for name in ("dom", "qm"):
+            cast_second(name, 1, 0, "S")
+        both(product, "pw", 1)
+        for name in ("dom", "qm"):
+            quant_second(name, 0, 0, 1)
+            out_passes(name, 0, 0, 1)
         product("ds", 1, 0)
-        quant_group("pw", 1, 0)
+        both(quant_half, "pw", 1)
         product("ds", 1, 1)
-        quant_group("pw", 1, 1)
-        quant_group("ds", 1, 0)
-        for left, right, g in passes:
-            quant_second(left, g, 0)
-        quant_group("ds", 1, 1)
-        for i in range(len(passes)):
-            out_pass(0, i)
-        finish(0)
+        quant_half("ds", 1, 0)
+        quant_second("dom", 0, 1, 2)
+        out_passes("dom", 0, 1, 2)
+        quant_half("ds", 1, 1)
+        quant_second("qm", 0, 1, 2)
+        out_passes("qm", 0, 1, 2)
         for k in range(1, DT):
-            for i, (left, right, g) in enumerate(passes):
-                cast_second(left, g, k, "V" if (k > 1 and i >= 2) else "S")
-            for i, (left, right, g) in enumerate(passes):
-                quant_second(left, g, k)
-                out_pass(k, i)
-            finish(k)
+            for name in ("dom", "qm"):
+                for g in range(G):
+                    cast_second(name, g, k, "S")
+                quant_second(name, k, 0, 2)
+                out_passes(name, k, 0, 2)
+            finish(k - 1)
+        finish(DT - 1)

@@ -48,7 +48,7 @@ def tile_attend_gat_lse_c_kernel(tc, qT, cT, doT, lse, delta, rw, qm, dom, offs,
         c_rows = cT.rearrange("(p j) w -> j p w", j=PACK)
         nc.sync.dma_start(out=planes[0][:], in_=c_rows[0])
         nc.sync.dma_start(offsets[:], offs)
-        for j in range(1, PACK - 1):
+        for j in range(1, PACK):
             nc.sync.dma_start(out=planes[j][:], in_=c_rows[j])
 
         vecs = {}
@@ -58,24 +58,21 @@ def tile_attend_gat_lse_c_kernel(tc, qT, cT, doT, lse, delta, rw, qm, dom, offs,
 
         def load(src, rows, cols):
             width = cols.stop - cols.start
-            raw = ring.tile([P, PACK, width], F32, name="raw", tag="raw%d" % width, bufs=12 if width == 256 else 2)
+            raw = ring.tile([P, PACK, width], F32, name="raw", tag="raw%d" % width, bufs=8)
             nc.sync.dma_start(out=raw[:], in_=src[0][rows, cols].rearrange("(p j) w -> p j w", j=PACK))
             return raw
 
         alld = slice(0, D)
         H = KP // 2
         raw = {}
-        first_half = load(qT, alld, slice(0, H))
-        nc.sync.dma_start(out=planes[PACK - 1][:], in_=c_rows[PACK - 1])
-        raw["q", 0] = [first_half, load(qT, alld, slice(H, KP))]
-        raw["do", 0] = [load(doT, alld, slice(h * H, (h + 1) * H)) for h in range(2)]
-        for name, src in (("q", qT), ("do", doT)):
-            whole = load(src, alld, slice(KP, 2 * KP))
-            raw[name, 1] = [whole]
-        for h in range(2):
+        for g in range(G):
+            for name, src in (("q", qT), ("do", doT)):
+                raw[name, g] = [load(src, alld, slice(g * KP, (g + 1) * KP))]
+        for g in range(G):
             for name, src in (("dom", dom), ("qm", qm)):
-                for g in range(G):
-                    raw[name, g, h] = load(src, slice(g * KP, (g + 1) * KP), slice(h * H, (h + 1) * H))
+                whole = load(src, slice(g * KP, (g + 1) * KP), alld)
+                for h in range(2):
+                    raw[name, g, h] = whole[:, :, h * H:(h + 1) * H]
 
         windows = [keep.tile([P, T], F32, name="window%d" % k) for k in range(DT)]
         for k in range(DT):
@@ -88,14 +85,18 @@ def tile_attend_gat_lse_c_kernel(tc, qT, cT, doT, lse, delta, rw, qm, dom, offs,
                                        op0=ALU.mult, op1=ALU.mult)
 
         c_bf = keep.tile([P, N, PACK], BF16, name="c_bf", align_bytes=64)
-        for j in range(PACK):
-            nc.vector.tensor_copy(out=c_bf[:, :, j], in_=planes[j][:].indirect(offsets[:]))
+        early = keep.tile([P, PACK - 1, N], BF16, name="early")
+        for j in range(PACK - 1):
+            nc.vector.tensor_copy(out=early[:, j, :], in_=planes[j][:].indirect(offsets[:]))
+        cast("S", c_bf[:, :, 0:2], early[:, 0:2, :].rearrange("p e n -> p n e"))
+        cast("V", c_bf[:, :, 2], early[:, 2, :])
+        nc.vector.tensor_copy(out=c_bf[:, :, PACK - 1], in_=planes[PACK - 1][:].indirect(offsets[:]))
         c_mx = mx_pair("c", N)
         quantize(c_mx, E4, slice(0, N), c_bf[:].rearrange("p n j -> p (n j)"))
 
 
-        def half_tile(name):
-            return ring.tile([P, H * PACK], BF16, name=name, tag="half", bufs=12, align_bytes=64)
+        def half_tile(name, tag):
+            return ring.tile([P, H * PACK], BF16, name=name, tag=tag, bufs=8 if tag == "half" else 2, align_bytes=64)
 
         fmt = {"q": E4, "do": E5, "qm": E4, "dom": E5, "pw": E4, "ds": E5}
         mx = {}
@@ -103,7 +104,8 @@ def tile_attend_gat_lse_c_kernel(tc, qT, cT, doT, lse, delta, rw, qm, dom, offs,
 
         def halves(name, g):
             if (name, g) not in grp:
-                grp[name, g] = [half_tile(name + "_bf") for u in range(2)]
+                tag = {("do", 1): "even", ("ds", 0): "odd"}.get((name, g), "half")
+                grp[name, g] = [half_tile(name + "_bf", tag) for u in range(2)]
             return grp[name, g]
 
         def cast_q(name, g, part, u, engine):
@@ -146,21 +148,21 @@ def tile_attend_gat_lse_c_kernel(tc, qT, cT, doT, lse, delta, rw, qm, dom, offs,
             (e_sb if name == "q" else g_sb)[g] = tiles
 
         def product(name, g, h):
-            dst = halves(name, g)[h][:].rearrange("p (c i t) -> p c t i", i=4, t=PACK)
-            in0 = e_sb[g][h].rearrange("p t (c i) -> p c t i", i=4)
+            dst = halves(name, g)[h][:].rearrange("p (c i t) -> p c t i", i=2, t=PACK)
+            in0 = e_sb[g][h].rearrange("p t (c i) -> p c t i", i=2)
             if name == "pw":
-                in1 = vecs["rw"][:, g, :].unsqueeze(1).unsqueeze(3).broadcast_to([P, 64, PACK, 4])
+                in1 = vecs["rw"][:, g, :].unsqueeze(1).unsqueeze(3).broadcast_to([P, 128, PACK, 2])
             else:
-                in1 = g_sb[g][h].rearrange("p t (c i) -> p c t i", i=4)
+                in1 = g_sb[g][h].rearrange("p t (c i) -> p c t i", i=2)
             nc.vector.tensor_tensor(out=dst, in0=in0, in1=in1, op=ALU.mult)
 
         second = {}
 
         def cast_second(name, g, k, engine):
             if (name, k) not in second:
-                second[name, k] = ring.tile([P, G, P * PACK], BF16, name="second_bf", tag="second", bufs=4, align_bytes=64)
-            src = raw[name, g, k // 2][:, :, (k % 2) * P:(k % 2 + 1) * P].rearrange("p j (c i) -> p c j i", i=4)
-            cast(engine, second[name, k][:, g, :].rearrange("p (c i j) -> p c j i", i=4, j=PACK), src)
+                second[name, k] = half_tile("second_bf", "odd" if k % 2 else "even")[:].rearrange("p (g w) -> p g w", g=G)
+            src = raw[name, g, k // 2][:, :, (k % 2) * P:(k % 2 + 1) * P].rearrange("p j (c i) -> p c j i", i=2)
+            cast(engine, second[name, k][:, g, :].rearrange("p (c i j) -> p c j i", i=2, j=PACK), src)
 
         def quant_second(name, k, lo, hi):
             if (name, k) not in mx:
@@ -180,9 +182,15 @@ def tile_attend_gat_lse_c_kernel(tc, qT, cT, doT, lse, delta, rw, qm, dom, offs,
                                     rhs=mx[right, g][0][:].bitcast(fmt[right]), rhs_scale=mx[right, g][1][:],
                                     start=(name == "dom" and g == 0), stop=(name == "qm" and g == G - 1))
 
-        def finish(k):
+        stages = {}
+
+        def drain(k):
             stage = ring.tile([P, N], F32, name="stage", tag="stage", bufs=2)
+            stages[k] = stage
             cast("V" if k == 0 else "S", stage[:], acc[k][:])
+
+        def finish(k):
+            stage = stages[k]
             nc.vector.tensor_copy(out=windows[k][:].indirect(offsets[:]), in_=stage[:])
             nc.sync.dma_start(out=out[k * P:(k + 1) * P, :], in_=windows[k][:])
 
@@ -190,15 +198,12 @@ def tile_attend_gat_lse_c_kernel(tc, qT, cT, doT, lse, delta, rw, qm, dom, offs,
             for h in range(2):
                 step(name, g, h)
 
-        for h in range(2):
-            for u in range(2):
-                cast_q("q", 0, h, u, "S")
+        cast_q("q", 0, 0, 0, "V")
+        cast_q("q", 0, 0, 1, "S")
         both(quant_half, "q", 0)
-        for u in range(2):
-            cast_q("do", 0, 0, u, "S")
         read_banks("q", 0, 1)
         for u in range(2):
-            cast_q("do", 0, 1, u, "V")
+            cast_q("do", 0, 0, u, "V")
         both(quant_half, "do", 0)
         read_banks("do", 0, 1)
         for u in range(2):
@@ -207,22 +212,21 @@ def tile_attend_gat_lse_c_kernel(tc, qT, cT, doT, lse, delta, rw, qm, dom, offs,
         for u in range(2):
             cast_q("do", 1, 0, u, "S")
         read_banks("q", 1, 1)
-        for name in ("dom", "qm"):
-            cast_second(name, 0, 0, "S")
         both(product, "pw", 0)
         both(product, "ds", 0)
         both(quant_half, "do", 1)
         both(quant_half, "pw", 0)
         both(quant_half, "ds", 0)
         read_banks("do", 1, 2)
-        for name in ("dom", "qm"):
-            cast_second(name, 1, 0, "S")
+        for g in range(G):
+            for name in ("dom", "qm"):
+                cast_second(name, g, 0, "S")
         both(product, "pw", 1)
+        product("ds", 1, 0)
+        both(quant_half, "pw", 1)
         for name in ("dom", "qm"):
             quant_second(name, 0, 0, 1)
             out_passes(name, 0, 0, 1)
-        product("ds", 1, 0)
-        both(quant_half, "pw", 1)
         product("ds", 1, 1)
         quant_half("ds", 1, 0)
         quant_second("dom", 0, 1, 2)
@@ -230,11 +234,15 @@ def tile_attend_gat_lse_c_kernel(tc, qT, cT, doT, lse, delta, rw, qm, dom, offs,
         quant_half("ds", 1, 1)
         quant_second("qm", 0, 1, 2)
         out_passes("qm", 0, 1, 2)
+        drain(0)
         for k in range(1, DT):
             for name in ("dom", "qm"):
                 for g in range(G):
-                    cast_second(name, g, k, "S")
+                    cast_second(name, g, k, "V" if name == "qm" and (g == 1 or k > 1) else "S")
                 quant_second(name, k, 0, 2)
                 out_passes(name, k, 0, 2)
+            if k > 1:
+                drain(k - 1)
             finish(k - 1)
+        drain(DT - 1)
         finish(DT - 1)

@@ -1,6 +1,7 @@
 from contextlib import ExitStack
 
 import concourse.mybir as mybir
+from concourse.masks import make_identity
 
 N, T, D, R = 512, 2048, 512, 1024
 FLOPS = 4 * 2 * R * N * D
@@ -48,13 +49,21 @@ def tile_attend_gat_lse_c_kernel(tc, qT, cT, doT, lse, delta, rw, qm, dom, offs,
         c_rows = cT.rearrange("(p j) w -> j p w", j=PACK)
         nc.sync.dma_start(out=planes[0][:], in_=c_rows[0])
         nc.sync.dma_start(offsets[:], offs)
+        rows = keep.tile([P, KP], F32, name="rows")
+        nc.vector.memset(rows[:], 0.0)
+        for i, src in enumerate((lse, rw, delta)):
+            nc.sync.dma_start(out=rows[G * i:G * (i + 1), :], in_=src[0].rearrange("(g w) o -> g (w o)", g=G))
         for j in range(1, PACK):
             nc.sync.dma_start(out=planes[j][:], in_=c_rows[j])
 
-        vecs = {}
-        for name, src in (("lse", lse), ("rw", rw), ("delta", delta)):
-            vecs[name] = keep.tile([P, G, PACK], F32, name=name + "_sb")
-            nc.scalar.dma_start(out=vecs[name][:], in_=src[0].rearrange("(g p t) o -> p g (t o)", g=G, t=PACK))
+        identity = keep.tile([P, P], F32, name="identity")
+        make_identity(nc, identity[:])
+        turned = psum.tile([P, PACK, P], F32, name="turned", tag="bank", bufs=8)
+        for t in range(PACK):
+            nc.tensor.transpose(turned[:, t, :], rows[:, t::PACK], identity[:])
+        columns = keep.tile([P, 3, G, PACK], F32, name="columns")
+        nc.scalar.copy(out=columns[:].rearrange("p v g t -> p (v g) t"), in_=turned[:, :, 0:3 * G].rearrange("p t r -> p r t"))
+        vecs = {name: columns[:, i] for i, name in enumerate(("lse", "rw", "delta"))}
 
         def load(src, rows, cols):
             width = cols.stop - cols.start
@@ -88,8 +97,7 @@ def tile_attend_gat_lse_c_kernel(tc, qT, cT, doT, lse, delta, rw, qm, dom, offs,
         early = keep.tile([P, PACK - 1, N], BF16, name="early")
         for j in range(PACK - 1):
             nc.vector.tensor_copy(out=early[:, j, :], in_=planes[j][:].indirect(offsets[:]))
-        cast("S", c_bf[:, :, 0:2], early[:, 0:2, :].rearrange("p e n -> p n e"))
-        cast("V", c_bf[:, :, 2], early[:, 2, :])
+        cast("V", c_bf[:, :, 0:PACK - 1], early[:].rearrange("p j n -> p n j"))
         nc.vector.tensor_copy(out=c_bf[:, :, PACK - 1], in_=planes[PACK - 1][:].indirect(offsets[:]))
         c_mx = mx_pair("c", N)
         quantize(c_mx, E4, slice(0, N), c_bf[:].rearrange("p n j -> p (n j)"))

@@ -33,6 +33,8 @@ def tile_attend_gat_lse_c_kernel(tc, qT, cT, doT, lse, delta, rw, qm, dom, offs,
         def cast(engine, dst, src):
             if engine == "S":
                 nc.scalar.copy(out=dst, in_=src)
+            elif engine == "G":
+                nc.gpsimd.tensor_scalar(out=dst, in0=src, scalar1=1.0, scalar2=0.0, op0=ALU.mult, op1=ALU.add)
             else:
                 nc.vector.tensor_copy(out=dst, in_=src)
 
@@ -58,7 +60,7 @@ def tile_attend_gat_lse_c_kernel(tc, qT, cT, doT, lse, delta, rw, qm, dom, offs,
 
         identity = keep.tile([P, P], F32, name="identity")
         make_identity(nc, identity[:])
-        turned = psum.tile([P, PACK, P], F32, name="turned", tag="bank", bufs=8)
+        turned = psum.tile([P, PACK, P], F32, name="turned")
         for t in range(PACK):
             nc.tensor.transpose(turned[:, t, :], rows[:, t::PACK], identity[:])
         columns = keep.tile([P, 3, G, PACK], F32, name="columns")
@@ -127,11 +129,14 @@ def tile_attend_gat_lse_c_kernel(tc, qT, cT, doT, lse, delta, rw, qm, dom, offs,
                 mx[name, g] = mx_pair("%s%d" % (name, g), KP)
             quantize(mx[name, g], fmt[name], slice(h * H, (h + 1) * H), halves(name, g)[h][:])
 
+        def quant_quarter(i):
+            quantize(mx["ds", 1], E5, slice(H + i * P, H + (i + 1) * P), halves("ds", 1)[1][:, i * KP:(i + 1) * KP])
+
         e_sb = {}
         g_sb = {}
 
         def score(name, g, t):
-            bank = psum.tile([P, N], F32, name="score", tag="bank", bufs=8)
+            bank = psum.tile([P, N], F32, name="score", tag="bank", bufs=7)
             codes, scales = mx[name, g]
             cols = slice(t * P, (t + 1) * P)
             nc.tensor.matmul_mx(out=bank[:], lhsT=codes[:, cols].bitcast(fmt[name]), lhsT_scale=scales[:, cols],
@@ -155,22 +160,23 @@ def tile_attend_gat_lse_c_kernel(tc, qT, cT, doT, lse, delta, rw, qm, dom, offs,
                                              scale=rw_sb[:, u:u + 1])
             (e_sb if name == "q" else g_sb)[g] = tiles
 
-        def product(name, g, h):
-            dst = halves(name, g)[h][:].rearrange("p (c i t) -> p c t i", i=2, t=PACK)
-            in0 = e_sb[g][h].rearrange("p t (c i) -> p c t i", i=2)
+        def product(name, g, h, lo=0, hi=P):
+            dst = halves(name, g)[h][:].rearrange("p (c i t) -> p c t i", i=2, t=PACK)[:, lo:hi]
+            in0 = e_sb[g][h].rearrange("p t (c i) -> p c t i", i=2)[:, lo:hi]
             if name == "pw":
-                in1 = vecs["rw"][:, g, :].unsqueeze(1).unsqueeze(3).broadcast_to([P, 128, PACK, 2])
+                in1 = turned[:, :, G + g].unsqueeze(1).unsqueeze(3).broadcast_to([P, 128, PACK, 2])
             else:
-                in1 = g_sb[g][h].rearrange("p t (c i) -> p c t i", i=2)
+                in1 = g_sb[g][h].rearrange("p t (c i) -> p c t i", i=2)[:, lo:hi]
             nc.vector.tensor_tensor(out=dst, in0=in0, in1=in1, op=ALU.mult)
 
         second = {}
 
         def cast_second(name, g, k, engine):
             if (name, k) not in second:
-                second[name, k] = half_tile("second_bf", "odd" if k % 2 else "even")[:].rearrange("p (g w) -> p g w", g=G)
-            src = raw[name, g, k // 2][:, :, (k % 2) * P:(k % 2 + 1) * P].rearrange("p j (c i) -> p c j i", i=2)
-            cast(engine, second[name, k][:, g, :].rearrange("p (c i j) -> p c j i", i=2, j=PACK), src)
+                second[name, k] = half_tile("second_bf", "even" if k % 2 else "odd")[:].rearrange("p (g w) -> p g w", g=G)
+            run = 1 if engine == "G" else 2
+            src = raw[name, g, k // 2][:, :, (k % 2) * P:(k % 2 + 1) * P].rearrange("p j (c i) -> p c j i", i=run)
+            cast(engine, second[name, k][:, g, :].rearrange("p (c i j) -> p c j i", i=run, j=PACK), src)
 
         def quant_second(name, k, lo, hi):
             if (name, k) not in mx:
@@ -182,7 +188,7 @@ def tile_attend_gat_lse_c_kernel(tc, qT, cT, doT, lse, delta, rw, qm, dom, offs,
 
         def out_passes(name, k, lo, hi):
             if k not in acc:
-                acc[k] = psum.tile([P, N], F32, name="acc", tag="bank", bufs=8)
+                acc[k] = psum.tile([P, N], F32, name="acc", tag="bank", bufs=7)
             right = partner[name]
             for g in range(lo, hi):
                 cols = slice(g * P, (g + 1) * P)
@@ -195,7 +201,7 @@ def tile_attend_gat_lse_c_kernel(tc, qT, cT, doT, lse, delta, rw, qm, dom, offs,
         def drain(k):
             stage = ring.tile([P, N], F32, name="stage", tag="stage", bufs=2)
             stages[k] = stage
-            cast("V" if k == 0 else "S", stage[:], acc[k][:])
+            cast("S", stage[:], acc[k][:])
 
         def finish(k):
             stage = stages[k]
@@ -228,29 +234,33 @@ def tile_attend_gat_lse_c_kernel(tc, qT, cT, doT, lse, delta, rw, qm, dom, offs,
         read_banks("do", 1, 2)
         for g in range(G):
             for name in ("dom", "qm"):
-                cast_second(name, g, 0, "S")
+                cast_second(name, g, 0, "G" if g == 0 else "S")
         both(product, "pw", 1)
         product("ds", 1, 0)
         both(quant_half, "pw", 1)
         for name in ("dom", "qm"):
             quant_second(name, 0, 0, 1)
             out_passes(name, 0, 0, 1)
-        product("ds", 1, 1)
+        product("ds", 1, 1, 0, P // 2)
         quant_half("ds", 1, 0)
         quant_second("dom", 0, 1, 2)
         out_passes("dom", 0, 1, 2)
-        quant_half("ds", 1, 1)
+        product("ds", 1, 1, P // 2, P)
+        quant_quarter(0)
         quant_second("qm", 0, 1, 2)
+        quant_quarter(1)
         out_passes("qm", 0, 1, 2)
-        drain(0)
+        parts = [keep.tile([P, H], F32, name="first%d" % h) for h in range(2)]
+        for h in range(2):
+            nc.vector.tensor_copy(out=parts[h][:], in_=acc[0][:, h * H:(h + 1) * H])
+        for h in range(2):
+            nc.vector.tensor_copy(out=windows[0][:].indirect(offsets[:, h * H // 16:(h + 1) * H // 16]), in_=parts[h][:])
+        nc.sync.dma_start(out=out[0:P, :], in_=windows[0][:])
         for k in range(1, DT):
             for name in ("dom", "qm"):
                 for g in range(G):
                     cast_second(name, g, k, "V" if name == "qm" and (g == 1 or k > 1) else "S")
                 quant_second(name, k, 0, 2)
                 out_passes(name, k, 0, 2)
-            if k > 1:
-                drain(k - 1)
-            finish(k - 1)
-        drain(DT - 1)
-        finish(DT - 1)
+            drain(k)
+            finish(k)

@@ -21,6 +21,7 @@ PACK = 4
 KP = P * PACK
 G = R // KP
 DT = D // P
+SHARE = 64
 
 
 def tile_attend_gat_lse_c_kernel(tc, qT, cT, doT, lse, delta, rw, qm, dom, offs, out):
@@ -118,11 +119,15 @@ def tile_attend_gat_lse_c_kernel(tc, qT, cT, doT, lse, delta, rw, qm, dom, offs,
                 grp[name, g] = [half_tile(name + "_bf", tag) for u in range(2)]
             return grp[name, g]
 
-        def cast_q(name, g, part, u, engine):
+        def cast_q(name, g, part, u, engine, lo=0):
             src = raw[name, g][part][:].rearrange("p j (m u e) -> p u m j e", u=2, e=2)[:, u]
             dst = halves(name, g)[u][:].rearrange("p (e m j) -> p m j e", e=2, j=PACK)
-            width = src.shape[1]
-            cast(engine, dst[:, part * width:(part + 1) * width], src)
+            cast(engine, dst[:, lo:], src[:, lo:])
+
+        def cast_q_plain(name, g, u):
+            src = raw[name, g][0][:].rearrange("p j (m u e) -> p u e m j", u=2, e=2)[:, u, :, 0:SHARE]
+            dst = halves(name, g)[u][:].rearrange("p (e m j) -> p e m j", e=2, j=PACK)[:, :, 0:SHARE]
+            cast("G", dst, src)
 
         def quant_half(name, g, h):
             if (name, g) not in mx:
@@ -223,8 +228,9 @@ def tile_attend_gat_lse_c_kernel(tc, qT, cT, doT, lse, delta, rw, qm, dom, offs,
         for u in range(2):
             cast_q("q", 1, 0, u, "V")
         both(quant_half, "q", 1)
-        for u in range(2):
-            cast_q("do", 1, 0, u, "S")
+        cast_q("do", 1, 0, 0, "S")
+        cast_q("do", 1, 0, 1, "S", SHARE)
+        cast_q_plain("do", 1, 1)
         read_banks("q", 1, 1)
         both(product, "pw", 0)
         both(product, "ds", 0)

@@ -21,7 +21,10 @@ PACK = 4
 KP = P * PACK
 G = R // KP
 DT = D // P
-SHARE = 64
+H = N // 2
+GPSIMD_DO0 = 96
+SCALAR_DO1 = 80
+SEQ_BUFS = 36
 
 
 def tile_attend_gat_lse_c_kernel(tc, qT, cT, doT, lse, delta, rw, qm, dom, offs, out):
@@ -39,16 +42,24 @@ def tile_attend_gat_lse_c_kernel(tc, qT, cT, doT, lse, delta, rw, qm, dom, offs,
             else:
                 nc.vector.tensor_copy(out=dst, in_=src)
 
-        def mx_pair(name, width):
-            codes = keep.tile([P, width], U32, name=name + "_codes", align_bytes=64)
+        def seq_tile(name, width, dtype):
+            return ring.tile([P, width], dtype, name=name, tag="seq", bufs=SEQ_BUFS, align_bytes=64)
+
+        def relay_tile(name):
+            return ring.tile([P, H * PACK], BF16, name=name, tag="relay", bufs=1, align_bytes=64)
+
+        def big_tile(name, shape):
+            return ring.tile(shape, F32, name=name, tag="big", bufs=PACK)
+
+        def quantize(name, fmt, src):
+            width = src.shape[1] // PACK
+            codes = seq_tile(name + "_codes", width, U32)
             scales = keep.tile([P, width], U8, name=name + "_scales", align_bytes=64)
+            nc.vector.quantize_mx(out=codes[:].bitcast(fmt), scales=scales[:], in_=src)
             return codes, scales
 
-        def quantize(pair, fmt, words, src):
-            nc.vector.quantize_mx(out=pair[0][:, words].bitcast(fmt), scales=pair[1][:, words], in_=src)
-
         offsets = keep.tile([P, N // 16], U16, name="offsets")
-        planes = [keep.tile([P, T], F32, name="plane%d" % j) for j in range(PACK)]
+        planes = [big_tile("plane%d" % j, [P, T]) for j in range(PACK)]
         c_rows = cT.rearrange("(p j) w -> j p w", j=PACK)
         nc.sync.dma_start(out=planes[0][:], in_=c_rows[0])
         nc.sync.dma_start(offsets[:], offs)
@@ -59,6 +70,26 @@ def tile_attend_gat_lse_c_kernel(tc, qT, cT, doT, lse, delta, rw, qm, dom, offs,
         for j in range(1, PACK):
             nc.sync.dma_start(out=planes[j][:], in_=c_rows[j])
 
+        def load(name, src, rows, cols):
+            raw = keep.tile([P, PACK, cols.stop - cols.start], F32, name=name)
+            nc.sync.dma_start(out=raw[:], in_=src[0][rows, cols].rearrange("(p j) w -> p j w", j=PACK))
+            return raw
+
+        alld = slice(0, D)
+        raw = {}
+        for name, src in (("q", qT), ("do", doT)):
+            for g in range(G):
+                raw[name, g] = load("%s%d" % (name, g), src, alld, slice(g * KP, (g + 1) * KP))
+        for name, src in (("dom", dom), ("qm", qm)):
+            whole = load(name + "0", src, slice(0, KP), alld)
+            for k in range(DT):
+                raw[name, 0, k] = whole[:, :, k * P:(k + 1) * P]
+        for h in range(2):
+            for name, src in (("dom", dom), ("qm", qm)):
+                half = load("%s1%d" % (name, h), src, slice(KP, R), slice(h * H, (h + 1) * H))
+                for i in range(2):
+                    raw[name, 1, 2 * h + i] = half[:, :, i * P:(i + 1) * P]
+
         identity = keep.tile([P, P], F32, name="identity")
         make_identity(nc, identity[:])
         turned = psum.tile([P, PACK, P], F32, name="turned")
@@ -66,207 +97,177 @@ def tile_attend_gat_lse_c_kernel(tc, qT, cT, doT, lse, delta, rw, qm, dom, offs,
             nc.tensor.transpose(turned[:, t, :], rows[:, t::PACK], identity[:])
         columns = keep.tile([P, 3, G, PACK], F32, name="columns")
         nc.scalar.copy(out=columns[:].rearrange("p v g t -> p (v g) t"), in_=turned[:, :, 0:3 * G].rearrange("p t r -> p r t"))
-        vecs = {name: columns[:, i] for i, name in enumerate(("lse", "rw", "delta"))}
-
-        def load(src, rows, cols):
-            width = cols.stop - cols.start
-            raw = ring.tile([P, PACK, width], F32, name="raw", tag="raw%d" % width, bufs=8)
-            nc.sync.dma_start(out=raw[:], in_=src[0][rows, cols].rearrange("(p j) w -> p j w", j=PACK))
-            return raw
-
-        alld = slice(0, D)
-        H = KP // 2
-        raw = {}
-        for g in range(G):
-            for name, src in (("q", qT), ("do", doT)):
-                raw[name, g] = [load(src, alld, slice(g * KP, (g + 1) * KP))]
-        for g in range(G):
-            for name, src in (("dom", dom), ("qm", qm)):
-                whole = load(src, slice(g * KP, (g + 1) * KP), alld)
-                for h in range(2):
-                    raw[name, g, h] = whole[:, :, h * H:(h + 1) * H]
+        vecs = {name: columns[:, i].rearrange("p g t -> p (g t)") for i, name in enumerate(("lse", "rw", "delta"))}
 
         windows = [keep.tile([P, T], F32, name="window%d" % k) for k in range(DT)]
         for k in range(DT):
             nc.vector.memset(windows[k][:], 0.0)
         neg_lse = keep.tile([P, G * PACK], F32, name="neg_lse")
-        nc.scalar.activation(out=neg_lse[:], in_=vecs["lse"][:].rearrange("p g t -> p (g t)"), func=ACT.Identity, scale=-1.0)
-        rw_sb = vecs["rw"][:].rearrange("p g t -> p (g t)")
+        nc.scalar.activation(out=neg_lse[:], in_=vecs["lse"], func=ACT.Identity, scale=-1.0)
         neg_rwd = keep.tile([P, G * PACK], F32, name="neg_rwd")
-        nc.vector.scalar_tensor_tensor(out=neg_rwd[:], in0=vecs["delta"][:].rearrange("p g t -> p (g t)"), scalar=-1.0, in1=rw_sb,
-                                       op0=ALU.mult, op1=ALU.mult)
+        nc.vector.scalar_tensor_tensor(out=neg_rwd[:], in0=vecs["delta"], scalar=-1.0, in1=vecs["rw"], op0=ALU.mult, op1=ALU.mult)
 
         c_bf = keep.tile([P, N, PACK], BF16, name="c_bf", align_bytes=64)
         early = keep.tile([P, PACK - 1, N], BF16, name="early")
         for j in range(PACK - 1):
-            nc.vector.tensor_copy(out=early[:, j, :], in_=planes[j][:].indirect(offsets[:]))
+            nc.scalar.activation(out=early[:, j, :], in_=planes[j][:].indirect(offsets[:]), func=ACT.Copy)
         cast("V", c_bf[:, :, 0:PACK - 1], early[:].rearrange("p j n -> p n j"))
         nc.vector.tensor_copy(out=c_bf[:, :, PACK - 1], in_=planes[PACK - 1][:].indirect(offsets[:]))
-        c_mx = mx_pair("c", N)
-        quantize(c_mx, E4, slice(0, N), c_bf[:].rearrange("p n j -> p (n j)"))
-
-
-        def half_tile(name, tag):
-            return ring.tile([P, H * PACK], BF16, name=name, tag=tag, bufs=8 if tag == "half" else 2, align_bytes=64)
+        c_mx = quantize("c", E4, c_bf[:].rearrange("p n j -> p (n j)"))
 
         fmt = {"q": E4, "do": E5, "qm": E4, "dom": E5, "pw": E4, "ds": E5}
+        bf = {}
         mx = {}
-        grp = {}
 
-        def halves(name, g):
-            if (name, g) not in grp:
-                tag = {("do", 1): "even", ("ds", 0): "odd"}.get((name, g), "half")
-                grp[name, g] = [half_tile(name + "_bf", tag) for u in range(2)]
-            return grp[name, g]
+        def cast_queries(engine, name, g, u, lo=0, hi=P, make=None):
+            if make is not None:
+                bf[name, g, u] = make("%s%d%d_bf" % (name, g, u))
+            order = "e m j" if engine == "G" else "m j e"
+            src = raw[name, g][:].rearrange("p j (m u e) -> p u j m e", u=2, e=2)[:, u, :, lo:hi].rearrange("p j m e -> p " + order)
+            dst = bf[name, g, u][:].rearrange("p (e m j) -> p e m j", e=2, j=PACK)[:, :, lo:hi].rearrange("p e m j -> p " + order)
+            cast(engine, dst, src)
 
-        def cast_q(name, g, part, u, engine, lo=0):
-            src = raw[name, g][part][:].rearrange("p j (m u e) -> p u m j e", u=2, e=2)[:, u]
-            dst = halves(name, g)[u][:].rearrange("p (e m j) -> p m j e", e=2, j=PACK)
-            cast(engine, dst[:, lo:], src[:, lo:])
+        def in_seq(name):
+            return seq_tile(name, H * PACK, BF16)
 
-        def cast_q_plain(name, g, u):
-            src = raw[name, g][0][:].rearrange("p j (m u e) -> p u e m j", u=2, e=2)[:, u, :, 0:SHARE]
-            dst = halves(name, g)[u][:].rearrange("p (e m j) -> p e m j", e=2, j=PACK)[:, :, 0:SHARE]
-            cast("G", dst, src)
+        def quant(name, g, h):
+            mx[name, g, h] = quantize("%s%d%d" % (name, g, h), fmt[name], bf[name, g, h][:])
 
-        def quant_half(name, g, h):
-            if (name, g) not in mx:
-                mx[name, g] = mx_pair("%s%d" % (name, g), KP)
-            quantize(mx[name, g], fmt[name], slice(h * H, (h + 1) * H), halves(name, g)[h][:])
+        def bank_tile(width):
+            return psum.tile([P, width], F32, name="bank", tag="bank", bufs=7)
 
-        def quant_quarter(i):
-            quantize(mx["ds", 1], E5, slice(H + i * P, H + (i + 1) * P), halves("ds", 1)[1][:, i * KP:(i + 1) * KP])
+        read = {}
 
-        e_sb = {}
-        g_sb = {}
-
-        def score(name, g, t):
-            bank = psum.tile([P, N], F32, name="score", tag="bank", bufs=7)
-            codes, scales = mx[name, g]
-            cols = slice(t * P, (t + 1) * P)
+        def score(name, g, t, lo, hi):
+            if (name, g) not in read:
+                read[name, g] = big_tile("%s%d_read" % (name, g), [P, 2, PACK, H])
+            bank = bank_tile((hi - lo) * H)
+            codes, scales = mx[name, g, t // 2]
+            cols = slice((t % 2) * P, (t % 2 + 1) * P)
+            slots = slice(lo * H, hi * H)
             nc.tensor.matmul_mx(out=bank[:], lhsT=codes[:, cols].bitcast(fmt[name]), lhsT_scale=scales[:, cols],
-                                rhs=c_mx[0][:].bitcast(E4), rhs_scale=c_mx[1][:], start=True, stop=True)
-            return bank
-
-        def read_banks(name, g, parts):
-            banks = [score(name, g, t) for t in range(PACK)]
-            width = N // parts
-            tiles = []
-            for part in range(parts):
-                tile = keep.tile([P, PACK, width], F32, name="%s_f32_%d_%d" % (name, g, part))
-                tiles.extend([tile[:, :, i * H:(i + 1) * H] for i in range(width // H)])
-                cols = slice(part * width, (part + 1) * width)
-                for t in range(PACK):
-                    u = g * PACK + t
-                    if name == "q":
-                        nc.scalar.activation(out=tile[:, t, :], in_=banks[t][:, cols], func=ACT.Exp, bias=neg_lse[:, u:u + 1], scale=1.0)
-                    else:
-                        nc.scalar.activation(out=tile[:, t, :], in_=banks[t][:, cols], func=ACT.Identity, bias=neg_rwd[:, u:u + 1],
-                                             scale=rw_sb[:, u:u + 1])
-            (e_sb if name == "q" else g_sb)[g] = tiles
-
-        def product(name, g, h, lo=0, hi=P):
-            dst = halves(name, g)[h][:].rearrange("p (c i t) -> p c t i", i=2, t=PACK)[:, lo:hi]
-            in0 = e_sb[g][h].rearrange("p t (c i) -> p c t i", i=2)[:, lo:hi]
-            if name == "pw":
-                in1 = turned[:, :, G + g].unsqueeze(1).unsqueeze(3).broadcast_to([P, 128, PACK, 2])
+                                rhs=c_mx[0][:, slots].bitcast(E4), rhs_scale=c_mx[1][:, slots], start=True, stop=True)
+            u = g * PACK + t
+            dst = read[name, g][:, lo:hi, t, :]
+            src = bank[:].rearrange("p (h n) -> p h n", n=H)
+            if name == "q":
+                nc.scalar.activation(out=dst, in_=src, func=ACT.Exp, bias=neg_lse[:, u:u + 1], scale=1.0)
             else:
-                in1 = g_sb[g][h].rearrange("p t (c i) -> p c t i", i=2)[:, lo:hi]
+                nc.scalar.activation(out=dst, in_=src, func=ACT.Identity, bias=neg_rwd[:, u:u + 1], scale=vecs["rw"][:, u:u + 1])
+
+        def product(name, g, h):
+            bf[name, g, h] = in_seq("%s%d%d_bf" % (name, g, h))
+            dst = bf[name, g, h][:].rearrange("p (c i t) -> p c t i", i=2, t=PACK)
+            in0 = read["q", g][:, h].rearrange("p t (c i) -> p c t i", i=2)
+            if name == "pw":
+                in1 = turned[:, :, G + g].unsqueeze(1).unsqueeze(3).broadcast_to([P, H // 2, PACK, 2])
+            else:
+                in1 = read["do", g][:, h].rearrange("p t (c i) -> p c t i", i=2)
             nc.vector.tensor_tensor(out=dst, in0=in0, in1=in1, op=ALU.mult)
 
-        second = {}
+        def cast_rows(engine, name, k):
+            bf[name, k] = in_seq("%s_bf%d" % (name, k))
+            for g in range(G):
+                src = raw[name, g, k].rearrange("p j (c i) -> p c j i", i=2)
+                dst = bf[name, k][:, g * KP:(g + 1) * KP].rearrange("p (c i j) -> p c j i", i=2, j=PACK)
+                cast(engine, dst, src)
 
-        def cast_second(name, g, k, engine):
-            if (name, k) not in second:
-                second[name, k] = half_tile("second_bf", "even" if k % 2 else "odd")[:].rearrange("p (g w) -> p g w", g=G)
-            run = 1 if engine == "G" else 2
-            src = raw[name, g, k // 2][:, :, (k % 2) * P:(k % 2 + 1) * P].rearrange("p j (c i) -> p c j i", i=run)
-            cast(engine, second[name, k][:, g, :].rearrange("p (c i j) -> p c j i", i=run, j=PACK), src)
-
-        def quant_second(name, k, lo, hi):
-            if (name, k) not in mx:
-                mx[name, k] = mx_pair("%s%d" % (name, k), G * P)
-            quantize(mx[name, k], fmt[name], slice(lo * P, hi * P), second[name, k][:, lo:hi, :].rearrange("p g w -> p (g w)"))
+        def quant_rows(name, k):
+            mx[name, k] = quantize("%s%d" % (name, k), fmt[name], bf[name, k][:])
 
         acc = {}
         partner = {"dom": "pw", "qm": "ds"}
 
-        def out_passes(name, k, lo, hi):
-            if k not in acc:
-                acc[k] = psum.tile([P, N], F32, name="acc", tag="bank", bufs=7)
+        def out_passes(name, k, h):
+            if (k, h) not in acc:
+                acc[k, h] = bank_tile(H)
             right = partner[name]
-            for g in range(lo, hi):
+            for g in range(G):
                 cols = slice(g * P, (g + 1) * P)
-                nc.tensor.matmul_mx(out=acc[k][:], lhsT=mx[name, k][0][:, cols].bitcast(fmt[name]), lhsT_scale=mx[name, k][1][:, cols],
-                                    rhs=mx[right, g][0][:].bitcast(fmt[right]), rhs_scale=mx[right, g][1][:],
+                nc.tensor.matmul_mx(out=acc[k, h][:], lhsT=mx[name, k][0][:, cols].bitcast(fmt[name]), lhsT_scale=mx[name, k][1][:, cols],
+                                    rhs=mx[right, g, h][0][:].bitcast(fmt[right]), rhs_scale=mx[right, g, h][1][:],
                                     start=(name == "dom" and g == 0), stop=(name == "qm" and g == G - 1))
 
-        stages = {}
+        stage = {}
 
-        def drain(k):
-            stage = ring.tile([P, N], F32, name="stage", tag="stage", bufs=2)
-            stages[k] = stage
-            cast("S", stage[:], acc[k][:])
+        def drain(k, h):
+            stage[k, h] = ring.tile([P, H], F32, name="stage", tag="stage", bufs=4)
+            cast("S", stage[k, h][:], acc[k, h][:])
 
-        def finish(k):
-            stage = stages[k]
-            nc.vector.tensor_copy(out=windows[k][:].indirect(offsets[:]), in_=stage[:])
+        def scatter(k, h):
+            cols = slice(h * H // 16, (h + 1) * H // 16)
+            nc.scalar.activation(out=windows[k][:].indirect(offsets[:, cols]), in_=stage[k, h][:], func=ACT.Copy)
+
+        def store(k):
             nc.sync.dma_start(out=out[k * P:(k + 1) * P, :], in_=windows[k][:])
 
-        def both(step, name, g):
-            for h in range(2):
-                step(name, g, h)
-
-        cast_q("q", 0, 0, 0, "V")
-        cast_q("q", 0, 0, 1, "S")
-        both(quant_half, "q", 0)
-        read_banks("q", 0, 1)
-        for u in range(2):
-            cast_q("do", 0, 0, u, "V")
-        both(quant_half, "do", 0)
-        read_banks("do", 0, 1)
-        for u in range(2):
-            cast_q("q", 1, 0, u, "V")
-        both(quant_half, "q", 1)
-        cast_q("do", 1, 0, 0, "S")
-        cast_q("do", 1, 0, 1, "S", SHARE)
-        cast_q_plain("do", 1, 1)
-        read_banks("q", 1, 1)
-        both(product, "pw", 0)
-        both(product, "ds", 0)
-        both(quant_half, "do", 1)
-        both(quant_half, "pw", 0)
-        both(quant_half, "ds", 0)
-        read_banks("do", 1, 2)
-        for g in range(G):
-            for name in ("dom", "qm"):
-                cast_second(name, g, 0, "G" if g == 0 else "S")
-        both(product, "pw", 1)
+        cast_queries("V", "q", 0, 0, make=in_seq)
+        cast_queries("S", "q", 0, 1, make=relay_tile)
+        quant("q", 0, 0)
+        quant("q", 0, 1)
+        for h in range(2):
+            for t in range(PACK):
+                score("q", 0, t, h, h + 1)
+        cast_queries("V", "q", 1, 0, make=relay_tile)
+        quant("q", 1, 0)
+        cast_queries("G", "q", 1, 1, make=relay_tile)
+        product("pw", 0, 0)
+        quant("q", 1, 1)
+        for t in range(PACK):
+            score("q", 1, t, 0, 2)
+        cast_queries("G", "do", 0, 0, 0, GPSIMD_DO0, make=relay_tile)
+        product("pw", 0, 1)
+        cast_queries("V", "do", 0, 1, make=in_seq)
+        cast_queries("S", "do", 1, 0, 0, SCALAR_DO1, make=in_seq)
+        cast_queries("V", "do", 0, 0, GPSIMD_DO0, P)
+        quant("do", 0, 1)
+        quant("do", 0, 0)
+        for t in (2, 3, 0, 1):
+            score("do", 0, t, 0, 2)
+        cast_queries("G", "do", 1, 1, make=relay_tile)
+        cast_queries("G", "do", 1, 0, SCALAR_DO1, P)
+        product("pw", 1, 0)
+        product("pw", 1, 1)
+        quant("do", 1, 1)
+        quant("do", 1, 0)
+        for t in (2, 3, 0, 1):
+            score("do", 1, t, 0, 2)
+        product("ds", 0, 0)
+        quant("pw", 0, 0)
+        quant("pw", 1, 0)
+        product("ds", 0, 1)
+        cast_rows("S", "dom", 0)
+        cast_rows("S", "qm", 0)
+        cast_rows("S", "dom", 1)
+        quant("ds", 0, 0)
         product("ds", 1, 0)
-        both(quant_half, "pw", 1)
-        for name in ("dom", "qm"):
-            quant_second(name, 0, 0, 1)
-            out_passes(name, 0, 0, 1)
-        product("ds", 1, 1, 0, P // 2)
-        quant_half("ds", 1, 0)
-        quant_second("dom", 0, 1, 2)
-        out_passes("dom", 0, 1, 2)
-        product("ds", 1, 1, P // 2, P)
-        quant_quarter(0)
-        quant_second("qm", 0, 1, 2)
-        quant_quarter(1)
-        out_passes("qm", 0, 1, 2)
-        parts = [keep.tile([P, H], F32, name="first%d" % h) for h in range(2)]
+        quant("pw", 0, 1)
+        quant("pw", 1, 1)
+        quant("ds", 1, 0)
+        quant_rows("dom", 0)
         for h in range(2):
-            nc.vector.tensor_copy(out=parts[h][:], in_=acc[0][:, h * H:(h + 1) * H])
-        for h in range(2):
-            nc.vector.tensor_copy(out=windows[0][:].indirect(offsets[:, h * H // 16:(h + 1) * H // 16]), in_=parts[h][:])
-        nc.sync.dma_start(out=out[0:P, :], in_=windows[0][:])
+            out_passes("dom", 0, h)
+        quant_rows("qm", 0)
+        out_passes("qm", 0, 0)
+        drain(0, 0)
+        scatter(0, 0)
+        product("ds", 1, 1)
+        quant("ds", 0, 1)
+        quant("ds", 1, 1)
+        out_passes("qm", 0, 1)
+        drain(0, 1)
+        scatter(0, 1)
+        store(0)
         for k in range(1, DT):
+            if k > 1:
+                cast_rows("V", "dom", k)
+            cast_rows("V", "qm", k)
             for name in ("dom", "qm"):
-                for g in range(G):
-                    cast_second(name, g, k, "V" if name == "qm" and (g == 1 or k > 1) else "S")
-                quant_second(name, k, 0, 2)
-                out_passes(name, k, 0, 2)
-            drain(k)
-            finish(k)
+                quant_rows(name, k)
+                for h in range(2):
+                    out_passes(name, k, h)
+            for h in range(2):
+                drain(k, h)
+            for h in range(2):
+                scatter(k, h)
+            store(k)

@@ -22,8 +22,6 @@ KP = P * PACK
 G = R // KP
 DT = D // P
 H = N // 2
-GPSIMD_DO0 = 96
-SCALAR_DO1 = 80
 SEQ_BUFS = 36
 
 
@@ -209,44 +207,42 @@ def tile_attend_gat_lse_c_kernel(tc, qT, cT, doT, lse, delta, rw, qm, dom, offs,
             for t in range(PACK):
                 score("q", 0, t, h, h + 1)
         cast_queries("V", "q", 1, 0, make=relay_tile)
+        cast_queries("V", "q", 1, 1, make=in_seq)
         quant("q", 1, 0)
-        cast_queries("G", "q", 1, 1, make=relay_tile)
-        product("pw", 0, 0)
         quant("q", 1, 1)
         for t in range(PACK):
             score("q", 1, t, 0, 2)
-        cast_queries("G", "do", 0, 0, 0, GPSIMD_DO0, make=relay_tile)
+        product("pw", 0, 0)
         product("pw", 0, 1)
-        cast_queries("V", "do", 0, 1, make=in_seq)
-        cast_queries("S", "do", 1, 0, 0, SCALAR_DO1, make=in_seq)
-        cast_queries("V", "do", 0, 0, GPSIMD_DO0, P)
-        quant("do", 0, 1)
-        quant("do", 0, 0)
-        for t in (2, 3, 0, 1):
+        for u in range(2):
+            cast_queries("V", "do", 0, u, make=in_seq)
+        for u in range(2):
+            cast_queries("S", "do", 1, u, make=in_seq)
+        for u in range(2):
+            quant("do", 0, u)
+        for t in range(PACK):
             score("do", 0, t, 0, 2)
-        cast_queries("G", "do", 1, 1, make=relay_tile)
-        cast_queries("G", "do", 1, 0, SCALAR_DO1, P)
+        quant("pw", 0, 0)
+        quant("pw", 0, 1)
         product("pw", 1, 0)
         product("pw", 1, 1)
-        quant("do", 1, 1)
-        quant("do", 1, 0)
-        for t in (2, 3, 0, 1):
+        for u in range(2):
+            quant("do", 1, u)
+        for t in range(PACK):
             score("do", 1, t, 0, 2)
         product("ds", 0, 0)
-        quant("pw", 0, 0)
         quant("pw", 1, 0)
+        quant("pw", 1, 1)
         product("ds", 0, 1)
         cast_rows("S", "dom", 0)
         cast_rows("S", "qm", 0)
         cast_rows("S", "dom", 1)
         quant("ds", 0, 0)
         product("ds", 1, 0)
-        quant("pw", 0, 1)
-        quant("pw", 1, 1)
-        quant("ds", 1, 0)
         quant_rows("dom", 0)
         for h in range(2):
             out_passes("dom", 0, h)
+        quant("ds", 1, 0)
         quant_rows("qm", 0)
         out_passes("qm", 0, 0)
         drain(0, 0)

@@ -75,18 +75,16 @@ def tile_attend_gat_lse_c_kernel(tc, qT, cT, doT, lse, delta, rw, qm, dom, offs,
 
         alld = slice(0, D)
         raw = {}
-        for name, src in (("q", qT), ("do", doT)):
-            for g in range(G):
-                raw[name, g] = load("%s%d" % (name, g), src, alld, slice(g * KP, (g + 1) * KP))
-        for name, src in (("dom", dom), ("qm", qm)):
-            whole = load(name + "0", src, slice(0, KP), alld)
-            for k in range(DT):
-                raw[name, 0, k] = whole[:, :, k * P:(k + 1) * P]
+        raw["q", 0] = [load("q0", qT, alld, slice(0, KP))]
+        raw["q", 1] = [load("q1%d" % i, qT, alld, slice(KP + i * H, KP + (i + 1) * H)) for i in range(2)]
+        for g in range(G):
+            raw["do", g] = [load("do%d" % g, doT, alld, slice(g * KP, (g + 1) * KP))]
         for h in range(2):
-            for name, src in (("dom", dom), ("qm", qm)):
-                half = load("%s1%d" % (name, h), src, slice(KP, R), slice(h * H, (h + 1) * H))
-                for i in range(2):
-                    raw[name, 1, 2 * h + i] = half[:, :, i * P:(i + 1) * P]
+            for g in range(G):
+                for name, src in (("dom", dom), ("qm", qm)):
+                    half = load("%s%d%d" % (name, g, h), src, slice(g * KP, (g + 1) * KP), slice(h * H, (h + 1) * H))
+                    for i in range(2):
+                        raw[name, g, 2 * h + i] = half[:, :, i * P:(i + 1) * P]
 
         identity = keep.tile([P, P], F32, name="identity")
         make_identity(nc, identity[:])
@@ -117,12 +115,12 @@ def tile_attend_gat_lse_c_kernel(tc, qT, cT, doT, lse, delta, rw, qm, dom, offs,
         bf = {}
         mx = {}
 
-        def cast_queries(engine, name, g, u, lo=0, hi=P, make=None):
-            if make is not None:
+        def cast_queries(engine, name, g, u, make, part=0):
+            if part == 0:
                 bf[name, g, u] = make("%s%d%d_bf" % (name, g, u))
-            order = "e m j" if engine == "G" else "m j e"
-            src = raw[name, g][:].rearrange("p j (m u e) -> p u j m e", u=2, e=2)[:, u, :, lo:hi].rearrange("p j m e -> p " + order)
-            dst = bf[name, g, u][:].rearrange("p (e m j) -> p e m j", e=2, j=PACK)[:, :, lo:hi].rearrange("p e m j -> p " + order)
+            width = P // len(raw[name, g])
+            src = raw[name, g][part][:].rearrange("p j (m u e) -> p u m j e", u=2, e=2)[:, u]
+            dst = bf[name, g, u][:].rearrange("p (e m j) -> p m j e", e=2, j=PACK)[:, part * width:(part + 1) * width]
             cast(engine, dst, src)
 
         def in_seq(name):
@@ -153,8 +151,8 @@ def tile_attend_gat_lse_c_kernel(tc, qT, cT, doT, lse, delta, rw, qm, dom, offs,
             else:
                 nc.scalar.activation(out=dst, in_=src, func=ACT.Identity, bias=neg_rwd[:, u:u + 1], scale=vecs["rw"][:, u:u + 1])
 
-        def product(name, g, h):
-            bf[name, g, h] = in_seq("%s%d%d_bf" % (name, g, h))
+        def product(name, g, h, make=in_seq):
+            bf[name, g, h] = make("%s%d%d_bf" % (name, g, h))
             dst = bf[name, g, h][:].rearrange("p (c i t) -> p c t i", i=2, t=PACK)
             in0 = read["q", g][:, h].rearrange("p t (c i) -> p c t i", i=2)
             if name == "pw":
@@ -163,26 +161,29 @@ def tile_attend_gat_lse_c_kernel(tc, qT, cT, doT, lse, delta, rw, qm, dom, offs,
                 in1 = read["do", g][:, h].rearrange("p t (c i) -> p c t i", i=2)
             nc.vector.tensor_tensor(out=dst, in0=in0, in1=in1, op=ALU.mult)
 
-        def cast_rows(engine, name, k):
-            bf[name, k] = in_seq("%s_bf%d" % (name, k))
-            for g in range(G):
-                src = raw[name, g, k].rearrange("p j (c i) -> p c j i", i=2)
-                dst = bf[name, k][:, g * KP:(g + 1) * KP].rearrange("p (c i j) -> p c j i", i=2, j=PACK)
+        def cast_rows(engine, name, k, lo=0, hi=G, make=in_seq):
+            bf[name, k, lo] = make("%s_bf%d%d" % (name, k, lo))
+            run = 1 if engine == "G" else 2
+            for g in range(lo, hi):
+                src = raw[name, g, k].rearrange("p j (c i) -> p c j i", i=run)
+                dst = bf[name, k, lo][:, (g - lo) * KP:(g - lo + 1) * KP].rearrange("p (c i j) -> p c j i", i=run, j=PACK)
                 cast(engine, dst, src)
 
-        def quant_rows(name, k):
-            mx[name, k] = quantize("%s%d" % (name, k), fmt[name], bf[name, k][:])
+        def quant_rows(name, k, lo=0, hi=G):
+            codes, scales = quantize("%s%d%d" % (name, k, lo), fmt[name], bf[name, k, lo][:, 0:(hi - lo) * KP])
+            for g in range(lo, hi):
+                cols = slice((g - lo) * P, (g - lo + 1) * P)
+                mx[name, k, g] = codes[:, cols], scales[:, cols]
 
         acc = {}
         partner = {"dom": "pw", "qm": "ds"}
 
-        def out_passes(name, k, h):
+        def out_passes(name, k, h, lo=0, hi=G):
             if (k, h) not in acc:
                 acc[k, h] = bank_tile(H)
             right = partner[name]
-            for g in range(G):
-                cols = slice(g * P, (g + 1) * P)
-                nc.tensor.matmul_mx(out=acc[k, h][:], lhsT=mx[name, k][0][:, cols].bitcast(fmt[name]), lhsT_scale=mx[name, k][1][:, cols],
+            for g in range(lo, hi):
+                nc.tensor.matmul_mx(out=acc[k, h][:], lhsT=mx[name, k, g][0].bitcast(fmt[name]), lhsT_scale=mx[name, k, g][1],
                                     rhs=mx[right, g, h][0][:].bitcast(fmt[right]), rhs_scale=mx[right, g, h][1][:],
                                     start=(name == "dom" and g == 0), stop=(name == "qm" and g == G - 1))
 
@@ -192,6 +193,10 @@ def tile_attend_gat_lse_c_kernel(tc, qT, cT, doT, lse, delta, rw, qm, dom, offs,
             stage[k, h] = ring.tile([P, H], F32, name="stage", tag="stage", bufs=4)
             cast("S", stage[k, h][:], acc[k, h][:])
 
+        def out_pass(name, k, g):
+            for h in range(2):
+                out_passes(name, k, h, g, g + 1)
+
         def scatter(k, h):
             cols = slice(h * H // 16, (h + 1) * H // 16)
             nc.scalar.activation(out=windows[k][:].indirect(offsets[:, cols]), in_=stage[k, h][:], func=ACT.Copy)
@@ -199,47 +204,52 @@ def tile_attend_gat_lse_c_kernel(tc, qT, cT, doT, lse, delta, rw, qm, dom, offs,
         def store(k):
             nc.sync.dma_start(out=out[k * P:(k + 1) * P, :], in_=windows[k][:])
 
-        cast_queries("V", "q", 0, 0, make=in_seq)
-        cast_queries("S", "q", 0, 1, make=relay_tile)
+        cast_queries("V", "q", 0, 0, in_seq)
+        cast_queries("S", "q", 0, 1, relay_tile)
         quant("q", 0, 0)
         quant("q", 0, 1)
         for h in range(2):
             for t in range(PACK):
                 score("q", 0, t, h, h + 1)
-        cast_queries("V", "q", 1, 0, make=relay_tile)
-        cast_queries("V", "q", 1, 1, make=in_seq)
+        for part in range(2):
+            cast_queries("V", "q", 1, 0, relay_tile, part)
+            cast_queries("V", "q", 1, 1, in_seq, part)
         quant("q", 1, 0)
         quant("q", 1, 1)
         for t in range(PACK):
             score("q", 1, t, 0, 2)
-        product("pw", 0, 0)
+        product("pw", 0, 0, relay_tile)
         product("pw", 0, 1)
-        for u in range(2):
-            cast_queries("V", "do", 0, u, make=in_seq)
-        for u in range(2):
-            cast_queries("S", "do", 1, u, make=in_seq)
-        for u in range(2):
-            quant("do", 0, u)
-        for t in range(PACK):
-            score("do", 0, t, 0, 2)
+        cast_queries("V", "do", 0, 0, in_seq)
         quant("pw", 0, 0)
+        cast_queries("S", "do", 0, 1, relay_tile)
+        quant("do", 0, 0)
+        for t in (0, 1):
+            score("do", 0, t, 0, 2)
+        cast_queries("V", "do", 1, 0, in_seq)
+        cast_queries("S", "do", 1, 1, in_seq)
         quant("pw", 0, 1)
+        quant("do", 1, 0)
+        quant("do", 0, 1)
+        for t in (2, 3):
+            score("do", 0, t, 0, 2)
+        cast_rows("G", "dom", 0, 0, 1, relay_tile)
         product("pw", 1, 0)
         product("pw", 1, 1)
-        for u in range(2):
-            quant("do", 1, u)
+        quant("do", 1, 1)
         for t in range(PACK):
             score("do", 1, t, 0, 2)
-        product("ds", 0, 0)
         quant("pw", 1, 0)
         quant("pw", 1, 1)
+        quant_rows("dom", 0, 0, 1)
+        product("ds", 0, 0)
         product("ds", 0, 1)
-        cast_rows("S", "dom", 0)
+        cast_rows("S", "dom", 0, 1, 2)
         cast_rows("S", "qm", 0)
         cast_rows("S", "dom", 1)
         quant("ds", 0, 0)
         product("ds", 1, 0)
-        quant_rows("dom", 0)
+        quant_rows("dom", 0, 1, 2)
         for h in range(2):
             out_passes("dom", 0, h)
         quant("ds", 1, 0)
@@ -248,6 +258,7 @@ def tile_attend_gat_lse_c_kernel(tc, qT, cT, doT, lse, delta, rw, qm, dom, offs,
         drain(0, 0)
         scatter(0, 0)
         product("ds", 1, 1)
+        cast_rows("S", "qm", 1, 0, 1)
         quant("ds", 0, 1)
         quant("ds", 1, 1)
         out_passes("qm", 0, 1)
@@ -257,13 +268,25 @@ def tile_attend_gat_lse_c_kernel(tc, qT, cT, doT, lse, delta, rw, qm, dom, offs,
         for k in range(1, DT):
             if k > 1:
                 cast_rows("V", "dom", k)
-            cast_rows("V", "qm", k)
-            for name in ("dom", "qm"):
-                quant_rows(name, k)
+                cast_rows("V", "qm", k, 0, 1)
+            else:
+                cast_rows("V", "qm", k, 1, 2)
+            quant_rows("dom", k)
+            for h in range(2):
+                out_passes("dom", k, h)
+            if k > 1:
+                cast_rows("V", "qm", k, 1, 2)
+            for g in range(G):
+                quant_rows("qm", k, g, g + 1)
+                out_pass("qm", k, g)
+            if k < DT - 1:
                 for h in range(2):
-                    out_passes(name, k, h)
-            for h in range(2):
-                drain(k, h)
-            for h in range(2):
-                scatter(k, h)
+                    drain(k, h)
+                for h in range(2):
+                    scatter(k, h)
+            else:
+                last = keep.tile([P, N], F32, name="last")
+                for h in range(2):
+                    cast("V", last[:, h * H:(h + 1) * H], acc[3, h][:])
+                nc.vector.tensor_copy(out=windows[3][:].indirect(offsets[:]), in_=last[:])
             store(k)

@@ -22,6 +22,7 @@ KP = P * PACK
 G = R // KP
 DT = D // P
 H = N // 2
+RUN = 8
 SEQ_BUFS = 36
 
 
@@ -46,6 +47,9 @@ def tile_attend_gat_lse_c_kernel(tc, qT, cT, doT, lse, delta, rw, qm, dom, offs,
         def relay_tile(name):
             return ring.tile([P, H * PACK], BF16, name=name, tag="relay", bufs=1, align_bytes=64)
 
+        def relay2_tile(name):
+            return ring.tile([P, H * PACK], BF16, name=name, tag="relay2", bufs=1, align_bytes=64)
+
         def big_tile(name, shape):
             return ring.tile(shape, F32, name=name, tag="big", bufs=PACK)
 
@@ -64,7 +68,7 @@ def tile_attend_gat_lse_c_kernel(tc, qT, cT, doT, lse, delta, rw, qm, dom, offs,
         rows = keep.tile([P, KP], F32, name="rows")
         nc.vector.memset(rows[:], 0.0)
         for i, src in enumerate((lse, rw, delta)):
-            nc.sync.dma_start(out=rows[G * i:G * (i + 1), :], in_=src[0].rearrange("(g w) o -> g (w o)", g=G))
+            nc.sync.dma_start(out=rows[i:P:P // G, :], in_=src[0].rearrange("(g w) o -> g (w o)", g=G))
         for j in range(1, PACK):
             nc.sync.dma_start(out=planes[j][:], in_=c_rows[j])
 
@@ -75,24 +79,38 @@ def tile_attend_gat_lse_c_kernel(tc, qT, cT, doT, lse, delta, rw, qm, dom, offs,
 
         alld = slice(0, D)
         raw = {}
-        raw["q", 0] = [load("q0", qT, alld, slice(0, KP))]
-        raw["q", 1] = [load("q1%d" % i, qT, alld, slice(KP + i * H, KP + (i + 1) * H)) for i in range(2)]
-        for g in range(G):
-            raw["do", g] = [load("do%d" % g, doT, alld, slice(g * KP, (g + 1) * KP))]
+        for name, src in (("q", qT), ("do", doT)):
+            for g in range(G):
+                raw[name, g] = load("%s%d" % (name, g), src, alld, slice(g * KP, (g + 1) * KP))
+
+        def load_runs(name, src, cols):
+            tile = keep.tile([P, PACK, cols.stop - cols.start], F32, name=name)
+            runs = src[0][KP:R, cols].rearrange("(b j q) w -> j b q w", j=PACK, q=RUN)
+            for j in range(PACK):
+                nc.sync.dma_start(out=tile[:, j, :], in_=runs[j])
+            return tile
+
         for h in range(2):
             for g in range(G):
                 for name, src in (("dom", dom), ("qm", qm)):
-                    half = load("%s%d%d" % (name, g, h), src, slice(g * KP, (g + 1) * KP), slice(h * H, (h + 1) * H))
+                    cols = slice(h * H, (h + 1) * H)
+                    label = "%s%d%d" % (name, g, h)
+                    half = load(label, src, slice(0, KP), cols) if g == 0 else load_runs(label, src, cols)
                     for i in range(2):
                         raw[name, g, 2 * h + i] = half[:, :, i * P:(i + 1) * P]
 
         identity = keep.tile([P, P], F32, name="identity")
         make_identity(nc, identity[:])
         turned = psum.tile([P, PACK, P], F32, name="turned")
+        dealt = keep.tile([P, KP], F32, name="dealt")
+        lower, upper = slice(0, P // G), slice(P // G, P)
+        cast("G", dealt[lower, :], rows[lower, :])
+        cast("G", dealt[upper, :].rearrange("p (b q t) -> p b q t", q=RUN, t=PACK),
+             rows[upper, :].rearrange("p (b t q) -> p b q t", q=RUN, t=PACK))
         for t in range(PACK):
-            nc.tensor.transpose(turned[:, t, :], rows[:, t::PACK], identity[:])
+            nc.tensor.transpose(turned[:, t, :], dealt[:, t::PACK], identity[:])
         columns = keep.tile([P, 3, G, PACK], F32, name="columns")
-        nc.scalar.copy(out=columns[:].rearrange("p v g t -> p (v g) t"), in_=turned[:, :, 0:3 * G].rearrange("p t r -> p r t"))
+        nc.scalar.copy(out=columns[:].rearrange("p v g t -> p g v t"), in_=turned[:].rearrange("p t (g v) -> p g v t", g=G)[:, :, 0:3])
         vecs = {name: columns[:, i].rearrange("p g t -> p (g t)") for i, name in enumerate(("lse", "rw", "delta"))}
 
         windows = [keep.tile([P, T], F32, name="window%d" % k) for k in range(DT)]
@@ -115,13 +133,17 @@ def tile_attend_gat_lse_c_kernel(tc, qT, cT, doT, lse, delta, rw, qm, dom, offs,
         bf = {}
         mx = {}
 
-        def cast_queries(engine, name, g, u, make, part=0):
-            if part == 0:
-                bf[name, g, u] = make("%s%d%d_bf" % (name, g, u))
-            width = P // len(raw[name, g])
-            src = raw[name, g][part][:].rearrange("p j (m u e) -> p u m j e", u=2, e=2)[:, u]
-            dst = bf[name, g, u][:].rearrange("p (e m j) -> p m j e", e=2, j=PACK)[:, part * width:(part + 1) * width]
-            cast(engine, dst, src)
+        def cast_queries(engine, name, g, u, make):
+            bf[name, g, u] = make("%s%d%d_bf" % (name, g, u))
+            if g == 0:
+                src = raw[name, g][:].rearrange("p j (m u e) -> p u m j e", u=2, e=2)[:, u]
+                cast(engine, bf[name, g, u][:].rearrange("p (e m j) -> p m j e", e=2, j=PACK), src)
+            else:
+                run = 1 if engine == "G" else 2
+                for e in range(2):
+                    src = raw[name, g][:].rearrange("p j (b t c i) -> p t b c j i", t=PACK, c=RUN // run, i=run)[:, 2 * u + e]
+                    dst = bf[name, g, u][:, e * KP:(e + 1) * KP].rearrange("p (b c i j) -> p b c j i", c=RUN // run, i=run, j=PACK)
+                    cast(engine, dst, src)
 
         def in_seq(name):
             return seq_tile(name, H * PACK, BF16)
@@ -156,7 +178,7 @@ def tile_attend_gat_lse_c_kernel(tc, qT, cT, doT, lse, delta, rw, qm, dom, offs,
             dst = bf[name, g, h][:].rearrange("p (c i t) -> p c t i", i=2, t=PACK)
             in0 = read["q", g][:, h].rearrange("p t (c i) -> p c t i", i=2)
             if name == "pw":
-                in1 = turned[:, :, G + g].unsqueeze(1).unsqueeze(3).broadcast_to([P, H // 2, PACK, 2])
+                in1 = turned[:, :, g * (P // G) + 1].unsqueeze(1).unsqueeze(3).broadcast_to([P, H // 2, PACK, 2])
             else:
                 in1 = read["do", g][:, h].rearrange("p t (c i) -> p c t i", i=2)
             nc.vector.tensor_tensor(out=dst, in0=in0, in1=in1, op=ALU.mult)
@@ -211,49 +233,48 @@ def tile_attend_gat_lse_c_kernel(tc, qT, cT, doT, lse, delta, rw, qm, dom, offs,
         for h in range(2):
             for t in range(PACK):
                 score("q", 0, t, h, h + 1)
-        for part in range(2):
-            cast_queries("V", "q", 1, 0, relay_tile, part)
-            cast_queries("V", "q", 1, 1, in_seq, part)
+        cast_queries("V", "q", 1, 0, relay_tile)
         quant("q", 1, 0)
-        quant("q", 1, 1)
-        for t in range(PACK):
+        cast_queries("G", "q", 1, 1, relay_tile)
+        for t in (0, 1):
             score("q", 1, t, 0, 2)
-        product("pw", 0, 0, relay_tile)
-        product("pw", 0, 1)
+        product("pw", 0, 0)
+        cast_queries("S", "do", 0, 1, in_seq)
+        product("pw", 0, 1, relay2_tile)
+        quant("q", 1, 1)
+        for t in (2, 3):
+            score("q", 1, t, 0, 2)
         cast_queries("V", "do", 0, 0, in_seq)
         quant("pw", 0, 0)
-        cast_queries("S", "do", 0, 1, relay_tile)
         quant("do", 0, 0)
-        for t in (0, 1):
-            score("do", 0, t, 0, 2)
-        cast_queries("V", "do", 1, 0, in_seq)
-        cast_queries("S", "do", 1, 1, in_seq)
-        quant("pw", 0, 1)
-        quant("do", 1, 0)
+        cast_queries("S", "do", 1, 0, in_seq)
         quant("do", 0, 1)
-        for t in (2, 3):
+        for t in range(PACK):
             score("do", 0, t, 0, 2)
-        cast_rows("G", "dom", 0, 0, 1, relay_tile)
+        quant("pw", 0, 1)
+        cast_queries("G", "do", 1, 1, relay2_tile)
         product("pw", 1, 0)
         product("pw", 1, 1)
+        quant("do", 1, 0)
         quant("do", 1, 1)
         for t in range(PACK):
             score("do", 1, t, 0, 2)
         quant("pw", 1, 0)
         quant("pw", 1, 1)
-        quant_rows("dom", 0, 0, 1)
         product("ds", 0, 0)
         product("ds", 0, 1)
-        cast_rows("S", "dom", 0, 1, 2)
-        cast_rows("S", "qm", 0)
+        cast_rows("S", "dom", 0)
+        cast_rows("S", "qm", 0, 0, 1)
         cast_rows("S", "dom", 1)
         quant("ds", 0, 0)
         product("ds", 1, 0)
-        quant_rows("dom", 0, 1, 2)
+        cast_rows("V", "qm", 0, 1, 2)
+        quant_rows("dom", 0)
         for h in range(2):
             out_passes("dom", 0, h)
         quant("ds", 1, 0)
-        quant_rows("qm", 0)
+        for g in (1, 0):
+            quant_rows("qm", 0, g, g + 1)
         out_passes("qm", 0, 0)
         drain(0, 0)
         scatter(0, 0)

@@ -23,6 +23,8 @@ G = R // KP
 DT = D // P
 H = N // 2
 RUN = 8
+BLOCKS = 16
+GPSIMD_BLOCKS = 8
 SEQ_BUFS = 36
 
 
@@ -133,23 +135,30 @@ def tile_attend_gat_lse_c_kernel(tc, qT, cT, doT, lse, delta, rw, qm, dom, offs,
         bf = {}
         mx = {}
 
-        def cast_queries(engine, name, g, u, make):
+        def cast_queries(engine, name, g, u, make, left=0):
             bf[name, g, u] = make("%s%d%d_bf" % (name, g, u))
             if g == 0:
                 src = raw[name, g][:].rearrange("p j (m u e) -> p u m j e", u=2, e=2)[:, u]
                 cast(engine, bf[name, g, u][:].rearrange("p (e m j) -> p m j e", e=2, j=PACK), src)
             else:
-                run = 1 if engine == "G" else 2
                 for e in range(2):
-                    src = raw[name, g][:].rearrange("p j (b t c i) -> p t b c j i", t=PACK, c=RUN // run, i=run)[:, 2 * u + e]
-                    dst = bf[name, g, u][:, e * KP:(e + 1) * KP].rearrange("p (b c i j) -> p b c j i", c=RUN // run, i=run, j=PACK)
-                    cast(engine, dst, src)
+                    cast_bank(engine, name, 2 * u + e, 0, BLOCKS - (left if e == 1 else 0))
+
+        def cast_bank(engine, name, t, lo, hi):
+            run = 1 if engine == "G" else 2
+            src = raw[name, 1][:].rearrange("p j (b t c i) -> p t b c j i", t=PACK, c=RUN // run, i=run)[:, t, lo:hi]
+            dst = bf[name, 1, t // 2][:, (t % 2) * KP:(t % 2 + 1) * KP].rearrange("p (b c i j) -> p b c j i", c=RUN // run, i=run, j=PACK)
+            cast(engine, dst[:, lo:hi], src)
 
         def in_seq(name):
             return seq_tile(name, H * PACK, BF16)
 
         def quant(name, g, h):
             mx[name, g, h] = quantize("%s%d%d" % (name, g, h), fmt[name], bf[name, g, h][:])
+
+        def quant_bank(name, g, t):
+            cols = slice((t % 2) * KP, (t % 2 + 1) * KP)
+            mx[name, g, "bank", t] = quantize("%s%d_bank%d" % (name, g, t), fmt[name], bf[name, g, t // 2][:, cols])
 
         def bank_tile(width):
             return psum.tile([P, width], F32, name="bank", tag="bank", bufs=7)
@@ -160,8 +169,12 @@ def tile_attend_gat_lse_c_kernel(tc, qT, cT, doT, lse, delta, rw, qm, dom, offs,
             if (name, g) not in read:
                 read[name, g] = big_tile("%s%d_read" % (name, g), [P, 2, PACK, H])
             bank = bank_tile((hi - lo) * H)
-            codes, scales = mx[name, g, t // 2]
-            cols = slice((t % 2) * P, (t % 2 + 1) * P)
+            if (name, g, "bank", t) in mx:
+                codes, scales = mx[name, g, "bank", t]
+                cols = slice(0, P)
+            else:
+                codes, scales = mx[name, g, t // 2]
+                cols = slice((t % 2) * P, (t % 2 + 1) * P)
             slots = slice(lo * H, hi * H)
             nc.tensor.matmul_mx(out=bank[:], lhsT=codes[:, cols].bitcast(fmt[name]), lhsT_scale=scales[:, cols],
                                 rhs=c_mx[0][:, slots].bitcast(E4), rhs_scale=c_mx[1][:, slots], start=True, stop=True)
@@ -228,13 +241,15 @@ def tile_attend_gat_lse_c_kernel(tc, qT, cT, doT, lse, delta, rw, qm, dom, offs,
 
         cast_queries("V", "q", 0, 0, in_seq)
         cast_queries("S", "q", 0, 1, relay_tile)
-        quant("q", 0, 0)
+        for t in (0, 1):
+            quant_bank("q", 0, t)
         quant("q", 0, 1)
         for h in range(2):
             for t in range(PACK):
                 score("q", 0, t, h, h + 1)
         cast_queries("V", "q", 1, 0, relay_tile)
-        quant("q", 1, 0)
+        for t in (0, 1):
+            quant_bank("q", 1, t)
         cast_queries("G", "q", 1, 1, relay_tile)
         for t in (0, 1):
             score("q", 1, t, 0, 2)
@@ -247,12 +262,13 @@ def tile_attend_gat_lse_c_kernel(tc, qT, cT, doT, lse, delta, rw, qm, dom, offs,
         cast_queries("V", "do", 0, 0, in_seq)
         quant("pw", 0, 0)
         quant("do", 0, 0)
-        cast_queries("S", "do", 1, 0, in_seq)
+        cast_queries("S", "do", 1, 0, in_seq, GPSIMD_BLOCKS)
         quant("do", 0, 1)
         for t in range(PACK):
             score("do", 0, t, 0, 2)
         quant("pw", 0, 1)
         cast_queries("G", "do", 1, 1, relay2_tile)
+        cast_bank("G", "do", 1, BLOCKS - GPSIMD_BLOCKS, BLOCKS)
         product("pw", 1, 0)
         product("pw", 1, 1)
         quant("do", 1, 0)

@@ -22,10 +22,7 @@ KP = P * PACK
 G = R // KP
 DT = D // P
 H = N // 2
-RUN = 8
-BLOCKS = 16
-GPSIMD_BLOCKS = 8
-SEQ_BUFS = 36
+SEQ_BUFS = 49
 
 
 def tile_attend_gat_lse_c_kernel(tc, qT, cT, doT, lse, delta, rw, qm, dom, offs, out):
@@ -49,11 +46,19 @@ def tile_attend_gat_lse_c_kernel(tc, qT, cT, doT, lse, delta, rw, qm, dom, offs,
         def relay_tile(name):
             return ring.tile([P, H * PACK], BF16, name=name, tag="relay", bufs=1, align_bytes=64)
 
-        def relay2_tile(name):
-            return ring.tile([P, H * PACK], BF16, name=name, tag="relay2", bufs=1, align_bytes=64)
+        def wide_tile(name):
+            return ring.tile([P, H * PACK], BF16, name=name, tag="wide", bufs=1, align_bytes=64)
+
+        def wide_relay(name, key):
+            tile = ring.tile([P, N * PACK], BF16, name=name, tag="wide", bufs=1, align_bytes=64)
+            for u in range(2):
+                bf[key + (u,)] = tile[:, u * H * PACK:(u + 1) * H * PACK]
 
         def big_tile(name, shape):
             return ring.tile(shape, F32, name=name, tag="big", bufs=PACK)
+
+        def raw_tile(name, shape):
+            return ring.tile(shape, F32, name=name, tag="raw", bufs=6)
 
         def quantize(name, fmt, src):
             width = src.shape[1] // PACK
@@ -74,43 +79,31 @@ def tile_attend_gat_lse_c_kernel(tc, qT, cT, doT, lse, delta, rw, qm, dom, offs,
         for j in range(1, PACK):
             nc.sync.dma_start(out=planes[j][:], in_=c_rows[j])
 
-        def load(name, src, rows, cols):
-            raw = keep.tile([P, PACK, cols.stop - cols.start], F32, name=name)
-            nc.sync.dma_start(out=raw[:], in_=src[0][rows, cols].rearrange("(p j) w -> p j w", j=PACK))
-            return raw
+        def load(tile, src, rows, cols):
+            nc.sync.dma_start(out=tile, in_=src[0][rows, cols].rearrange("(p j) w -> p j w", j=PACK))
+            return tile
 
-        alld = slice(0, D)
         raw = {}
         for name, src in (("q", qT), ("do", doT)):
             for g in range(G):
-                raw[name, g] = load("%s%d" % (name, g), src, alld, slice(g * KP, (g + 1) * KP))
-
-        def load_runs(name, src, cols):
-            tile = keep.tile([P, PACK, cols.stop - cols.start], F32, name=name)
-            runs = src[0][KP:R, cols].rearrange("(b j q) w -> j b q w", j=PACK, q=RUN)
-            for j in range(PACK):
-                nc.sync.dma_start(out=tile[:, j, :], in_=runs[j])
-            return tile
-
+                raw[name, g] = load(raw_tile("%s%d" % (name, g), [P, PACK, KP])[:], src, slice(0, D), slice(g * KP, (g + 1) * KP))
+        pair = (("dom", dom), ("qm", qm))
+        for name, src in pair:
+            whole = load(raw_tile(name + "0", [P, PACK, D])[:], src, slice(0, KP), slice(0, D))
+            for k in range(DT):
+                raw[name, 0, k] = whole[:, :, k * P:(k + 1) * P]
         for h in range(2):
-            for g in range(G):
-                for name, src in (("dom", dom), ("qm", qm)):
-                    cols = slice(h * H, (h + 1) * H)
-                    label = "%s%d%d" % (name, g, h)
-                    half = load(label, src, slice(0, KP), cols) if g == 0 else load_runs(label, src, cols)
-                    for i in range(2):
-                        raw[name, g, 2 * h + i] = half[:, :, i * P:(i + 1) * P]
+            both = raw_tile("second%d" % h, [P, 2, PACK, H])
+            for n, (name, src) in enumerate(pair):
+                half = load(both[:, n], src, slice(KP, R), slice(h * H, (h + 1) * H))
+                for i in range(2):
+                    raw[name, 1, 2 * h + i] = half[:, :, i * P:(i + 1) * P]
 
         identity = keep.tile([P, P], F32, name="identity")
         make_identity(nc, identity[:])
         turned = psum.tile([P, PACK, P], F32, name="turned")
-        dealt = keep.tile([P, KP], F32, name="dealt")
-        lower, upper = slice(0, P // G), slice(P // G, P)
-        cast("G", dealt[lower, :], rows[lower, :])
-        cast("G", dealt[upper, :].rearrange("p (b q t) -> p b q t", q=RUN, t=PACK),
-             rows[upper, :].rearrange("p (b t q) -> p b q t", q=RUN, t=PACK))
         for t in range(PACK):
-            nc.tensor.transpose(turned[:, t, :], dealt[:, t::PACK], identity[:])
+            nc.tensor.transpose(turned[:, t, :], rows[:, t::PACK], identity[:])
         columns = keep.tile([P, 3, G, PACK], F32, name="columns")
         nc.scalar.copy(out=columns[:].rearrange("p v g t -> p g v t"), in_=turned[:].rearrange("p t (g v) -> p g v t", g=G)[:, :, 0:3])
         vecs = {name: columns[:, i].rearrange("p g t -> p (g t)") for i, name in enumerate(("lse", "rw", "delta"))}
@@ -135,26 +128,19 @@ def tile_attend_gat_lse_c_kernel(tc, qT, cT, doT, lse, delta, rw, qm, dom, offs,
         bf = {}
         mx = {}
 
-        def cast_queries(engine, name, g, u, make, left=0):
-            bf[name, g, u] = make("%s%d%d_bf" % (name, g, u))
-            if g == 0:
-                src = raw[name, g][:].rearrange("p j (m u e) -> p u m j e", u=2, e=2)[:, u]
-                cast(engine, bf[name, g, u][:].rearrange("p (e m j) -> p m j e", e=2, j=PACK), src)
-            else:
-                for e in range(2):
-                    cast_bank(engine, name, 2 * u + e, 0, BLOCKS - (left if e == 1 else 0))
-
-        def cast_bank(engine, name, t, lo, hi):
-            run = 1 if engine == "G" else 2
-            src = raw[name, 1][:].rearrange("p j (b t c i) -> p t b c j i", t=PACK, c=RUN // run, i=run)[:, t, lo:hi]
-            dst = bf[name, 1, t // 2][:, (t % 2) * KP:(t % 2 + 1) * KP].rearrange("p (b c i j) -> p b c j i", c=RUN // run, i=run, j=PACK)
-            cast(engine, dst[:, lo:hi], src)
-
         def in_seq(name):
             return seq_tile(name, H * PACK, BF16)
 
+        def pair_tile(name, g, u, make=in_seq):
+            bf[name, g, u] = make("%s%d%d_bf" % (name, g, u))[:]
+
+        def cast_pair(engine, name, g, u, lo=0, hi=P):
+            order = "m e j" if engine == "G" else "m j e"
+            src = raw[name, g].rearrange("p j (m u e) -> p u " + order, u=2, e=2)[:, u, lo:hi]
+            cast(engine, bf[name, g, u].rearrange("p (e m j) -> p " + order, e=2, j=PACK)[:, lo:hi], src)
+
         def quant(name, g, h):
-            mx[name, g, h] = quantize("%s%d%d" % (name, g, h), fmt[name], bf[name, g, h][:])
+            mx[name, g, h] = quantize("%s%d%d" % (name, g, h), fmt[name], bf[name, g, h])
 
         def quant_bank(name, g, t):
             cols = slice((t % 2) * KP, (t % 2 + 1) * KP)
@@ -186,9 +172,17 @@ def tile_attend_gat_lse_c_kernel(tc, qT, cT, doT, lse, delta, rw, qm, dom, offs,
             else:
                 nc.scalar.activation(out=dst, in_=src, func=ACT.Identity, bias=neg_rwd[:, u:u + 1], scale=vecs["rw"][:, u:u + 1])
 
+        def scores(name, g, whole):
+            for t in range(whole):
+                score(name, g, t, 0, 2)
+            for h in range(2):
+                for t in range(whole, PACK):
+                    score(name, g, t, h, h + 1)
+
         def product(name, g, h, make=in_seq):
-            bf[name, g, h] = make("%s%d%d_bf" % (name, g, h))
-            dst = bf[name, g, h][:].rearrange("p (c i t) -> p c t i", i=2, t=PACK)
+            if (name, g, h) not in bf:
+                bf[name, g, h] = make("%s%d%d_bf" % (name, g, h))[:]
+            dst = bf[name, g, h].rearrange("p (c i t) -> p c t i", i=2, t=PACK)
             in0 = read["q", g][:, h].rearrange("p t (c i) -> p c t i", i=2)
             if name == "pw":
                 in1 = turned[:, :, g * (P // G) + 1].unsqueeze(1).unsqueeze(3).broadcast_to([P, H // 2, PACK, 2])
@@ -196,19 +190,20 @@ def tile_attend_gat_lse_c_kernel(tc, qT, cT, doT, lse, delta, rw, qm, dom, offs,
                 in1 = read["do", g][:, h].rearrange("p t (c i) -> p c t i", i=2)
             nc.vector.tensor_tensor(out=dst, in0=in0, in1=in1, op=ALU.mult)
 
-        def cast_rows(engine, name, k, lo=0, hi=G, make=in_seq):
-            bf[name, k, lo] = make("%s_bf%d%d" % (name, k, lo))
-            run = 1 if engine == "G" else 2
+        def cast_rows(engine, name, k, lo, hi):
+            tile = seq_tile("%s_bf%d%d" % (name, k, lo), (hi - lo) * KP, BF16)
+            bf[name, "rows", k, lo] = tile[:]
             for g in range(lo, hi):
-                src = raw[name, g, k].rearrange("p j (c i) -> p c j i", i=run)
-                dst = bf[name, k, lo][:, (g - lo) * KP:(g - lo + 1) * KP].rearrange("p (c i j) -> p c j i", i=run, j=PACK)
+                src = raw[name, g, k].rearrange("p j (c i) -> p c j i", i=2)
+                dst = tile[:, (g - lo) * KP:(g - lo + 1) * KP].rearrange("p (c i j) -> p c j i", i=2, j=PACK)
                 cast(engine, dst, src)
 
-        def quant_rows(name, k, lo=0, hi=G):
-            codes, scales = quantize("%s%d%d" % (name, k, lo), fmt[name], bf[name, k, lo][:, 0:(hi - lo) * KP])
+        def quant_rows(name, k, first, lo, hi):
+            src = bf[name, "rows", k, first][:, (lo - first) * KP:(hi - first) * KP]
+            codes, scales = quantize("%s%d%d" % (name, k, lo), fmt[name], src)
             for g in range(lo, hi):
                 cols = slice((g - lo) * P, (g - lo + 1) * P)
-                mx[name, k, g] = codes[:, cols], scales[:, cols]
+                mx[name, "rows", k, g] = codes[:, cols], scales[:, cols]
 
         acc = {}
         partner = {"dom": "pw", "qm": "ds"}
@@ -218,7 +213,7 @@ def tile_attend_gat_lse_c_kernel(tc, qT, cT, doT, lse, delta, rw, qm, dom, offs,
                 acc[k, h] = bank_tile(H)
             right = partner[name]
             for g in range(lo, hi):
-                nc.tensor.matmul_mx(out=acc[k, h][:], lhsT=mx[name, k, g][0].bitcast(fmt[name]), lhsT_scale=mx[name, k, g][1],
+                nc.tensor.matmul_mx(out=acc[k, h][:], lhsT=mx[name, "rows", k, g][0].bitcast(fmt[name]), lhsT_scale=mx[name, "rows", k, g][1],
                                     rhs=mx[right, g, h][0][:].bitcast(fmt[right]), rhs_scale=mx[right, g, h][1][:],
                                     start=(name == "dom" and g == 0), stop=(name == "qm" and g == G - 1))
 
@@ -228,10 +223,6 @@ def tile_attend_gat_lse_c_kernel(tc, qT, cT, doT, lse, delta, rw, qm, dom, offs,
             stage[k, h] = ring.tile([P, H], F32, name="stage", tag="stage", bufs=4)
             cast("S", stage[k, h][:], acc[k, h][:])
 
-        def out_pass(name, k, g):
-            for h in range(2):
-                out_passes(name, k, h, g, g + 1)
-
         def scatter(k, h):
             cols = slice(h * H // 16, (h + 1) * H // 16)
             nc.scalar.activation(out=windows[k][:].indirect(offsets[:, cols]), in_=stage[k, h][:], func=ACT.Copy)
@@ -239,91 +230,116 @@ def tile_attend_gat_lse_c_kernel(tc, qT, cT, doT, lse, delta, rw, qm, dom, offs,
         def store(k):
             nc.sync.dma_start(out=out[k * P:(k + 1) * P, :], in_=windows[k][:])
 
-        cast_queries("V", "q", 0, 0, in_seq)
-        cast_queries("S", "q", 0, 1, relay_tile)
-        for t in (0, 1):
+        def finish(k):
+            for h in range(2):
+                drain(k, h)
+            for h in range(2):
+                scatter(k, h)
+            store(k)
+
+        pair_tile("q", 0, 0)
+        cast_pair("V", "q", 0, 0)
+        pair_tile("q", 0, 1, relay_tile)
+        cast_pair("S", "q", 0, 1, 0, 88)
+        cast_pair("V", "q", 0, 1, 88, P)
+        for t in range(PACK):
             quant_bank("q", 0, t)
-        quant("q", 0, 1)
-        for h in range(2):
-            for t in range(PACK):
-                score("q", 0, t, h, h + 1)
-        cast_queries("V", "q", 1, 0, relay_tile)
+        scores("q", 0, 0)
+        pair_tile("q", 1, 0, relay_tile)
+        cast_pair("V", "q", 1, 0)
         for t in (0, 1):
             quant_bank("q", 1, t)
-        cast_queries("G", "q", 1, 1, relay_tile)
+        pair_tile("q", 1, 1, relay_tile)
+        for lo in (0, 64):
+            cast_pair("G", "q", 1, 1, lo, lo + 64)
+        product("pw", 0, 0)
         for t in (0, 1):
             score("q", 1, t, 0, 2)
-        product("pw", 0, 0)
-        cast_queries("S", "do", 0, 1, in_seq)
-        product("pw", 0, 1, relay2_tile)
+        product("pw", 0, 1, wide_tile)
+        pair_tile("do", 0, 1)
+        cast_pair("S", "do", 0, 1)
         quant("q", 1, 1)
-        for t in (2, 3):
-            score("q", 1, t, 0, 2)
-        cast_queries("V", "do", 0, 0, in_seq)
+        for h in range(2):
+            for t in (2, 3):
+                score("q", 1, t, h, h + 1)
+        pair_tile("do", 0, 0)
+        cast_pair("V", "do", 0, 0)
         quant("pw", 0, 0)
         quant("do", 0, 0)
-        cast_queries("S", "do", 1, 0, in_seq, GPSIMD_BLOCKS)
-        quant("do", 0, 1)
-        for t in range(PACK):
-            score("do", 0, t, 0, 2)
         quant("pw", 0, 1)
-        cast_queries("G", "do", 1, 1, relay2_tile)
-        cast_bank("G", "do", 1, BLOCKS - GPSIMD_BLOCKS, BLOCKS)
+        quant("do", 0, 1)
+        wide_relay("do1_bf", ("do", 1))
+        for lo in (0, 64):
+            cast_pair("G", "do", 1, 0, lo, lo + 64)
+        cast_pair("G", "do", 1, 1, 0, 48)
+        cast_pair("S", "do", 1, 1, 48, P)
         product("pw", 1, 0)
+        scores("do", 0, 4)
         product("pw", 1, 1)
         quant("do", 1, 0)
-        quant("do", 1, 1)
-        for t in range(PACK):
-            score("do", 1, t, 0, 2)
         quant("pw", 1, 0)
+        quant("do", 1, 1)
         quant("pw", 1, 1)
+        cast_rows("S", "dom", 0, 0, 1)
+        scores("do", 1, 2)
         product("ds", 0, 0)
         product("ds", 0, 1)
-        cast_rows("S", "dom", 0)
-        cast_rows("S", "qm", 0, 0, 1)
-        cast_rows("S", "dom", 1)
         quant("ds", 0, 0)
         product("ds", 1, 0)
+        cast_rows("S", "dom", 0, 1, 2)
         cast_rows("V", "qm", 0, 1, 2)
-        quant_rows("dom", 0)
+        quant_rows("dom", 0, 0, 0, 1)
+        quant("ds", 0, 1)
+        cast_rows("S", "qm", 0, 0, 1)
+        quant("ds", 1, 0)
+        quant_rows("dom", 0, 1, 1, 2)
         for h in range(2):
             out_passes("dom", 0, h)
-        quant("ds", 1, 0)
-        for g in (1, 0):
-            quant_rows("qm", 0, g, g + 1)
+        quant_rows("qm", 0, 1, 1, 2)
+        quant_rows("qm", 0, 0, 0, 1)
         out_passes("qm", 0, 0)
-        drain(0, 0)
-        scatter(0, 0)
+        out_passes("qm", 0, 1, 0, 1)
+        cast_rows("S", "dom", 1, 0, 1)
         product("ds", 1, 1)
         cast_rows("S", "qm", 1, 0, 1)
-        quant("ds", 0, 1)
+        cast_rows("S", "dom", 2, 0, 1)
+        drain(0, 0)
+        scatter(0, 0)
+        cast_rows("V", "dom", 1, 1, 2)
         quant("ds", 1, 1)
-        out_passes("qm", 0, 1)
+        out_passes("qm", 0, 1, 1, 2)
         drain(0, 1)
         scatter(0, 1)
         store(0)
-        for k in range(1, DT):
-            if k > 1:
-                cast_rows("V", "dom", k)
-                cast_rows("V", "qm", k, 0, 1)
-            else:
-                cast_rows("V", "qm", k, 1, 2)
-            quant_rows("dom", k)
-            for h in range(2):
-                out_passes("dom", k, h)
-            if k > 1:
-                cast_rows("V", "qm", k, 1, 2)
+        cast_rows("V", "qm", 1, 1, 2)
+        for name in ("dom", "qm"):
             for g in range(G):
-                quant_rows("qm", k, g, g + 1)
-                out_pass("qm", k, g)
-            if k < DT - 1:
-                for h in range(2):
-                    drain(k, h)
-                for h in range(2):
-                    scatter(k, h)
-            else:
-                last = keep.tile([P, N], F32, name="last")
-                for h in range(2):
-                    cast("V", last[:, h * H:(h + 1) * H], acc[3, h][:])
-                nc.vector.tensor_copy(out=windows[3][:].indirect(offsets[:]), in_=last[:])
-            store(k)
+                quant_rows(name, 1, g, g, g + 1)
+            for h in range(2):
+                out_passes(name, 1, h)
+        finish(1)
+        cast_rows("V", "dom", 2, 1, 2)
+        cast_rows("V", "qm", 2, 0, 2)
+        for g in range(G):
+            quant_rows("dom", 2, g, g, g + 1)
+        for h in range(2):
+            out_passes("dom", 2, h)
+        quant_rows("qm", 2, 0, 0, 2)
+        for h in range(2):
+            out_passes("qm", 2, h)
+        finish(2)
+        cast_rows("V", "dom", 3, 0, 2)
+        cast_rows("V", "qm", 3, 0, 1)
+        quant_rows("dom", 3, 0, 0, 2)
+        for h in range(2):
+            out_passes("dom", 3, h)
+        cast_rows("V", "qm", 3, 1, 2)
+        for g in range(G):
+            quant_rows("qm", 3, g, g, g + 1)
+            for h in range(2):
+                out_passes("qm", 3, h, g, g + 1)
+        last = keep.tile([P, N], F32, name="last")
+        for h in range(2):
+            cast("V", last[:, h * H:(h + 1) * H], acc[3, h][:])
+        nc.vector.tensor_copy(out=windows[3][:].indirect(offsets[:]), in_=last[:])
+        store(3)

@@ -22,7 +22,7 @@ KP = P * PACK
 G = R // KP
 DT = D // P
 H = N // 2
-SEQ_BUFS = 49
+SEQ_BUFS = 50
 
 
 def tile_attend_gat_lse_c_kernel(tc, qT, cT, doT, lse, delta, rw, qm, dom, offs, out):
@@ -45,14 +45,6 @@ def tile_attend_gat_lse_c_kernel(tc, qT, cT, doT, lse, delta, rw, qm, dom, offs,
 
         def relay_tile(name):
             return ring.tile([P, H * PACK], BF16, name=name, tag="relay", bufs=1, align_bytes=64)
-
-        def wide_tile(name):
-            return ring.tile([P, H * PACK], BF16, name=name, tag="wide", bufs=1, align_bytes=64)
-
-        def wide_relay(name, key):
-            tile = ring.tile([P, N * PACK], BF16, name=name, tag="wide", bufs=1, align_bytes=64)
-            for u in range(2):
-                bf[key + (u,)] = tile[:, u * H * PACK:(u + 1) * H * PACK]
 
         def big_tile(name, shape):
             return ring.tile(shape, F32, name=name, tag="big", bufs=PACK)
@@ -240,8 +232,8 @@ def tile_attend_gat_lse_c_kernel(tc, qT, cT, doT, lse, delta, rw, qm, dom, offs,
         pair_tile("q", 0, 0)
         cast_pair("V", "q", 0, 0)
         pair_tile("q", 0, 1, relay_tile)
-        cast_pair("S", "q", 0, 1, 0, 88)
-        cast_pair("V", "q", 0, 1, 88, P)
+        cast_pair("S", "q", 0, 1, 0, 72)
+        cast_pair("V", "q", 0, 1, 72, P)
         for t in range(PACK):
             quant_bank("q", 0, t)
         scores("q", 0, 0)
@@ -250,32 +242,34 @@ def tile_attend_gat_lse_c_kernel(tc, qT, cT, doT, lse, delta, rw, qm, dom, offs,
         for t in (0, 1):
             quant_bank("q", 1, t)
         pair_tile("q", 1, 1, relay_tile)
-        for lo in (0, 64):
-            cast_pair("G", "q", 1, 1, lo, lo + 64)
+        cast_pair("G", "q", 1, 1)
         product("pw", 0, 0)
         for t in (0, 1):
             score("q", 1, t, 0, 2)
-        product("pw", 0, 1, wide_tile)
+        product("pw", 0, 1)
         pair_tile("do", 0, 1)
-        cast_pair("S", "do", 0, 1)
+        cast_pair("G", "do", 0, 1, 88, P)
+        cast_pair("S", "do", 0, 1, 0, 88)
         quant("q", 1, 1)
         for h in range(2):
             for t in (2, 3):
                 score("q", 1, t, h, h + 1)
-        pair_tile("do", 0, 0)
-        cast_pair("V", "do", 0, 0)
         quant("pw", 0, 0)
+        pair_tile("do", 0, 0, relay_tile)
+        cast_pair("V", "do", 0, 0)
+        quant("do", 0, 1)
         quant("do", 0, 0)
         quant("pw", 0, 1)
-        quant("do", 0, 1)
-        wide_relay("do1_bf", ("do", 1))
-        for lo in (0, 64):
-            cast_pair("G", "do", 1, 0, lo, lo + 64)
-        cast_pair("G", "do", 1, 1, 0, 48)
-        cast_pair("S", "do", 1, 1, 48, P)
+        pair_tile("do", 1, 0, relay_tile)
+        cast_pair("G", "do", 1, 0)
         product("pw", 1, 0)
-        scores("do", 0, 4)
         product("pw", 1, 1)
+        pair_tile("do", 1, 1)
+        cast_pair("G", "do", 1, 1, 0, 40)
+        cast_pair("S", "do", 1, 1, 40, 64)
+        for t in (2, 3, 0, 1):
+            score("do", 0, t, 0, 2)
+        cast_pair("V", "do", 1, 1, 64, P)
         quant("do", 1, 0)
         quant("pw", 1, 0)
         quant("do", 1, 1)

@@ -22,6 +22,7 @@ KP = P * PACK
 G = R // KP
 DT = D // P
 H = N // 2
+HALF_BYTES = PACK * H * 4
 SEQ_BUFS = 50
 
 
@@ -30,6 +31,7 @@ def tile_attend_gat_lse_c_kernel(tc, qT, cT, doT, lse, delta, rw, qm, dom, offs,
     with ExitStack() as ctx:
         keep = ctx.enter_context(tc.tile_pool(name="keep", bufs=1))
         ring = ctx.enter_context(tc.tile_pool(name="ring", bufs=1))
+        inputs = ctx.enter_context(tc.tile_pool(name="inputs", bufs=1))
         psum = ctx.enter_context(tc.psum_pool(name="psum", bufs=1))
 
         def cast(engine, dst, src):
@@ -46,11 +48,14 @@ def tile_attend_gat_lse_c_kernel(tc, qT, cT, doT, lse, delta, rw, qm, dom, offs,
         def relay_tile(name):
             return ring.tile([P, H * PACK], BF16, name=name, tag="relay", bufs=1, align_bytes=64)
 
+        def second_tile(name):
+            return ring.tile([P, H * PACK], BF16, name=name, tag="second", bufs=1, align_bytes=64)
+
         def big_tile(name, shape):
             return ring.tile(shape, F32, name=name, tag="big", bufs=PACK)
 
-        def raw_tile(name, shape):
-            return ring.tile(shape, F32, name=name, tag="raw", bufs=6)
+        def raw_tile(name, width, place):
+            return inputs.tile([P, PACK, width], F32, name=name, offset=int(place * HALF_BYTES))
 
         def quantize(name, fmt, src):
             width = src.shape[1] // PACK
@@ -76,20 +81,26 @@ def tile_attend_gat_lse_c_kernel(tc, qT, cT, doT, lse, delta, rw, qm, dom, offs,
             return tile
 
         raw = {}
-        for name, src in (("q", qT), ("do", doT)):
+        for n, (name, src) in enumerate((("q", qT), ("do", doT))):
             for g in range(G):
-                raw[name, g] = load(raw_tile("%s%d" % (name, g), [P, PACK, KP])[:], src, slice(0, D), slice(g * KP, (g + 1) * KP))
-        pair = (("dom", dom), ("qm", qm))
-        for name, src in pair:
-            whole = load(raw_tile(name + "0", [P, PACK, D])[:], src, slice(0, KP), slice(0, D))
-            for k in range(DT):
-                raw[name, 0, k] = whole[:, :, k * P:(k + 1) * P]
-        for h in range(2):
-            both = raw_tile("second%d" % h, [P, 2, PACK, H])
-            for n, (name, src) in enumerate(pair):
-                half = load(both[:, n], src, slice(KP, R), slice(h * H, (h + 1) * H))
-                for i in range(2):
-                    raw[name, 1, 2 * h + i] = half[:, :, i * P:(i + 1) * P]
+                raw[name, g] = load(raw_tile("%s%d" % (name, g), KP, 2 * (G * n + g))[:], src, slice(0, D), slice(g * KP, (g + 1) * KP))
+        source = {"dom": dom, "qm": qm}
+
+        def load_tiles(name, g, lo, hi, place):
+            tile = raw_tile("%s%d%d" % (name, g, lo), (hi - lo) * P, place)
+            load(tile[:], source[name], slice(g * KP, (g + 1) * KP), slice(lo * P, hi * P))
+            for k in range(lo, hi):
+                raw[name, g, k] = tile[:, :, (k - lo) * P:(k - lo + 1) * P]
+
+        for g in range(G):
+            for n, name in enumerate(source):
+                load_tiles(name, g, 0, 2, 8 + 2 * g + n)
+        load_tiles("dom", 0, 2, 4, 0)
+
+        def placed(place, width):
+            def make(name):
+                return inputs.tile([P, width], BF16, name=name, offset=int(place * HALF_BYTES), align_bytes=64)
+            return make
 
         identity = keep.tile([P, P], F32, name="identity")
         make_identity(nc, identity[:])
@@ -182,8 +193,9 @@ def tile_attend_gat_lse_c_kernel(tc, qT, cT, doT, lse, delta, rw, qm, dom, offs,
                 in1 = read["do", g][:, h].rearrange("p t (c i) -> p c t i", i=2)
             nc.vector.tensor_tensor(out=dst, in0=in0, in1=in1, op=ALU.mult)
 
-        def cast_rows(engine, name, k, lo, hi):
-            tile = seq_tile("%s_bf%d%d" % (name, k, lo), (hi - lo) * KP, BF16)
+        def cast_rows(engine, name, k, lo, hi, make=None):
+            label = "%s_bf%d%d" % (name, k, lo)
+            tile = make(label) if make else seq_tile(label, (hi - lo) * KP, BF16)
             bf[name, "rows", k, lo] = tile[:]
             for g in range(lo, hi):
                 src = raw[name, g, k].rearrange("p j (c i) -> p c j i", i=2)
@@ -232,8 +244,8 @@ def tile_attend_gat_lse_c_kernel(tc, qT, cT, doT, lse, delta, rw, qm, dom, offs,
         pair_tile("q", 0, 0)
         cast_pair("V", "q", 0, 0)
         pair_tile("q", 0, 1, relay_tile)
-        cast_pair("S", "q", 0, 1, 0, 72)
-        cast_pair("V", "q", 0, 1, 72, P)
+        cast_pair("S", "q", 0, 1, 0, 80)
+        cast_pair("V", "q", 0, 1, 80, P)
         for t in range(PACK):
             quant_bank("q", 0, t)
         scores("q", 0, 0)
@@ -246,44 +258,43 @@ def tile_attend_gat_lse_c_kernel(tc, qT, cT, doT, lse, delta, rw, qm, dom, offs,
         product("pw", 0, 0)
         for t in (0, 1):
             score("q", 1, t, 0, 2)
-        product("pw", 0, 1)
-        pair_tile("do", 0, 1)
-        cast_pair("G", "do", 0, 1, 88, P)
-        cast_pair("S", "do", 0, 1, 0, 88)
+        product("pw", 0, 1, second_tile)
         quant("q", 1, 1)
-        for h in range(2):
-            for t in (2, 3):
-                score("q", 1, t, h, h + 1)
+        pair_tile("do", 0, 1)
+        cast_pair("S", "do", 0, 1, 0, 128)
+        for t in (2, 3):
+            score("q", 1, t, 0, 2)
         quant("pw", 0, 0)
-        pair_tile("do", 0, 0, relay_tile)
+        pair_tile("do", 0, 0)
         cast_pair("V", "do", 0, 0)
-        quant("do", 0, 1)
         quant("do", 0, 0)
+        quant("do", 0, 1)
+        pair_tile("do", 1, 1)
+        cast_pair("V", "do", 1, 1, 64, P)
+        cast_pair("S", "do", 1, 1, 0, 64)
         quant("pw", 0, 1)
-        pair_tile("do", 1, 0, relay_tile)
+        pair_tile("do", 1, 0, second_tile)
         cast_pair("G", "do", 1, 0)
         product("pw", 1, 0)
-        product("pw", 1, 1)
-        pair_tile("do", 1, 1)
-        cast_pair("G", "do", 1, 1, 0, 40)
-        cast_pair("S", "do", 1, 1, 40, 64)
-        for t in (2, 3, 0, 1):
+        for t in range(PACK):
             score("do", 0, t, 0, 2)
-        cast_pair("V", "do", 1, 1, 64, P)
+        product("pw", 1, 1)
         quant("do", 1, 0)
         quant("pw", 1, 0)
         quant("do", 1, 1)
         quant("pw", 1, 1)
-        cast_rows("S", "dom", 0, 0, 1)
-        scores("do", 1, 2)
-        product("ds", 0, 0)
-        product("ds", 0, 1)
+        cast_rows("S", "dom", 0, 0, 1, placed(6.375, KP))
+        scores("do", 1, 4)
+        product("ds", 0, 0, placed(1, H * PACK))
+        product("ds", 0, 1, placed(4.25, H * PACK))
         quant("ds", 0, 0)
+        load_tiles("qm", 0, 2, 4, 1)
         product("ds", 1, 0)
         cast_rows("S", "dom", 0, 1, 2)
         cast_rows("V", "qm", 0, 1, 2)
         quant_rows("dom", 0, 0, 0, 1)
-        quant("ds", 0, 1)
+        load_tiles("dom", 1, 2, 3, 6)
+        load_tiles("qm", 1, 2, 3, 6.5)
         cast_rows("S", "qm", 0, 0, 1)
         quant("ds", 1, 0)
         quant_rows("dom", 0, 1, 1, 2)
@@ -292,16 +303,17 @@ def tile_attend_gat_lse_c_kernel(tc, qT, cT, doT, lse, delta, rw, qm, dom, offs,
         quant_rows("qm", 0, 1, 1, 2)
         quant_rows("qm", 0, 0, 0, 1)
         out_passes("qm", 0, 0)
-        out_passes("qm", 0, 1, 0, 1)
         cast_rows("S", "dom", 1, 0, 1)
         product("ds", 1, 1)
         cast_rows("S", "qm", 1, 0, 1)
-        cast_rows("S", "dom", 2, 0, 1)
+        cast_rows("S", "dom", 1, 1, 2)
         drain(0, 0)
         scatter(0, 0)
-        cast_rows("V", "dom", 1, 1, 2)
+        quant("ds", 0, 1)
+        load_tiles("dom", 1, 3, 4, 4)
+        load_tiles("qm", 1, 3, 4, 4.5)
         quant("ds", 1, 1)
-        out_passes("qm", 0, 1, 1, 2)
+        out_passes("qm", 0, 1)
         drain(0, 1)
         scatter(0, 1)
         store(0)
@@ -312,10 +324,9 @@ def tile_attend_gat_lse_c_kernel(tc, qT, cT, doT, lse, delta, rw, qm, dom, offs,
             for h in range(2):
                 out_passes(name, 1, h)
         finish(1)
-        cast_rows("V", "dom", 2, 1, 2)
+        cast_rows("V", "dom", 2, 0, 2)
         cast_rows("V", "qm", 2, 0, 2)
-        for g in range(G):
-            quant_rows("dom", 2, g, g, g + 1)
+        quant_rows("dom", 2, 0, 0, 2)
         for h in range(2):
             out_passes("dom", 2, h)
         quant_rows("qm", 2, 0, 0, 2)

@@ -22,8 +22,9 @@ KP = P * PACK
 G = R // KP
 DT = D // P
 H = N // 2
+Q = N // 4
 HALF_BYTES = PACK * H * 4
-SEQ_BUFS = 50
+SEQ_BUFS = 49
 
 
 def tile_attend_gat_lse_c_kernel(tc, qT, cT, doT, lse, delta, rw, qm, dom, offs, out):
@@ -48,8 +49,8 @@ def tile_attend_gat_lse_c_kernel(tc, qT, cT, doT, lse, delta, rw, qm, dom, offs,
         def relay_tile(name):
             return ring.tile([P, H * PACK], BF16, name=name, tag="relay", bufs=1, align_bytes=64)
 
-        def second_tile(name):
-            return ring.tile([P, H * PACK], BF16, name=name, tag="second", bufs=1, align_bytes=64)
+        def second_tile(name, width=H * PACK):
+            return ring.tile([P, width], BF16, name=name, tag="second", bufs=1, align_bytes=64)
 
         def big_tile(name, shape):
             return ring.tile(shape, F32, name=name, tag="big", bufs=PACK)
@@ -145,6 +146,14 @@ def tile_attend_gat_lse_c_kernel(tc, qT, cT, doT, lse, delta, rw, qm, dom, offs,
         def quant(name, g, h):
             mx[name, g, h] = quantize("%s%d%d" % (name, g, h), fmt[name], bf[name, g, h])
 
+        pieces = {}
+
+        def quant_slots(name, g, lo, hi, src):
+            pieces.setdefault((name, g), []).append((lo, hi) + quantize("%s%d_%d" % (name, g, lo), fmt[name], src))
+
+        def quant_half(name, g, h):
+            quant_slots(name, g, h * H, (h + 1) * H, bf[name, g, h])
+
         def quant_bank(name, g, t):
             cols = slice((t % 2) * KP, (t % 2 + 1) * KP)
             mx[name, g, "bank", t] = quantize("%s%d_bank%d" % (name, g, t), fmt[name], bf[name, g, t // 2][:, cols])
@@ -212,33 +221,46 @@ def tile_attend_gat_lse_c_kernel(tc, qT, cT, doT, lse, delta, rw, qm, dom, offs,
         acc = {}
         partner = {"dom": "pw", "qm": "ds"}
 
-        def out_passes(name, k, h, lo=0, hi=G):
-            if (k, h) not in acc:
-                acc[k, h] = bank_tile(H)
+        def out_pass(name, k, g, first, lo, hi, start=False, stop=False):
             right = partner[name]
-            for g in range(lo, hi):
-                nc.tensor.matmul_mx(out=acc[k, h][:], lhsT=mx[name, "rows", k, g][0].bitcast(fmt[name]), lhsT_scale=mx[name, "rows", k, g][1],
-                                    rhs=mx[right, g, h][0][:].bitcast(fmt[right]), rhs_scale=mx[right, g, h][1][:],
-                                    start=(name == "dom" and g == 0), stop=(name == "qm" and g == G - 1))
+            left = mx[name, "rows", k, g]
+            for a, b, codes, scales in pieces[right, g]:
+                x, y = max(a, lo), min(b, hi)
+                if x < y:
+                    nc.tensor.matmul_mx(out=acc[k, first][:, x - first:y - first], lhsT=left[0].bitcast(fmt[name]), lhsT_scale=left[1],
+                                        rhs=codes[:, x - a:y - a].bitcast(fmt[right]), rhs_scale=scales[:, x - a:y - a],
+                                        start=start, stop=stop and y == hi)
 
-        stage = {}
+        def product_part(name, g, lo, hi):
+            tile = seq_tile("%s%d_%d_bf" % (name, g, lo), (hi - lo) * PACK, BF16)
+            h, cols = lo // H, slice(lo % H, (hi - 1) % H + 1)
+            nc.vector.tensor_tensor(out=tile[:].rearrange("p (c i t) -> p c t i", i=2, t=PACK),
+                                    in0=read["q", g][:, h, :, cols].rearrange("p t (c i) -> p c t i", i=2),
+                                    in1=read["do", g][:, h, :, cols].rearrange("p t (c i) -> p c t i", i=2), op=ALU.mult)
+            return tile[:]
 
-        def drain(k, h):
-            stage[k, h] = ring.tile([P, H], F32, name="stage", tag="stage", bufs=4)
-            cast("S", stage[k, h][:], acc[k, h][:])
+        def stage_tile():
+            return ring.tile([P, N], F32, name="stage", tag="stage", bufs=2)
 
-        def scatter(k, h):
+        def scatter(k, h, stage):
             cols = slice(h * H // 16, (h + 1) * H // 16)
-            nc.scalar.activation(out=windows[k][:].indirect(offsets[:, cols]), in_=stage[k, h][:], func=ACT.Copy)
+            nc.scalar.activation(out=windows[k][:].indirect(offsets[:, cols]), in_=stage[:, h * H:(h + 1) * H], func=ACT.Copy)
 
         def store(k):
             nc.sync.dma_start(out=out[k * P:(k + 1) * P, :], in_=windows[k][:])
 
+        def half_passes(name, k, g):
+            for h in range(2):
+                if (k, h * H) not in acc:
+                    acc[k, h * H] = bank_tile(H)
+                out_pass(name, k, g, h * H, h * H, (h + 1) * H, start=(name, g) == ("dom", 0), stop=(name, g) == ("qm", 1))
+
         def finish(k):
+            stage = stage_tile()
             for h in range(2):
-                drain(k, h)
+                cast("S", stage[:, h * H:(h + 1) * H], acc[k, h * H][:])
             for h in range(2):
-                scatter(k, h)
+                scatter(k, h, stage)
             store(k)
 
         pair_tile("q", 0, 0)
@@ -261,90 +283,99 @@ def tile_attend_gat_lse_c_kernel(tc, qT, cT, doT, lse, delta, rw, qm, dom, offs,
         product("pw", 0, 1, second_tile)
         quant("q", 1, 1)
         pair_tile("do", 0, 1)
-        cast_pair("S", "do", 0, 1, 0, 128)
-        for t in (2, 3):
-            score("q", 1, t, 0, 2)
-        quant("pw", 0, 0)
+        cast_pair("S", "do", 0, 1)
+        for h in range(2):
+            for t in (2, 3):
+                score("q", 1, t, h, h + 1)
         pair_tile("do", 0, 0)
         cast_pair("V", "do", 0, 0)
+        quant_half("pw", 0, 0)
         quant("do", 0, 0)
         quant("do", 0, 1)
         pair_tile("do", 1, 1)
-        cast_pair("V", "do", 1, 1, 64, P)
-        cast_pair("S", "do", 1, 1, 0, 64)
-        quant("pw", 0, 1)
+        cast_pair("V", "do", 1, 1, 80, P)
+        quant_half("pw", 0, 1)
+        cast_pair("S", "do", 1, 1, 0, 80)
         pair_tile("do", 1, 0, second_tile)
         cast_pair("G", "do", 1, 0)
         product("pw", 1, 0)
         for t in range(PACK):
             score("do", 0, t, 0, 2)
         product("pw", 1, 1)
-        quant("do", 1, 0)
-        quant("pw", 1, 0)
-        quant("do", 1, 1)
-        quant("pw", 1, 1)
+        for h in range(2):
+            quant("do", 1, h)
+            quant_half("pw", 1, h)
         cast_rows("S", "dom", 0, 0, 1, placed(6.375, KP))
-        scores("do", 1, 4)
+        scores("do", 1, 2)
         product("ds", 0, 0, placed(1, H * PACK))
         product("ds", 0, 1, placed(4.25, H * PACK))
-        quant("ds", 0, 0)
+        quant_half("ds", 0, 0)
         load_tiles("qm", 0, 2, 4, 1)
         product("ds", 1, 0)
         cast_rows("S", "dom", 0, 1, 2)
-        cast_rows("V", "qm", 0, 1, 2)
         quant_rows("dom", 0, 0, 0, 1)
         load_tiles("dom", 1, 2, 3, 6)
         load_tiles("qm", 1, 2, 3, 6.5)
+        sums = ((0, H), (H, N))
+        for lo, hi in sums:
+            acc[0, lo] = bank_tile(hi - lo)
+            out_pass("dom", 0, 0, lo, lo, hi, start=True)
         cast_rows("S", "qm", 0, 0, 1)
-        quant("ds", 1, 0)
+        quant_half("ds", 1, 0)
         quant_rows("dom", 0, 1, 1, 2)
-        for h in range(2):
-            out_passes("dom", 0, h)
-        quant_rows("qm", 0, 1, 1, 2)
+        for lo, hi in sums:
+            out_pass("dom", 0, 1, lo, lo, hi)
+        cast_rows("S", "qm", 0, 1, 2)
+        third = product_part("ds", 1, H, H + Q)
         quant_rows("qm", 0, 0, 0, 1)
-        out_passes("qm", 0, 0)
+        out_pass("qm", 0, 0, 0, 0, H)
+        quant_rows("qm", 0, 1, 1, 2)
+        out_pass("qm", 0, 1, 0, 0, H, stop=True)
         cast_rows("S", "dom", 1, 0, 1)
-        product("ds", 1, 1)
-        cast_rows("S", "qm", 1, 0, 1)
-        cast_rows("S", "dom", 1, 1, 2)
-        drain(0, 0)
-        scatter(0, 0)
-        quant("ds", 0, 1)
+        quant_half("ds", 0, 1)
         load_tiles("dom", 1, 3, 4, 4)
         load_tiles("qm", 1, 3, 4, 4.5)
-        quant("ds", 1, 1)
-        out_passes("qm", 0, 1)
-        drain(0, 1)
-        scatter(0, 1)
+        for lo, hi in sums[1:]:
+            out_pass("qm", 0, 0, lo, lo, hi)
+        cast_rows("S", "qm", 1, 0, 1)
+        fourth = product_part("ds", 1, H + Q, N)
+        stage = stage_tile()
+        cast("S", stage[:, 0:H], acc[0, 0][:])
+        scatter(0, 0, stage)
+        for lo, src in ((H, third), (H + Q, fourth)):
+            quant_slots("ds", 1, lo, lo + Q, src)
+            out_pass("qm", 0, 1, H, lo, lo + Q, stop=lo > H)
+        cast("S", stage[:, H:N], acc[0, H][:])
+        scatter(0, 1, stage)
         store(0)
+        cast_rows("V", "dom", 1, 1, 2)
         cast_rows("V", "qm", 1, 1, 2)
-        for name in ("dom", "qm"):
-            for g in range(G):
-                quant_rows(name, 1, g, g, g + 1)
-            for h in range(2):
-                out_passes(name, 1, h)
-        finish(1)
-        cast_rows("V", "dom", 2, 0, 2)
-        cast_rows("V", "qm", 2, 0, 2)
-        quant_rows("dom", 2, 0, 0, 2)
-        for h in range(2):
-            out_passes("dom", 2, h)
-        quant_rows("qm", 2, 0, 0, 2)
-        for h in range(2):
-            out_passes("qm", 2, h)
-        finish(2)
-        cast_rows("V", "dom", 3, 0, 2)
-        cast_rows("V", "qm", 3, 0, 1)
-        quant_rows("dom", 3, 0, 0, 2)
-        for h in range(2):
-            out_passes("dom", 3, h)
-        cast_rows("V", "qm", 3, 1, 2)
         for g in range(G):
-            quant_rows("qm", 3, g, g, g + 1)
-            for h in range(2):
-                out_passes("qm", 3, h, g, g + 1)
-        last = keep.tile([P, N], F32, name="last")
+            quant_rows("dom", 1, g, g, g + 1)
+            half_passes("dom", 1, g)
+        for g in range(G):
+            quant_rows("qm", 1, g, g, g + 1)
+            half_passes("qm", 1, g)
+        cast_rows("S", "dom", 2, 0, 1)
+        finish(1)
+        for k in (2, 3):
+            first = 1 if k == 2 else 0
+            cast_rows("V", "dom", k, first, 2)
+            cast_rows("V", "qm", k, 0, 1)
+            if k == 2:
+                cast_rows("V", "qm", k, 1, 2)
+            for g in range(G):
+                quant_rows("dom", k, g * first, g, g + 1)
+                half_passes("dom", k, g)
+            if k == 3:
+                cast_rows("V", "qm", k, 1, 2)
+            for g in range(G):
+                quant_rows("qm", k, g, g, g + 1)
+                half_passes("qm", k, g)
+            if k == 2:
+                finish(k)
+        last = stage_tile()
         for h in range(2):
-            cast("V", last[:, h * H:(h + 1) * H], acc[3, h][:])
+            cast("V", last[:, h * H:(h + 1) * H], acc[3, h * H][:])
         nc.vector.tensor_copy(out=windows[3][:].indirect(offsets[:]), in_=last[:])
         store(3)

@@ -109,14 +109,14 @@ def tile_attend_gat_lse_c_kernel(tc, qT, cT, doT, lse, delta, rw, qm, dom, offs,
         for t in range(PACK):
             nc.tensor.transpose(turned[:, t, :], rows[:, t::PACK], identity[:])
         columns = keep.tile([P, 3, G, PACK], F32, name="columns")
-        nc.scalar.copy(out=columns[:].rearrange("p v g t -> p g v t"), in_=turned[:].rearrange("p t (g v) -> p g v t", g=G)[:, :, 0:3])
+        nc.vector.tensor_copy(out=columns[:].rearrange("p v g t -> p g v t"), in_=turned[:].rearrange("p t (g v) -> p g v t", g=G)[:, :, 0:3])
         vecs = {name: columns[:, i].rearrange("p g t -> p (g t)") for i, name in enumerate(("lse", "rw", "delta"))}
 
         windows = [keep.tile([P, T], F32, name="window%d" % k) for k in range(DT)]
         for k in range(DT):
             nc.vector.memset(windows[k][:], 0.0)
         neg_lse = keep.tile([P, G * PACK], F32, name="neg_lse")
-        nc.scalar.activation(out=neg_lse[:], in_=vecs["lse"], func=ACT.Identity, scale=-1.0)
+        nc.vector.tensor_scalar(out=neg_lse[:], in0=vecs["lse"], scalar1=-1.0, scalar2=None, op0=ALU.mult)
         neg_rwd = keep.tile([P, G * PACK], F32, name="neg_rwd")
         nc.vector.scalar_tensor_tensor(out=neg_rwd[:], in0=vecs["delta"], scalar=-1.0, in1=vecs["rw"], op0=ALU.mult, op1=ALU.mult)
 
@@ -149,7 +149,14 @@ def tile_attend_gat_lse_c_kernel(tc, qT, cT, doT, lse, delta, rw, qm, dom, offs,
         pieces = {}
 
         def quant_slots(name, g, lo, hi, src):
-            pieces.setdefault((name, g), []).append((lo, hi) + quantize("%s%d_%d" % (name, g, lo), fmt[name], src))
+            if g == 0:
+                pieces.setdefault((name, g), []).append((lo, hi) + quantize("%s%d_%d" % (name, g, lo), fmt[name], src))
+                return
+            if (name, g) not in pieces:
+                label = "%s%d" % (name, g)
+                pieces[name, g] = [(0, N, seq_tile(label + "_codes", N, U32), keep.tile([P, N], U8, name=label + "_scales", align_bytes=64))]
+            codes, scales = pieces[name, g][0][2:]
+            nc.vector.quantize_mx(out=codes[:, lo:hi].bitcast(fmt[name]), scales=scales[:, lo:hi], in_=src)
 
         def quant_half(name, g, h):
             quant_slots(name, g, h * H, (h + 1) * H, bf[name, g, h])
@@ -229,7 +236,7 @@ def tile_attend_gat_lse_c_kernel(tc, qT, cT, doT, lse, delta, rw, qm, dom, offs,
                 if x < y:
                     nc.tensor.matmul_mx(out=acc[k, first][:, x - first:y - first], lhsT=left[0].bitcast(fmt[name]), lhsT_scale=left[1],
                                         rhs=codes[:, x - a:y - a].bitcast(fmt[right]), rhs_scale=scales[:, x - a:y - a],
-                                        start=start, stop=stop and y == hi)
+                                        start=start and x == lo, stop=stop and y == hi)
 
         def product_part(name, g, lo, hi):
             tile = seq_tile("%s%d_%d_bf" % (name, g, lo), (hi - lo) * PACK, BF16)
@@ -240,27 +247,25 @@ def tile_attend_gat_lse_c_kernel(tc, qT, cT, doT, lse, delta, rw, qm, dom, offs,
             return tile[:]
 
         def stage_tile():
-            return ring.tile([P, N], F32, name="stage", tag="stage", bufs=2)
+            return ring.tile([P, N], F32, name="stage", tag="stage", bufs=1)
 
         def scatter(k, h, stage):
             cols = slice(h * H // 16, (h + 1) * H // 16)
-            nc.scalar.activation(out=windows[k][:].indirect(offsets[:, cols]), in_=stage[:, h * H:(h + 1) * H], func=ACT.Copy)
+            nc.scalar.activation(out=windows[k][:].indirect(offsets[:, cols]), in_=stage, func=ACT.Copy)
 
         def store(k):
             nc.sync.dma_start(out=out[k * P:(k + 1) * P, :], in_=windows[k][:])
 
-        def half_passes(name, k, g):
-            for h in range(2):
-                if (k, h * H) not in acc:
-                    acc[k, h * H] = bank_tile(H)
-                out_pass(name, k, g, h * H, h * H, (h + 1) * H, start=(name, g) == ("dom", 0), stop=(name, g) == ("qm", 1))
+        def whole_pass(name, k, g):
+            if (k, 0) not in acc:
+                acc[k, 0] = bank_tile(N)
+            out_pass(name, k, g, 0, 0, N, start=(name, g) == ("dom", 0), stop=(name, g) == ("qm", 1))
 
         def finish(k):
             stage = stage_tile()
+            cast("S", stage[:], acc[k, 0][:])
             for h in range(2):
-                cast("S", stage[:, h * H:(h + 1) * H], acc[k, h * H][:])
-            for h in range(2):
-                scatter(k, h, stage)
+                scatter(k, h, stage[:, h * H:(h + 1) * H])
             store(k)
 
         pair_tile("q", 0, 0)
@@ -308,10 +313,10 @@ def tile_attend_gat_lse_c_kernel(tc, qT, cT, doT, lse, delta, rw, qm, dom, offs,
         cast_rows("S", "dom", 0, 0, 1, placed(6.375, KP))
         scores("do", 1, 2)
         product("ds", 0, 0, placed(1, H * PACK))
-        product("ds", 0, 1, placed(4.25, H * PACK))
+        product("ds", 0, 1)
         quant_half("ds", 0, 0)
         load_tiles("qm", 0, 2, 4, 1)
-        product("ds", 1, 0)
+        product("ds", 1, 0, placed(4.25, H * PACK))
         cast_rows("S", "dom", 0, 1, 2)
         quant_rows("dom", 0, 0, 0, 1)
         load_tiles("dom", 1, 2, 3, 6)
@@ -322,6 +327,8 @@ def tile_attend_gat_lse_c_kernel(tc, qT, cT, doT, lse, delta, rw, qm, dom, offs,
             out_pass("dom", 0, 0, lo, lo, hi, start=True)
         cast_rows("S", "qm", 0, 0, 1)
         quant_half("ds", 1, 0)
+        load_tiles("dom", 1, 3, 4, 4)
+        load_tiles("qm", 1, 3, 4, 4.5)
         quant_rows("dom", 0, 1, 1, 2)
         for lo, hi in sums:
             out_pass("dom", 0, 1, lo, lo, hi)
@@ -331,51 +338,44 @@ def tile_attend_gat_lse_c_kernel(tc, qT, cT, doT, lse, delta, rw, qm, dom, offs,
         out_pass("qm", 0, 0, 0, 0, H)
         quant_rows("qm", 0, 1, 1, 2)
         out_pass("qm", 0, 1, 0, 0, H, stop=True)
+        quant_slots("ds", 1, H, H + Q, third)
+        out_pass("qm", 0, 1, H, H, H + Q)
         cast_rows("S", "dom", 1, 0, 1)
-        quant_half("ds", 0, 1)
-        load_tiles("dom", 1, 3, 4, 4)
-        load_tiles("qm", 1, 3, 4, 4.5)
-        for lo, hi in sums[1:]:
-            out_pass("qm", 0, 0, lo, lo, hi)
-        cast_rows("S", "qm", 1, 0, 1)
         fourth = product_part("ds", 1, H + Q, N)
+        cast_rows("S", "qm", 1, 0, 1)
         stage = stage_tile()
         cast("S", stage[:, 0:H], acc[0, 0][:])
-        scatter(0, 0, stage)
-        for lo, src in ((H, third), (H + Q, fourth)):
-            quant_slots("ds", 1, lo, lo + Q, src)
-            out_pass("qm", 0, 1, H, lo, lo + Q, stop=lo > H)
+        scatter(0, 0, stage[:, 0:H])
+        quant_half("ds", 0, 1)
+        out_pass("qm", 0, 0, H, H, N)
+        quant_slots("ds", 1, H + Q, N, fourth)
+        out_pass("qm", 0, 1, H, H + Q, N, stop=True)
         cast("S", stage[:, H:N], acc[0, H][:])
-        scatter(0, 1, stage)
+        scatter(0, 1, stage[:, H:N])
         store(0)
-        cast_rows("V", "dom", 1, 1, 2)
-        cast_rows("V", "qm", 1, 1, 2)
-        for g in range(G):
-            quant_rows("dom", 1, g, g, g + 1)
-            half_passes("dom", 1, g)
-        for g in range(G):
-            quant_rows("qm", 1, g, g, g + 1)
-            half_passes("qm", 1, g)
-        cast_rows("S", "dom", 2, 0, 1)
+        for name in ("dom", "qm"):
+            quant_rows(name, 1, 0, 0, 1)
+            whole_pass(name, 1, 0)
+        for name in ("dom", "qm"):
+            cast_rows("V", name, 1, 1, 2)
+        for name in ("dom", "qm"):
+            quant_rows(name, 1, 1, 1, 2)
+            whole_pass(name, 1, 1)
         finish(1)
         for k in (2, 3):
-            first = 1 if k == 2 else 0
-            cast_rows("V", "dom", k, first, 2)
+            cast_rows("V", "dom", k, 0, 1)
             cast_rows("V", "qm", k, 0, 1)
-            if k == 2:
-                cast_rows("V", "qm", k, 1, 2)
-            for g in range(G):
-                quant_rows("dom", k, g * first, g, g + 1)
-                half_passes("dom", k, g)
-            if k == 3:
-                cast_rows("V", "qm", k, 1, 2)
-            for g in range(G):
-                quant_rows("qm", k, g, g, g + 1)
-                half_passes("qm", k, g)
+            cast_rows("V", "dom", k, 1, 2)
+            for name in ("dom", "qm"):
+                quant_rows(name, k, 0, 0, 1)
+                whole_pass(name, k, 0)
+            cast_rows("V", "qm", k, 1, 2)
+            for name in ("dom", "qm"):
+                quant_rows(name, k, 1, 1, 2)
+                whole_pass(name, k, 1)
             if k == 2:
                 finish(k)
-        last = stage_tile()
-        for h in range(2):
-            cast("V", last[:, h * H:(h + 1) * H], acc[3, h * H][:])
+        last = keep.tile([P, N], F32, name="last")
+        cast("V", last[:], acc[3, 0][:])
         nc.vector.tensor_copy(out=windows[3][:].indirect(offsets[:]), in_=last[:])
         store(3)

@@ -33,6 +33,7 @@ def tile_attend_gat_lse_c_kernel(tc, qT, cT, doT, lse, delta, rw, qm, dom, offs,
         keep = ctx.enter_context(tc.tile_pool(name="keep", bufs=1))
         ring = ctx.enter_context(tc.tile_pool(name="ring", bufs=1))
         inputs = ctx.enter_context(tc.tile_pool(name="inputs", bufs=1))
+        stages = ctx.enter_context(tc.tile_pool(name="stages", bufs=1))
         psum = ctx.enter_context(tc.psum_pool(name="psum", bufs=1))
 
         def cast(engine, dst, src):
@@ -96,7 +97,14 @@ def tile_attend_gat_lse_c_kernel(tc, qT, cT, doT, lse, delta, rw, qm, dom, offs,
         for g in range(G):
             for n, name in enumerate(source):
                 load_tiles(name, g, 0, 2, 8 + 2 * g + n)
-        load_tiles("dom", 0, 2, 4, 0)
+        late = {}
+
+        def load_late(name, place):
+            late[name] = inputs.tile([P, G, PACK, H], F32, name=name + "_late", offset=place * HALF_BYTES)
+            for g in range(G):
+                load(late[name][:, g], source[name], slice(g * KP, (g + 1) * KP), slice(H, D))
+
+        load_late("dom", 0)
 
         def placed(place, width):
             def make(name):
@@ -170,9 +178,7 @@ def tile_attend_gat_lse_c_kernel(tc, qT, cT, doT, lse, delta, rw, qm, dom, offs,
 
         read = {}
 
-        def score(name, g, t, lo, hi):
-            if (name, g) not in read:
-                read[name, g] = big_tile("%s%d_read" % (name, g), [P, 2, PACK, H])
+        def multiply(name, g, t, lo, hi):
             bank = bank_tile((hi - lo) * H)
             if (name, g, "bank", t) in mx:
                 codes, scales = mx[name, g, "bank", t]
@@ -183,20 +189,27 @@ def tile_attend_gat_lse_c_kernel(tc, qT, cT, doT, lse, delta, rw, qm, dom, offs,
             slots = slice(lo * H, hi * H)
             nc.tensor.matmul_mx(out=bank[:], lhsT=codes[:, cols].bitcast(fmt[name]), lhsT_scale=scales[:, cols],
                                 rhs=c_mx[0][:, slots].bitcast(E4), rhs_scale=c_mx[1][:, slots], start=True, stop=True)
+            return bank[:]
+
+        def read_bank(name, g, t, lo, hi, bank):
+            if (name, g) not in read:
+                read[name, g] = big_tile("%s%d_read" % (name, g), [P, 2, PACK, H])
             u = g * PACK + t
             dst = read[name, g][:, lo:hi, t, :]
-            src = bank[:].rearrange("p (h n) -> p h n", n=H)
+            src = bank.rearrange("p (h n) -> p h n", n=H)
             if name == "q":
                 nc.scalar.activation(out=dst, in_=src, func=ACT.Exp, bias=neg_lse[:, u:u + 1], scale=1.0)
             else:
                 nc.scalar.activation(out=dst, in_=src, func=ACT.Identity, bias=neg_rwd[:, u:u + 1], scale=vecs["rw"][:, u:u + 1])
 
-        def scores(name, g, whole):
-            for t in range(whole):
-                score(name, g, t, 0, 2)
+        def score(name, g, t, lo, hi):
+            read_bank(name, g, t, lo, hi, multiply(name, g, t, lo, hi))
+
+        def last_banks(name, g):
+            banks = {t: multiply(name, g, t, 0, 2) for t in (2, 3)}
             for h in range(2):
-                for t in range(whole, PACK):
-                    score(name, g, t, h, h + 1)
+                for t in (2, 3):
+                    read_bank(name, g, t, h, h + 1, banks[t][:, h * H:(h + 1) * H])
 
         def product(name, g, h, make=in_seq):
             if (name, g, h) not in bf:
@@ -217,6 +230,12 @@ def tile_attend_gat_lse_c_kernel(tc, qT, cT, doT, lse, delta, rw, qm, dom, offs,
                 src = raw[name, g, k].rearrange("p j (c i) -> p c j i", i=2)
                 dst = tile[:, (g - lo) * KP:(g - lo + 1) * KP].rearrange("p (c i j) -> p c j i", i=2, j=PACK)
                 cast(engine, dst, src)
+
+        def cast_late(engine, name, k, lo, hi):
+            tile = seq_tile("%s_bf%d%d" % (name, k, lo), (hi - lo) * KP, BF16)
+            bf[name, "rows", k, lo] = tile[:]
+            src = late[name][:, lo:hi, :, (k - 2) * P:(k - 1) * P].rearrange("p g j (c i) -> p g c j i", i=2)
+            cast(engine, tile[:].rearrange("p (g c i j) -> p g c j i", g=hi - lo, i=2, j=PACK), src)
 
         def quant_rows(name, k, first, lo, hi):
             src = bf[name, "rows", k, first][:, (lo - first) * KP:(hi - first) * KP]
@@ -246,8 +265,8 @@ def tile_attend_gat_lse_c_kernel(tc, qT, cT, doT, lse, delta, rw, qm, dom, offs,
                                     in1=read["do", g][:, h, :, cols].rearrange("p t (c i) -> p c t i", i=2), op=ALU.mult)
             return tile[:]
 
-        def stage_tile():
-            return ring.tile([P, N], F32, name="stage", tag="stage", bufs=1)
+        def drained(name, shape, dtype, offset):
+            return stages.tile(shape, dtype, name=name, offset=offset, align_bytes=64)
 
         def scatter(k, h, stage):
             cols = slice(h * H // 16, (h + 1) * H // 16)
@@ -262,8 +281,9 @@ def tile_attend_gat_lse_c_kernel(tc, qT, cT, doT, lse, delta, rw, qm, dom, offs,
             out_pass(name, k, g, 0, 0, N, start=(name, g) == ("dom", 0), stop=(name, g) == ("qm", 1))
 
         def finish(k):
-            stage = stage_tile()
-            cast("S", stage[:], acc[k, 0][:])
+            stage = drained("stage%d" % k, [P, N], F32, 0)
+            for h in range(2):
+                cast("S", stage[:, h * H:(h + 1) * H], acc[k, 0][:, h * H:(h + 1) * H])
             for h in range(2):
                 scatter(k, h, stage[:, h * H:(h + 1) * H])
             store(k)
@@ -275,7 +295,9 @@ def tile_attend_gat_lse_c_kernel(tc, qT, cT, doT, lse, delta, rw, qm, dom, offs,
         cast_pair("V", "q", 0, 1, 80, P)
         for t in range(PACK):
             quant_bank("q", 0, t)
-        scores("q", 0, 0)
+        for h in range(2):
+            for t in range(PACK):
+                score("q", 0, t, h, h + 1)
         pair_tile("q", 1, 0, relay_tile)
         cast_pair("V", "q", 1, 0)
         for t in (0, 1):
@@ -289,9 +311,7 @@ def tile_attend_gat_lse_c_kernel(tc, qT, cT, doT, lse, delta, rw, qm, dom, offs,
         quant("q", 1, 1)
         pair_tile("do", 0, 1)
         cast_pair("S", "do", 0, 1)
-        for h in range(2):
-            for t in (2, 3):
-                score("q", 1, t, h, h + 1)
+        last_banks("q", 1)
         pair_tile("do", 0, 0)
         cast_pair("V", "do", 0, 0)
         quant_half("pw", 0, 0)
@@ -310,25 +330,23 @@ def tile_attend_gat_lse_c_kernel(tc, qT, cT, doT, lse, delta, rw, qm, dom, offs,
         for h in range(2):
             quant("do", 1, h)
             quant_half("pw", 1, h)
-        cast_rows("S", "dom", 0, 0, 1, placed(6.375, KP))
-        scores("do", 1, 2)
-        product("ds", 0, 0, placed(1, H * PACK))
+        cast_rows("S", "dom", 0, 0, 1, placed(6, KP))
+        for t in (0, 1):
+            score("do", 1, t, 0, 2)
+        last_banks("do", 1)
+        product("ds", 0, 0, placed(2, H * PACK))
         product("ds", 0, 1)
         quant_half("ds", 0, 0)
-        load_tiles("qm", 0, 2, 4, 1)
-        product("ds", 1, 0, placed(4.25, H * PACK))
+        load_late("qm", 2)
+        product("ds", 1, 0)
         cast_rows("S", "dom", 0, 1, 2)
         quant_rows("dom", 0, 0, 0, 1)
-        load_tiles("dom", 1, 2, 3, 6)
-        load_tiles("qm", 1, 2, 3, 6.5)
         sums = ((0, H), (H, N))
         for lo, hi in sums:
             acc[0, lo] = bank_tile(hi - lo)
             out_pass("dom", 0, 0, lo, lo, hi, start=True)
         cast_rows("S", "qm", 0, 0, 1)
         quant_half("ds", 1, 0)
-        load_tiles("dom", 1, 3, 4, 4)
-        load_tiles("qm", 1, 3, 4, 4.5)
         quant_rows("dom", 0, 1, 1, 2)
         for lo, hi in sums:
             out_pass("dom", 0, 1, lo, lo, hi)
@@ -343,15 +361,16 @@ def tile_attend_gat_lse_c_kernel(tc, qT, cT, doT, lse, delta, rw, qm, dom, offs,
         cast_rows("S", "dom", 1, 0, 1)
         fourth = product_part("ds", 1, H + Q, N)
         cast_rows("S", "qm", 1, 0, 1)
-        stage = stage_tile()
-        cast("S", stage[:, 0:H], acc[0, 0][:])
-        scatter(0, 0, stage[:, 0:H])
+        opening = drained("opening", [P, H], F32, 0)
+        cast("S", opening[:], acc[0, 0][:])
+        scatter(0, 0, opening[:])
         quant_half("ds", 0, 1)
         out_pass("qm", 0, 0, H, H, N)
         quant_slots("ds", 1, H + Q, N, fourth)
         out_pass("qm", 0, 1, H, H + Q, N, stop=True)
-        cast("S", stage[:, H:N], acc[0, H][:])
-        scatter(0, 1, stage[:, H:N])
+        closing = drained("closing", [P, H], F32, 1024)
+        cast("S", closing[:], acc[0, H][:])
+        scatter(0, 1, closing[:])
         store(0)
         for name in ("dom", "qm"):
             quant_rows(name, 1, 0, 0, 1)
@@ -361,21 +380,36 @@ def tile_attend_gat_lse_c_kernel(tc, qT, cT, doT, lse, delta, rw, qm, dom, offs,
         for name in ("dom", "qm"):
             quant_rows(name, 1, 1, 1, 2)
             whole_pass(name, 1, 1)
+        cast_late("V", "dom", 2, 1, 2)
+        cast_late("V", "qm", 2, 0, 2)
+        cast_late("S", "dom", 2, 0, 1)
         finish(1)
-        for k in (2, 3):
-            cast_rows("V", "dom", k, 0, 1)
-            cast_rows("V", "qm", k, 0, 1)
-            cast_rows("V", "dom", k, 1, 2)
-            for name in ("dom", "qm"):
-                quant_rows(name, k, 0, 0, 1)
-                whole_pass(name, k, 0)
-            cast_rows("V", "qm", k, 1, 2)
-            for name in ("dom", "qm"):
-                quant_rows(name, k, 1, 1, 2)
-                whole_pass(name, k, 1)
-            if k == 2:
-                finish(k)
+        quant_rows("dom", 2, 1, 1, 2)
+        quant_rows("dom", 2, 0, 0, 1)
+        for g in range(G):
+            whole_pass("dom", 2, g)
+        quant_rows("qm", 2, 0, 0, 2)
+        for g in range(G):
+            whole_pass("qm", 2, g)
+        finish(2)
+        for h in range(2):
+            acc[3, h * H] = bank_tile(H)
+
+        def last_passes(name, g):
+            for h in range(2):
+                out_pass(name, 3, g, h * H, h * H, (h + 1) * H, start=(name, g) == ("dom", 0), stop=(name, g) == ("qm", 1))
+
+        cast_late("V", "dom", 3, 0, 2)
+        cast_late("V", "qm", 3, 0, 1)
+        quant_rows("dom", 3, 0, 0, 2)
+        for g in range(G):
+            last_passes("dom", g)
+        cast_late("V", "qm", 3, 1, 2)
+        for g in range(G):
+            quant_rows("qm", 3, g, g, g + 1)
+            last_passes("qm", g)
         last = keep.tile([P, N], F32, name="last")
-        cast("V", last[:], acc[3, 0][:])
+        for h in range(2):
+            cast("V", last[:, h * H:(h + 1) * H], acc[3, h * H][:])
         nc.vector.tensor_copy(out=windows[3][:].indirect(offsets[:]), in_=last[:])
         store(3)

@@ -275,15 +275,17 @@ def tile_attend_gat_lse_c_kernel(tc, qT, cT, doT, lse, delta, rw, qm, dom, offs,
         def store(k):
             nc.sync.dma_start(out=out[k * P:(k + 1) * P, :], in_=windows[k][:])
 
-        def whole_pass(name, k, g):
-            if (k, 0) not in acc:
-                acc[k, 0] = bank_tile(N)
-            out_pass(name, k, g, 0, 0, N, start=(name, g) == ("dom", 0), stop=(name, g) == ("qm", 1))
-
-        def finish(k):
-            stage = drained("stage%d" % k, [P, N], F32, 0)
+        def half_passes(name, k, g):
+            start = (k, 0) not in acc
             for h in range(2):
-                cast("S", stage[:, h * H:(h + 1) * H], acc[k, 0][:, h * H:(h + 1) * H])
+                if start:
+                    acc[k, h * H] = bank_tile(H)
+                out_pass(name, k, g, h * H, h * H, (h + 1) * H, start=start, stop=(name, g) == ("qm", 1))
+
+        def finish(k, engines="SS"):
+            stage = drained("stage%d" % k, [P, N], F32, 0)
+            for h, engine in enumerate(engines):
+                cast(engine, stage[:, h * H:(h + 1) * H], acc[k, h * H][:])
             for h in range(2):
                 scatter(k, h, stage[:, h * H:(h + 1) * H])
             store(k)
@@ -323,13 +325,16 @@ def tile_attend_gat_lse_c_kernel(tc, qT, cT, doT, lse, delta, rw, qm, dom, offs,
         cast_pair("S", "do", 1, 1, 0, 80)
         pair_tile("do", 1, 0, second_tile)
         cast_pair("G", "do", 1, 0)
+        both = placed(4, N * PACK)("pw1_bf")
+        for h in range(2):
+            bf["pw", 1, h] = both[:, h * H * PACK:(h + 1) * H * PACK]
         product("pw", 1, 0)
         for t in range(PACK):
             score("do", 0, t, 0, 2)
         product("pw", 1, 1)
-        for h in range(2):
-            quant("do", 1, h)
-            quant_half("pw", 1, h)
+        for u in range(2):
+            quant("do", 1, u)
+        quant_slots("pw", 1, 0, N, both[:])
         cast_rows("S", "dom", 0, 0, 1, placed(6, KP))
         for t in (0, 1):
             score("do", 1, t, 0, 2)
@@ -368,18 +373,18 @@ def tile_attend_gat_lse_c_kernel(tc, qT, cT, doT, lse, delta, rw, qm, dom, offs,
         out_pass("qm", 0, 0, H, H, N)
         quant_slots("ds", 1, H + Q, N, fourth)
         out_pass("qm", 0, 1, H, H + Q, N, stop=True)
-        closing = drained("closing", [P, H], F32, 1024)
-        cast("S", closing[:], acc[0, H][:])
-        scatter(0, 1, closing[:])
-        store(0)
         for name in ("dom", "qm"):
             quant_rows(name, 1, 0, 0, 1)
-            whole_pass(name, 1, 0)
-        for name in ("dom", "qm"):
-            cast_rows("V", name, 1, 1, 2)
+            half_passes(name, 1, 0)
+        cast_rows("V", "dom", 1, 1, 2)
+        closing = seq_tile("closing", H, F32)
+        cast("V", closing[:], acc[0, H][:])
+        scatter(0, 1, closing[:])
+        store(0)
+        cast_rows("V", "qm", 1, 1, 2)
         for name in ("dom", "qm"):
             quant_rows(name, 1, 1, 1, 2)
-            whole_pass(name, 1, 1)
+            half_passes(name, 1, 1)
         cast_late("V", "dom", 2, 1, 2)
         cast_late("V", "qm", 2, 0, 2)
         cast_late("S", "dom", 2, 0, 1)
@@ -387,27 +392,20 @@ def tile_attend_gat_lse_c_kernel(tc, qT, cT, doT, lse, delta, rw, qm, dom, offs,
         quant_rows("dom", 2, 1, 1, 2)
         quant_rows("dom", 2, 0, 0, 1)
         for g in range(G):
-            whole_pass("dom", 2, g)
+            half_passes("dom", 2, g)
         quant_rows("qm", 2, 0, 0, 2)
         for g in range(G):
-            whole_pass("qm", 2, g)
+            half_passes("qm", 2, g)
         finish(2)
-        for h in range(2):
-            acc[3, h * H] = bank_tile(H)
-
-        def last_passes(name, g):
-            for h in range(2):
-                out_pass(name, 3, g, h * H, h * H, (h + 1) * H, start=(name, g) == ("dom", 0), stop=(name, g) == ("qm", 1))
-
         cast_late("V", "dom", 3, 0, 2)
         cast_late("V", "qm", 3, 0, 1)
         quant_rows("dom", 3, 0, 0, 2)
         for g in range(G):
-            last_passes("dom", g)
+            half_passes("dom", 3, g)
         cast_late("V", "qm", 3, 1, 2)
         for g in range(G):
             quant_rows("qm", 3, g, g, g + 1)
-            last_passes("qm", g)
+            half_passes("qm", 3, g)
         last = keep.tile([P, N], F32, name="last")
         for h in range(2):
             cast("V", last[:, h * H:(h + 1) * H], acc[3, h * H][:])

from contextlib import ExitStack

import concourse.mybir as mybir
from concourse.masks import make_identity

N, T, D, R = 512, 2048, 512, 1024
FLOPS = 4 * 2 * R * N * D

F32 = mybir.dt.float32
BF16 = mybir.dt.bfloat16
U32 = mybir.dt.uint32
U16 = mybir.dt.uint16
U8 = mybir.dt.uint8
E4 = mybir.dt.float8_e4m3fn_x4
E5 = mybir.dt.float8_e5m2_x4
ACT = mybir.ActivationFunctionType
ALU = mybir.AluOpType

P = 128
PACK = 4
KP = P * PACK
G = R // KP
DT = D // P
H = N // 2
Q = N // 4
HALF_BYTES = PACK * H * 4
SEQ_BUFS = 49


def tile_attend_gat_lse_c_kernel(tc, qT, cT, doT, lse, delta, rw, qm, dom, offs, out):
    nc = tc.nc
    with ExitStack() as ctx:
        keep = ctx.enter_context(tc.tile_pool(name="keep", bufs=1))
        ring = ctx.enter_context(tc.tile_pool(name="ring", bufs=1))
        inputs = ctx.enter_context(tc.tile_pool(name="inputs", bufs=1))
        stages = ctx.enter_context(tc.tile_pool(name="stages", bufs=1))
        psum = ctx.enter_context(tc.psum_pool(name="psum", bufs=1))

        def cast(engine, dst, src):
            if engine == "S":
                nc.scalar.copy(out=dst, in_=src)
            elif engine == "G":
                nc.gpsimd.tensor_scalar(out=dst, in0=src, scalar1=1.0, scalar2=0.0, op0=ALU.mult, op1=ALU.add)
            else:
                nc.vector.tensor_copy(out=dst, in_=src)

        def seq_tile(name, width, dtype):
            return ring.tile([P, width], dtype, name=name, tag="seq", bufs=SEQ_BUFS, align_bytes=64)

        def relay_tile(name):
            return ring.tile([P, H * PACK], BF16, name=name, tag="relay", bufs=1, align_bytes=64)

        def second_tile(name, width=H * PACK):
            return ring.tile([P, width], BF16, name=name, tag="second", bufs=1, align_bytes=64)

        def big_tile(name, shape):
            return ring.tile(shape, F32, name=name, tag="big", bufs=PACK)

        def raw_tile(name, width, place):
            return inputs.tile([P, PACK, width], F32, name=name, offset=int(place * HALF_BYTES))

        def quantize(name, fmt, src):
            width = src.shape[1] // PACK
            codes = seq_tile(name + "_codes", width, U32)
            scales = keep.tile([P, width], U8, name=name + "_scales", align_bytes=64)
            nc.vector.quantize_mx(out=codes[:].bitcast(fmt), scales=scales[:], in_=src)
            return codes, scales

        offsets = keep.tile([P, N // 16], U16, name="offsets")
        planes = [big_tile("plane%d" % j, [P, T]) for j in range(PACK)]
        c_rows = cT.rearrange("(p j) w -> j p w", j=PACK)
        nc.sync.dma_start(out=planes[0][:], in_=c_rows[0])
        nc.sync.dma_start(offsets[:], offs)
        rows = keep.tile([P, KP], F32, name="rows")
        nc.vector.memset(rows[:], 0.0)
        for i, src in enumerate((lse, rw, delta)):
            nc.sync.dma_start(out=rows[i:P:P // G, :], in_=src[0].rearrange("(g w) o -> g (w o)", g=G))
        for j in range(1, PACK):
            nc.sync.dma_start(out=planes[j][:], in_=c_rows[j])

        def load(tile, src, rows, cols):
            nc.sync.dma_start(out=tile, in_=src[0][rows, cols].rearrange("(p j) w -> p j w", j=PACK))
            return tile

        raw = {}
        for n, (name, src) in enumerate((("q", qT), ("do", doT))):
            for g in range(G):
                raw[name, g] = load(raw_tile("%s%d" % (name, g), KP, 2 * (G * n + g))[:], src, slice(0, D), slice(g * KP, (g + 1) * KP))
        source = {"dom": dom, "qm": qm}

        def load_tiles(name, g, lo, hi, place):
            tile = raw_tile("%s%d%d" % (name, g, lo), (hi - lo) * P, place)
            load(tile[:], source[name], slice(g * KP, (g + 1) * KP), slice(lo * P, hi * P))
            for k in range(lo, hi):
                raw[name, g, k] = tile[:, :, (k - lo) * P:(k - lo + 1) * P]

        for g in range(G):
            for n, name in enumerate(source):
                load_tiles(name, g, 0, 2, 8 + 2 * g + n)
        late = {}

        def load_late(name, place):
            late[name] = inputs.tile([P, G, PACK, H], F32, name=name + "_late", offset=place * HALF_BYTES)
            for g in range(G):
                load(late[name][:, g], source[name], slice(g * KP, (g + 1) * KP), slice(H, D))

        load_late("dom", 0)

        def placed(place, width):
            def make(name):
                return inputs.tile([P, width], BF16, name=name, offset=int(place * HALF_BYTES), align_bytes=64)
            return make

        identity = keep.tile([P, P], F32, name="identity")
        make_identity(nc, identity[:])
        turned = psum.tile([P, PACK, P], F32, name="turned")
        for t in range(PACK):
            nc.tensor.transpose(turned[:, t, :], rows[:, t::PACK], identity[:])
        columns = keep.tile([P, 3, G, PACK], F32, name="columns")
        nc.vector.tensor_copy(out=columns[:].rearrange("p v g t -> p g v t"), in_=turned[:].rearrange("p t (g v) -> p g v t", g=G)[:, :, 0:3])
        vecs = {name: columns[:, i].rearrange("p g t -> p (g t)") for i, name in enumerate(("lse", "rw", "delta"))}

        windows = [keep.tile([P, T], F32, name="window%d" % k) for k in range(DT)]
        for k in range(DT):
            nc.vector.memset(windows[k][:], 0.0)
        neg_lse = keep.tile([P, G * PACK], F32, name="neg_lse")
        nc.vector.tensor_scalar(out=neg_lse[:], in0=vecs["lse"], scalar1=-1.0, scalar2=None, op0=ALU.mult)
        neg_rwd = keep.tile([P, G * PACK], F32, name="neg_rwd")
        nc.vector.scalar_tensor_tensor(out=neg_rwd[:], in0=vecs["delta"], scalar=-1.0, in1=vecs["rw"], op0=ALU.mult, op1=ALU.mult)

        c_bf = keep.tile([P, N, PACK], BF16, name="c_bf", align_bytes=64)
        early = keep.tile([P, PACK - 1, N], BF16, name="early")
        for j in range(PACK - 1):
            nc.scalar.activation(out=early[:, j, :], in_=planes[j][:].indirect(offsets[:]), func=ACT.Copy)
        cast("V", c_bf[:, :, 0:PACK - 1], early[:].rearrange("p j n -> p n j"))
        nc.vector.tensor_copy(out=c_bf[:, :, PACK - 1], in_=planes[PACK - 1][:].indirect(offsets[:]))
        c_mx = quantize("c", E4, c_bf[:].rearrange("p n j -> p (n j)"))

        fmt = {"q": E4, "do": E5, "qm": E4, "dom": E5, "pw": E4, "ds": E5}
        bf = {}
        mx = {}

        def in_seq(name):
            return seq_tile(name, H * PACK, BF16)

        def pair_tile(name, g, u, make=in_seq):
            bf[name, g, u] = make("%s%d%d_bf" % (name, g, u))[:]

        def cast_pair(engine, name, g, u, lo=0, hi=P):
            order = "m e j" if engine == "G" else "m j e"
            src = raw[name, g].rearrange("p j (m u e) -> p u " + order, u=2, e=2)[:, u, lo:hi]
            cast(engine, bf[name, g, u].rearrange("p (e m j) -> p " + order, e=2, j=PACK)[:, lo:hi], src)

        def quant(name, g, h):
            mx[name, g, h] = quantize("%s%d%d" % (name, g, h), fmt[name], bf[name, g, h])

        pieces = {}

        def quant_slots(name, g, lo, hi, src):
            if g == 0:
                pieces.setdefault((name, g), []).append((lo, hi) + quantize("%s%d_%d" % (name, g, lo), fmt[name], src))
                return
            if (name, g) not in pieces:
                label = "%s%d" % (name, g)
                pieces[name, g] = [(0, N, seq_tile(label + "_codes", N, U32), keep.tile([P, N], U8, name=label + "_scales", align_bytes=64))]
            codes, scales = pieces[name, g][0][2:]
            nc.vector.quantize_mx(out=codes[:, lo:hi].bitcast(fmt[name]), scales=scales[:, lo:hi], in_=src)

        def quant_half(name, g, h):
            quant_slots(name, g, h * H, (h + 1) * H, bf[name, g, h])

        def quant_bank(name, g, t):
            cols = slice((t % 2) * KP, (t % 2 + 1) * KP)
            mx[name, g, "bank", t] = quantize("%s%d_bank%d" % (name, g, t), fmt[name], bf[name, g, t // 2][:, cols])

        def bank_tile(width):
            return psum.tile([P, width], F32, name="bank", tag="bank", bufs=7)

        read = {}

        def multiply(name, g, t, lo, hi):
            bank = bank_tile((hi - lo) * H)
            if (name, g, "bank", t) in mx:
                codes, scales = mx[name, g, "bank", t]
                cols = slice(0, P)
            else:
                codes, scales = mx[name, g, t // 2]
                cols = slice((t % 2) * P, (t % 2 + 1) * P)
            slots = slice(lo * H, hi * H)
            nc.tensor.matmul_mx(out=bank[:], lhsT=codes[:, cols].bitcast(fmt[name]), lhsT_scale=scales[:, cols],
                                rhs=c_mx[0][:, slots].bitcast(E4), rhs_scale=c_mx[1][:, slots], start=True, stop=True)
            return bank[:]

        def read_bank(name, g, t, lo, hi, bank):
            if (name, g) not in read:
                read[name, g] = big_tile("%s%d_read" % (name, g), [P, 2, PACK, H])
            u = g * PACK + t
            dst = read[name, g][:, lo:hi, t, :]
            src = bank.rearrange("p (h n) -> p h n", n=H)
            if name == "q":
                nc.scalar.activation(out=dst, in_=src, func=ACT.Exp, bias=neg_lse[:, u:u + 1], scale=1.0)
            else:
                nc.scalar.activation(out=dst, in_=src, func=ACT.Identity, bias=neg_rwd[:, u:u + 1], scale=vecs["rw"][:, u:u + 1])

        def score(name, g, t, lo, hi):
            read_bank(name, g, t, lo, hi, multiply(name, g, t, lo, hi))

        def last_banks(name, g):
            banks = {t: multiply(name, g, t, 0, 2) for t in (2, 3)}
            for h in range(2):
                for t in (2, 3):
                    read_bank(name, g, t, h, h + 1, banks[t][:, h * H:(h + 1) * H])

        def product(name, g, h, make=in_seq):
            if (name, g, h) not in bf:
                bf[name, g, h] = make("%s%d%d_bf" % (name, g, h))[:]
            dst = bf[name, g, h].rearrange("p (c i t) -> p c t i", i=2, t=PACK)
            in0 = read["q", g][:, h].rearrange("p t (c i) -> p c t i", i=2)
            if name == "pw":
                in1 = turned[:, :, g * (P // G) + 1].unsqueeze(1).unsqueeze(3).broadcast_to([P, H // 2, PACK, 2])
            else:
                in1 = read["do", g][:, h].rearrange("p t (c i) -> p c t i", i=2)
            nc.vector.tensor_tensor(out=dst, in0=in0, in1=in1, op=ALU.mult)

        def cast_rows(engine, name, k, lo, hi, make=None):
            label = "%s_bf%d%d" % (name, k, lo)
            tile = make(label) if make else seq_tile(label, (hi - lo) * KP, BF16)
            bf[name, "rows", k, lo] = tile[:]
            for g in range(lo, hi):
                src = raw[name, g, k].rearrange("p j (c i) -> p c j i", i=2)
                dst = tile[:, (g - lo) * KP:(g - lo + 1) * KP].rearrange("p (c i j) -> p c j i", i=2, j=PACK)
                cast(engine, dst, src)

        def cast_late(engine, name, k, lo, hi):
            tile = seq_tile("%s_bf%d%d" % (name, k, lo), (hi - lo) * KP, BF16)
            bf[name, "rows", k, lo] = tile[:]
            src = late[name][:, lo:hi, :, (k - 2) * P:(k - 1) * P].rearrange("p g j (c i) -> p g c j i", i=2)
            cast(engine, tile[:].rearrange("p (g c i j) -> p g c j i", g=hi - lo, i=2, j=PACK), src)

        def quant_rows(name, k, first, lo, hi):
            src = bf[name, "rows", k, first][:, (lo - first) * KP:(hi - first) * KP]
            codes, scales = quantize("%s%d%d" % (name, k, lo), fmt[name], src)
            for g in range(lo, hi):
                cols = slice((g - lo) * P, (g - lo + 1) * P)
                mx[name, "rows", k, g] = codes[:, cols], scales[:, cols]

        acc = {}
        partner = {"dom": "pw", "qm": "ds"}

        def out_pass(name, k, g, first, lo, hi, start=False, stop=False):
            right = partner[name]
            left = mx[name, "rows", k, g]
            for a, b, codes, scales in pieces[right, g]:
                x, y = max(a, lo), min(b, hi)
                if x < y:
                    nc.tensor.matmul_mx(out=acc[k, first][:, x - first:y - first], lhsT=left[0].bitcast(fmt[name]), lhsT_scale=left[1],
                                        rhs=codes[:, x - a:y - a].bitcast(fmt[right]), rhs_scale=scales[:, x - a:y - a],
                                        start=start and x == lo, stop=stop and y == hi)

        def product_part(name, g, lo, hi):
            tile = seq_tile("%s%d_%d_bf" % (name, g, lo), (hi - lo) * PACK, BF16)
            h, cols = lo // H, slice(lo % H, (hi - 1) % H + 1)
            nc.vector.tensor_tensor(out=tile[:].rearrange("p (c i t) -> p c t i", i=2, t=PACK),
                                    in0=read["q", g][:, h, :, cols].rearrange("p t (c i) -> p c t i", i=2),
                                    in1=read["do", g][:, h, :, cols].rearrange("p t (c i) -> p c t i", i=2), op=ALU.mult)
            return tile[:]

        def drained(name, shape, dtype, offset):
            return stages.tile(shape, dtype, name=name, offset=offset, align_bytes=64)

        def scatter(k, h, stage):
            cols = slice(h * H // 16, (h + 1) * H // 16)
            nc.scalar.activation(out=windows[k][:].indirect(offsets[:, cols]), in_=stage, func=ACT.Copy)

        def store(k):
            nc.sync.dma_start(out=out[k * P:(k + 1) * P, :], in_=windows[k][:])

        def half_passes(name, k, g):
            start = (k, 0) not in acc
            for h in range(2):
                if start:
                    acc[k, h * H] = bank_tile(H)
                out_pass(name, k, g, h * H, h * H, (h + 1) * H, start=start, stop=(name, g) == ("qm", 1))

        def finish(k, engines="SS"):
            stage = drained("stage%d" % k, [P, N], F32, 0)
            for h, engine in enumerate(engines):
                cast(engine, stage[:, h * H:(h + 1) * H], acc[k, h * H][:])
            for h in range(2):
                scatter(k, h, stage[:, h * H:(h + 1) * H])
            store(k)

        pair_tile("q", 0, 0)
        cast_pair("V", "q", 0, 0)
        pair_tile("q", 0, 1, relay_tile)
        cast_pair("S", "q", 0, 1, 0, 80)
        cast_pair("V", "q", 0, 1, 80, P)
        for t in range(PACK):
            quant_bank("q", 0, t)
        for h in range(2):
            for t in range(PACK):
                score("q", 0, t, h, h + 1)
        pair_tile("q", 1, 0, relay_tile)
        cast_pair("V", "q", 1, 0)
        for t in (0, 1):
            quant_bank("q", 1, t)
        pair_tile("q", 1, 1, relay_tile)
        cast_pair("G", "q", 1, 1)
        product("pw", 0, 0)
        for t in (0, 1):
            score("q", 1, t, 0, 2)
        product("pw", 0, 1, second_tile)
        quant("q", 1, 1)
        pair_tile("do", 0, 1)
        cast_pair("S", "do", 0, 1)
        last_banks("q", 1)
        pair_tile("do", 0, 0)
        cast_pair("V", "do", 0, 0)
        quant_half("pw", 0, 0)
        quant("do", 0, 0)
        quant("do", 0, 1)
        pair_tile("do", 1, 1)
        cast_pair("V", "do", 1, 1, 80, P)
        quant_half("pw", 0, 1)
        cast_pair("S", "do", 1, 1, 0, 80)
        pair_tile("do", 1, 0, second_tile)
        cast_pair("G", "do", 1, 0)
        both = placed(4, N * PACK)("pw1_bf")
        for h in range(2):
            bf["pw", 1, h] = both[:, h * H * PACK:(h + 1) * H * PACK]
        product("pw", 1, 0)
        for t in range(PACK):
            score("do", 0, t, 0, 2)
        product("pw", 1, 1)
        for u in range(2):
            quant("do", 1, u)
        quant_slots("pw", 1, 0, N, both[:])
        cast_rows("S", "dom", 0, 0, 1, placed(6, KP))
        for t in (0, 1):
            score("do", 1, t, 0, 2)
        last_banks("do", 1)
        product("ds", 0, 0, placed(2, H * PACK))
        product("ds", 0, 1)
        quant_half("ds", 0, 0)
        load_late("qm", 2)
        product("ds", 1, 0)
        cast_rows("S", "dom", 0, 1, 2)
        quant_rows("dom", 0, 0, 0, 1)
        sums = ((0, H), (H, N))
        for lo, hi in sums:
            acc[0, lo] = bank_tile(hi - lo)
            out_pass("dom", 0, 0, lo, lo, hi, start=True)
        cast_rows("S", "qm", 0, 0, 1)
        quant_half("ds", 1, 0)
        quant_rows("dom", 0, 1, 1, 2)
        for lo, hi in sums:
            out_pass("dom", 0, 1, lo, lo, hi)
        cast_rows("S", "qm", 0, 1, 2)
        third = product_part("ds", 1, H, H + Q)
        quant_rows("qm", 0, 0, 0, 1)
        out_pass("qm", 0, 0, 0, 0, H)
        quant_rows("qm", 0, 1, 1, 2)
        out_pass("qm", 0, 1, 0, 0, H, stop=True)
        quant_slots("ds", 1, H, H + Q, third)
        out_pass("qm", 0, 1, H, H, H + Q)
        cast_rows("S", "dom", 1, 0, 1)
        fourth = product_part("ds", 1, H + Q, N)
        cast_rows("S", "qm", 1, 0, 1)
        opening = drained("opening", [P, H], F32, 0)
        cast("S", opening[:], acc[0, 0][:])
        scatter(0, 0, opening[:])
        quant_half("ds", 0, 1)
        out_pass("qm", 0, 0, H, H, N)
        quant_slots("ds", 1, H + Q, N, fourth)
        out_pass("qm", 0, 1, H, H + Q, N, stop=True)
        for name in ("dom", "qm"):
            quant_rows(name, 1, 0, 0, 1)
            half_passes(name, 1, 0)
        cast_rows("V", "dom", 1, 1, 2)
        closing = seq_tile("closing", H, F32)
        cast("V", closing[:], acc[0, H][:])
        scatter(0, 1, closing[:])
        store(0)
        cast_rows("V", "qm", 1, 1, 2)
        for name in ("dom", "qm"):
            quant_rows(name, 1, 1, 1, 2)
            half_passes(name, 1, 1)
        cast_late("V", "dom", 2, 1, 2)
        cast_late("V", "qm", 2, 0, 2)
        cast_late("S", "dom", 2, 0, 1)
        finish(1)
        quant_rows("dom", 2, 1, 1, 2)
        quant_rows("dom", 2, 0, 0, 1)
        for g in range(G):
            half_passes("dom", 2, g)
        quant_rows("qm", 2, 0, 0, 2)
        for g in range(G):
            half_passes("qm", 2, g)
        finish(2)
        cast_late("V", "dom", 3, 0, 2)
        cast_late("V", "qm", 3, 0, 1)
        quant_rows("dom", 3, 0, 0, 2)
        for g in range(G):
            half_passes("dom", 3, g)
        cast_late("V", "qm", 3, 1, 2)
        for g in range(G):
            quant_rows("qm", 3, g, g, g + 1)
            half_passes("qm", 3, g)
        last = keep.tile([P, N], F32, name="last")
        for h in range(2):
            cast("V", last[:, h * H:(h + 1) * H], acc[3, h * H][:])
        nc.vector.tensor_copy(out=windows[3][:].indirect(offsets[:]), in_=last[:])
        store(3)
